import numpy as np
import ml_dtypes


def mxq(x, axis, fmt="e4m3"):
    dtype, down = {"e4m3": (ml_dtypes.float8_e4m3fn, 7), "e5m2": (ml_dtypes.float8_e5m2, 14)}[fmt]
    v = np.moveaxis(np.asarray(x, np.float32).astype(ml_dtypes.bfloat16).astype(np.float64), axis, -1)
    blocks = v.reshape(v.shape[:-1] + (-1, 32))
    amax = np.abs(blocks).max(-1, keepdims=True)
    byte = np.maximum(np.where(amax > 0, np.frexp(amax)[1] - 1 + 127, 0) - down, 1)
    scale = np.exp2(byte - 127.0)
    codes = (blocks / scale).astype(np.float32).astype(dtype).astype(np.float64)
    return np.moveaxis((codes * scale).reshape(v.shape), -1, axis)


WIDE = False


def mx_kscale(k):
    if not WIDE:
        return np.ones(k)
    levels = np.array([10, -10, 5, -5, 0])
    if k % 512:
        return np.exp2(np.random.permutation(np.resize(levels, k // 32))).repeat(32)
    a = np.empty((k // 512, 16))
    for p in range(k // 512):
        a[p, :8] = np.random.permutation(np.resize(levels, 8))
        for g in range(8):
            far = levels[np.abs(levels - a[p, g]) >= 10]
            a[p, g + 8] = far[np.random.randint(len(far))]
    return np.exp2(a.ravel()).repeat(32)


def f64(x):
    return np.asarray(x).astype(np.float64)


def striped(idx):
    return np.tile(idx.reshape(-1, 16).T, (8, 1)).astype(np.uint16)


def unstriped(offs):
    return offs[:16].T.reshape(-1).astype(np.int64)


E2M1 = np.array([0.0, 0.5, 1.0, 1.5, 2.0, 3.0, 4.0, 6.0, -0.0, -0.5, -1.0, -1.5, -2.0, -3.0, -4.0, -6.0])


def pack_weight(w, fmt):
    k, n = w.shape
    w = f64(np.asarray(w, np.float32).astype(ml_dtypes.bfloat16)).reshape(k // 32, 32, n)
    amax = np.abs(w).max(1)
    if fmt == "e4m3":
        byte = np.frexp(amax)[1] - 1 + 127 - 7
    else:
        mant, ex = np.frexp(amax / 6.0)
        byte = np.where(mant > 0.5, ex, ex - 1) + 127
    byte = np.clip(np.where(amax > 0, byte, 1), 1, 254)
    scaled = (w * np.exp2(127.0 - byte)[:, None, :]).reshape(k, n).astype(np.float32)
    by_word = np.ascontiguousarray(scaled.reshape(k // 512, 128, 4, n).transpose(0, 1, 3, 2))
    if fmt == "e4m3":
        words = by_word.astype(ml_dtypes.float8_e4m3fn).view(np.uint8)
    else:
        c = by_word.astype(ml_dtypes.float4_e2m1fn).view(np.uint8) & 0xF
        words = (c[..., 0::2] | (c[..., 1::2] << 4)).reshape(k // 512, 128, 2 * n)
    return np.ascontiguousarray(words), np.ascontiguousarray(byte.astype(np.uint8).reshape(k // 512, 16, n))


def unpack_weight(words, scales, fmt):
    g, _, n = scales.shape
    words = np.ascontiguousarray(words).reshape(g, 128, n, -1)
    if fmt == "e4m3":
        vals = words.view(ml_dtypes.float8_e4m3fn).astype(np.float64)
    else:
        nib = np.empty((g, 128, n, 4), np.uint8)
        nib[..., 0::2] = words & 0xF
        nib[..., 1::2] = words >> 4
        vals = E2M1[nib]
    vals = vals * np.repeat(np.exp2(scales.astype(np.float64) - 127.0), 8, axis=1)[..., None]
    return vals.transpose(0, 1, 3, 2).reshape(g * 512, n)


K, T, E, C, N = 512, 768, 12, 128, 512
M = 128


def by_expert(wq, xq):
    return np.concatenate([wq[e].T @ xq[:, e * C:(e + 1) * C] for e in range(E)], axis=1)


def setup_inputs():
    n = np.random.standard_normal
    s = mx_kscale(K)[:, None]
    v = mx_kscale(N)
    first = np.random.permutation(np.repeat(np.arange(E), T // E))
    second = (first + 1 + np.random.permutation(np.repeat(np.arange(E - 1), -(-T // (E - 1)))[:T])) % E
    while np.bincount(second, minlength=E).max() != T // E:
        load = np.bincount(second, minlength=E); hi, lo = int(load.argmax()), int(load.argmin())
        t = np.flatnonzero((second == hi) & (first != lo))[0]; second[t] = lo
    slot_token = np.empty(E * C, np.int64); pos = np.empty((2, T), np.int64); fill = np.zeros(E, np.int64)
    place = np.stack([np.random.permutation(C) for _ in range(E)])
    for r, deal in enumerate((first, second)):
        for t in np.random.permutation(T):
            e = deal[t]; j = e * C + place[e, fill[e]]; fill[e] += 1; slot_token[j] = t; pos[r, t] = j
    g = np.random.uniform(0.2, 0.8, T)
    w = [pack_weight(m, "e2m1") for m in n((E, K, N)) / np.sqrt(K) / s[None] * v[None, None, :]]
    x = pack_weight(n((K, T)) * s, "e4m3")
    return {
        "x_words": x[0],
        "x_scales": x[1],
        "w_words": np.stack([m[0] for m in w]),
        "w_scales": np.stack([m[1] for m in w]),
        "wp": (n((N, M)) / np.sqrt(N) / v[:, None]).astype(np.float32),
        "gate": np.stack([np.tile(g, (N, 1)), np.tile(1.0 - g, (N, 1))]).astype(np.float32),
        "offs": striped(slot_token),
        "pos1": striped(pos[0]),
        "pos2": striped(pos[1]),
    }


def reference(x_words, x_scales, w_words, w_scales, wp, gate, offs, pos1, pos2):
    idx = unstriped(offs)
    w = np.stack([unpack_weight(w_words[e], w_scales[e], "e2m1") for e in range(E)])
    xq = unpack_weight(x_words, x_scales, "e4m3")[:, idx]
    y = by_expert(w, xq)
    c = f64(gate[0]) * y[:, unstriped(pos1)] + f64(gate[1]) * y[:, unstriped(pos2)]
    return mxq(f64(wp), 0, "e4m3").T @ mxq(c, 0, "e4m3")

@@ -1,0 +1,214 @@
+from contextlib import ExitStack
+
+import concourse.mybir as mybir
+from concourse.masks import make_identity
+
+K, T, E, C, N, M = 512, 768, 12, 128, 512, 128
+S = E * C
+P = 128
+NB = N // P
+FLOPS = 2 * K * N * S + 2 * N * M * T
+BYTES = K * T + 16 * T + E * (K * N // 2 + 16 * N) + 4 * N * M + 2 * 4 * T + 2 * P * (S + 2 * T) // 16 + 4 * M * T
+
+F32 = mybir.dt.float32
+BF16 = mybir.dt.bfloat16
+I32 = mybir.dt.int32
+U32 = mybir.dt.uint32
+U16 = mybir.dt.uint16
+U8 = mybir.dt.uint8
+FP8X4 = mybir.dt.float8_e4m3fn_x4
+FP4X4 = mybir.dt.float4_e2m1fn_x4
+MULT = mybir.AluOpType.mult
+
+GROUP = 4
+TOKEN_CHUNKS = (256, 256, 128, 128)
+
+
+def tile_moe_nxt_lin_none_kernel(
+    tc, x_words, x_scales, w_words, w_scales, wp, gate, offs, pos1, pos2, out
+):
+    nc = tc.nc
+    with ExitStack() as ctx:
+        keep = ctx.enter_context(tc.tile_pool(name="keep", bufs=1))
+        ring = ctx.enter_context(tc.tile_pool(name="ring", bufs=8))
+        psum = ctx.enter_context(tc.psum_pool(name="psum", bufs=8))
+
+        offs_sb = keep.tile([P, S // 16], U16, name="offs_sb")
+        pos_sb = [keep.tile([P, T // 16], U16, name=f"pos_sb{i}") for i in range(2)]
+        xw = keep.tile([P, T], I32, name="xw", align_bytes=64)
+        xs = keep.tile([P, T], U8, name="xs", align_bytes=64)
+        ws = keep.tile([P, E * N], U8, name="ws", align_bytes=64)
+        ww = [keep.tile([P, GROUP * 2 * N], U8, name=f"ww{g}", align_bytes=64) for g in range(E // GROUP)]
+        starts = [sum(TOKEN_CHUNKS[:ci]) for ci in range(len(TOKEN_CHUNKS))]
+        gate_sb = [keep.tile([P, 2, tw], F32, name=f"gate_sb{ci}") for ci, tw in enumerate(TOKEN_CHUNKS)]
+        wp_raw = keep.tile([P, 4, M], F32, name="wp_raw")
+        ident = keep.tile([P, P], F32, name="ident")
+
+        nc.gpsimd.memset(xs[:].bitcast(I32), 0)
+        nc.vector.memset(ws[:].bitcast(I32), 0)
+        make_identity(nc, ident[:])
+
+        xs_rows = x_scales[0].rearrange("(q r) t -> r q t", r=4)
+        ws_rows = w_scales.rearrange("e a (q r) n -> r q (e a) n", r=4)
+        ww_rows = w_words.rearrange("e a p n -> p (e a) n")
+
+        def load_weights(g):
+            nc.sync.dma_start(
+                ww[g][:].bitcast(I32).rearrange("p (e n) -> p e n", e=GROUP),
+                ww_rows[:, g * GROUP : (g + 1) * GROUP, :].bitcast(I32),
+            )
+
+        def load_gate(ci):
+            t0, tw = starts[ci], TOKEN_CHUNKS[ci]
+            nc.sync.dma_start(gate_sb[ci][:], gate[:, 0:P, t0 : t0 + tw].rearrange("i p t -> p i t"))
+
+        nc.sync.dma_start(xw[:], x_words[0].rearrange("p t r -> p (t r)").bitcast(I32))
+        for r in range(4):
+            nc.sync.dma_start(xs[r:P:32, :].bitcast(I32), xs_rows[r].bitcast(I32))
+        nc.sync.dma_start(offs_sb[:], offs)
+        load_weights(0)
+        for r in range(4):
+            nc.sync.dma_start(
+                ws[r:P:32, :].bitcast(I32).rearrange("q (e n) -> q e n", e=E), ws_rows[r].bitcast(I32)
+            )
+        load_weights(1)
+        load_weights(2)
+        nc.sync.dma_start(wp_raw[:], wp.rearrange("(p j) f -> p j f", j=4))
+        nc.sync.dma_start(pos_sb[0][:], pos1)
+        nc.sync.dma_start(pos_sb[1][:], pos2)
+        for ci in range(len(TOKEN_CHUNKS)):
+            load_gate(ci)
+
+        y = [keep.tile([P, S], F32, name=f"y{b}") for b in range(NB)]
+        slot_scales = {}
+        slot_words = {}
+
+        def gather_tokens(source, dtype, first, last, label, into):
+            tile = keep.tile([P, (last - first) * C], dtype, name=f"{label}{first}", align_bytes=64)
+            nc.vector.tensor_copy(tile[:], source.indirect(offs_sb[:, first * C // 16 : last * C // 16]))
+            for e in range(first, last):
+                into[e] = tile[:, (e - first) * C : (e - first + 1) * C]
+
+        def experts(first, last, b):
+            bank = psum.tile([P, N], F32, name="bank")
+            for e in range(first, last):
+                g, u = divmod(e, GROUP)
+                nc.tensor.matmul_mx(
+                    out=bank[:, (e - first) * C : (e - first + 1) * C],
+                    lhsT=ww[g][:, 2 * (u * N + b * P) : 2 * (u * N + (b + 1) * P)].bitcast(FP4X4),
+                    lhsT_scale=ws[:, e * N + b * P : e * N + (b + 1) * P],
+                    rhs=slot_words[e].bitcast(FP8X4),
+                    rhs_scale=slot_scales[e],
+                    start=True,
+                    stop=True,
+                )
+            nc.scalar.copy(y[b][:, first * C : last * C], bank[:, 0 : (last - first) * C])
+
+        words_window = xw[:].bitcast(U32)
+        gather_tokens(xs[:], U8, 0, 4, "scales", slot_scales)
+        gather_tokens(words_window, U32, 0, 4, "words", slot_words)
+        for b in range(NB):
+            experts(0, 4, b)
+        gather_tokens(xs[:], U8, 4, 8, "scales", slot_scales)
+        gather_tokens(words_window, U32, 4, 8, "words", slot_words)
+        for b in range(NB - 1):
+            experts(4, 8, b)
+        gather_tokens(xs[:], U8, 8, 12, "scales", slot_scales)
+        gather_tokens(words_window, U32, 8, 11, "words", slot_words)
+        gather_tokens(words_window, U32, 11, 12, "words", slot_words)
+        experts(8, 11, 0)
+        experts(11, 12, 0)
+        experts(8, 12, 1)
+        experts(8, 12, 2)
+        experts(4, 8, 3)
+        experts(8, 12, 3)
+
+        wp_bf = keep.tile([P, M, 4], BF16, name="wp_bf", align_bytes=64)
+        wp_codes = keep.tile([P, M], U32, name="wp_codes", align_bytes=64)
+        wp_scales = keep.tile([P, M], U8, name="wp_scales", align_bytes=64)
+        nc.vector.tensor_copy(wp_bf[:], wp_raw[:].rearrange("p j f -> p f j"))
+        nc.vector.quantize_mx(
+            out=wp_codes[:].bitcast(FP8X4), scales=wp_scales[:], in_=wp_bf[:].rearrange("p f j -> p (f j)")
+        )
+
+        sums = {}
+        c_bf = {}
+
+        def combine(ci, b):
+            t0, tw = starts[ci], TOKEN_CHUNKS[ci]
+            tiles = tw // P
+            if b == 0:
+                sums[ci] = [psum.tile([P, N], F32, name="bank") for j in range(tiles)]
+            terms = []
+            for i in range(2):
+                term = ring.tile([P, tw], F32, name=f"term{i}")
+                nc.vector.tensor_tensor(
+                    term[:],
+                    y[b][:].indirect(pos_sb[i][:, t0 // 16 : (t0 + tw) // 16]),
+                    gate_sb[ci][:, i, :],
+                    MULT,
+                )
+                terms.append(term)
+            for j in range(tiles):
+                for i in range(2):
+                    nc.tensor.matmul(
+                        sums[ci][j][:, b * P : (b + 1) * P],
+                        lhsT=terms[i][:, j * P : (j + 1) * P],
+                        rhs=ident[:],
+                        is_transpose=True,
+                        start=(i == 0),
+                        stop=(i == 1),
+                    )
+
+        def turn_back(ci):
+            tw = TOKEN_CHUNKS[ci]
+            tiles = tw // P
+            back = psum.tile([P, N], F32, name="bank")
+            for j in range(tiles):
+                ct = ring.tile([P, N], BF16, name="ct")
+                nc.scalar.copy(
+                    ct[:].rearrange("p (u w e) -> p u w e", u=2, e=2),
+                    sums[ci][j][:].rearrange("p (w u e) -> p u w e", u=2, e=2),
+                )
+                pairs = ct[:].bitcast(F32)
+                for u in range(2):
+                    nc.tensor.transpose(
+                        back[:, (2 * j + u) * P : (2 * j + u + 1) * P], pairs[:, u * P : (u + 1) * P], ident[:]
+                    )
+            c_bf[ci] = keep.tile([P, 4 * tw], BF16, name=f"c_bf{ci}", align_bytes=64)
+            nc.scalar.copy(
+                c_bf[ci][:].bitcast(F32).rearrange("p (j t u) -> p j t u", j=tiles, u=2),
+                back[:, 0 : 2 * tw].rearrange("p (j u t) -> p j t u", j=tiles, u=2),
+            )
+
+        def project(ci):
+            t0, tw = starts[ci], TOKEN_CHUNKS[ci]
+            c_codes = keep.tile([P, tw], U32, name=f"c_codes{ci}", align_bytes=64)
+            c_scales = keep.tile([P, tw], U8, name=f"c_scales{ci}", align_bytes=64)
+            nc.vector.quantize_mx(out=c_codes[:].bitcast(FP8X4), scales=c_scales[:], in_=c_bf[ci][:])
+            acc = psum.tile([P, N], F32, name="bank")
+            nc.tensor.matmul_mx(
+                out=acc[:, 0:tw],
+                lhsT=wp_codes[:].bitcast(FP8X4),
+                lhsT_scale=wp_scales[:],
+                rhs=c_codes[:].bitcast(FP8X4),
+                rhs_scale=c_scales[:],
+                start=True,
+                stop=True,
+            )
+            res = keep.tile([P, tw], F32, name=f"res{ci}")
+            nc.scalar.copy(res[:], acc[:, 0:tw])
+            nc.sync.dma_start(out[:, t0 : t0 + tw], res[:])
+
+        last = len(TOKEN_CHUNKS) - 1
+        for ci in range(last + 1):
+            combine(ci, 0)
+            if ci > 0:
+                turn_back(ci - 1)
+            for b in range(1, NB):
+                combine(ci, b)
+            if ci > 0:
+                project(ci - 1)
+
+        turn_back(last)
+        project(last)

@@ -7,6 +7,7 @@ K, T, E, C, N, M = 512, 768, 12, 128, 512, 128
 S = E * C
 P = 128
 NB = N // P
+BANK = 512
 FLOPS = 2 * K * N * S + 2 * N * M * T
 BYTES = K * T + 16 * T + E * (K * N // 2 + 16 * N) + 4 * N * M + 2 * 4 * T + 2 * P * (S + 2 * T) // 16 + 4 * M * T
 
@@ -20,8 +21,11 @@ FP8X4 = mybir.dt.float8_e4m3fn_x4
 FP4X4 = mybir.dt.float4_e2m1fn_x4
 MULT = mybir.AluOpType.mult
 
-GROUP = 4
-TOKEN_CHUNKS = (256, 256, 128, 128)
+GROUP = BANK // C
+GROUPS = E // GROUP
+TOKEN_CHUNKS = (384, 256, 128)
+TERM_BUFS = 4
+BANK_BUFS = 4
 
 
 def tile_moe_nxt_lin_none_kernel(
@@ -30,15 +34,15 @@ def tile_moe_nxt_lin_none_kernel(
     nc = tc.nc
     with ExitStack() as ctx:
         keep = ctx.enter_context(tc.tile_pool(name="keep", bufs=1))
-        ring = ctx.enter_context(tc.tile_pool(name="ring", bufs=8))
-        psum = ctx.enter_context(tc.psum_pool(name="psum", bufs=8))
+        ring = ctx.enter_context(tc.tile_pool(name="ring", bufs=TERM_BUFS))
+        psum = ctx.enter_context(tc.psum_pool(name="psum", bufs=BANK_BUFS))
 
         offs_sb = keep.tile([P, S // 16], U16, name="offs_sb")
         pos_sb = [keep.tile([P, T // 16], U16, name=f"pos_sb{i}") for i in range(2)]
         xw = keep.tile([P, T], I32, name="xw", align_bytes=64)
         xs = keep.tile([P, T], U8, name="xs", align_bytes=64)
         ws = keep.tile([P, E * N], U8, name="ws", align_bytes=64)
-        ww = [keep.tile([P, GROUP * 2 * N], U8, name=f"ww{g}", align_bytes=64) for g in range(E // GROUP)]
+        ww = [keep.tile([P, GROUP * 2 * N], U8, name=f"ww{g}", align_bytes=64) for g in range(GROUPS)]
         starts = [sum(TOKEN_CHUNKS[:ci]) for ci in range(len(TOKEN_CHUNKS))]
         gate_sb = [keep.tile([P, 2, tw], F32, name=f"gate_sb{ci}") for ci, tw in enumerate(TOKEN_CHUNKS)]
         wp_raw = keep.tile([P, 4, M], F32, name="wp_raw")
@@ -52,45 +56,43 @@ def tile_moe_nxt_lin_none_kernel(
         ws_rows = w_scales.rearrange("e a (q r) n -> r q (e a) n", r=4)
         ww_rows = w_words.rearrange("e a p n -> p (e a) n")
 
-        def load_weights(g):
-            nc.sync.dma_start(
-                ww[g][:].bitcast(I32).rearrange("p (e n) -> p e n", e=GROUP),
-                ww_rows[:, g * GROUP : (g + 1) * GROUP, :].bitcast(I32),
-            )
-
         def load_gate(ci):
             t0, tw = starts[ci], TOKEN_CHUNKS[ci]
             nc.sync.dma_start(gate_sb[ci][:], gate[:, 0:P, t0 : t0 + tw].rearrange("i p t -> p i t"))
 
-        nc.sync.dma_start(xw[:], x_words[0].rearrange("p t r -> p (t r)").bitcast(I32))
-        for r in range(4):
-            nc.sync.dma_start(xs[r:P:32, :].bitcast(I32), xs_rows[r].bitcast(I32))
         nc.sync.dma_start(offs_sb[:], offs)
-        load_weights(0)
+        for r in range(4):
+            queue = nc.sync if r < 2 else nc.scalar
+            queue.dma_start(xs[r:P:32, :].bitcast(I32), xs_rows[r].bitcast(I32))
+        nc.sync.dma_start(xw[:], x_words[0].rearrange("p t r -> p (t r)").bitcast(I32))
         for r in range(4):
             nc.sync.dma_start(
                 ws[r:P:32, :].bitcast(I32).rearrange("q (e n) -> q e n", e=E), ws_rows[r].bitcast(I32)
             )
-        load_weights(1)
-        load_weights(2)
-        nc.sync.dma_start(wp_raw[:], wp.rearrange("(p j) f -> p j f", j=4))
+        for g in range(GROUPS):
+            nc.sync.dma_start(
+                ww[g][:].bitcast(I32).rearrange("p (e n) -> p e n", e=GROUP),
+                ww_rows[:, g * GROUP : (g + 1) * GROUP, :].bitcast(I32),
+            )
         nc.sync.dma_start(pos_sb[0][:], pos1)
         nc.sync.dma_start(pos_sb[1][:], pos2)
-        for ci in range(len(TOKEN_CHUNKS)):
+        load_gate(0)
+        nc.sync.dma_start(wp_raw[:], wp.rearrange("(p j) f -> p j f", j=4))
+        for ci in range(1, len(TOKEN_CHUNKS)):
             load_gate(ci)
 
         y = [keep.tile([P, S], F32, name=f"y{b}") for b in range(NB)]
         slot_scales = {}
         slot_words = {}
 
-        def gather_tokens(source, dtype, first, last, label, into):
+        def gather_tokens(window, dtype, first, last, label, by_expert):
             tile = keep.tile([P, (last - first) * C], dtype, name=f"{label}{first}", align_bytes=64)
-            nc.vector.tensor_copy(tile[:], source.indirect(offs_sb[:, first * C // 16 : last * C // 16]))
+            nc.vector.tensor_copy(tile[:], window.indirect(offs_sb[:, first * C // 16 : last * C // 16]))
             for e in range(first, last):
-                into[e] = tile[:, (e - first) * C : (e - first + 1) * C]
+                by_expert[e] = tile[:, (e - first) * C : (e - first + 1) * C]
 
-        def experts(first, last, b):
-            bank = psum.tile([P, N], F32, name="bank")
+        def experts(first, last, b, evict=nc.scalar.copy):
+            bank = psum.tile([P, BANK], F32, name="bank")
             for e in range(first, last):
                 g, u = divmod(e, GROUP)
                 nc.tensor.matmul_mx(
@@ -102,57 +104,57 @@ def tile_moe_nxt_lin_none_kernel(
                     start=True,
                     stop=True,
                 )
-            nc.scalar.copy(y[b][:, first * C : last * C], bank[:, 0 : (last - first) * C])
-
-        words_window = xw[:].bitcast(U32)
-        gather_tokens(xs[:], U8, 0, 4, "scales", slot_scales)
-        gather_tokens(words_window, U32, 0, 4, "words", slot_words)
-        for b in range(NB):
-            experts(0, 4, b)
-        gather_tokens(xs[:], U8, 4, 8, "scales", slot_scales)
-        gather_tokens(words_window, U32, 4, 8, "words", slot_words)
-        for b in range(NB - 1):
-            experts(4, 8, b)
-        gather_tokens(xs[:], U8, 8, 12, "scales", slot_scales)
-        gather_tokens(words_window, U32, 8, 11, "words", slot_words)
-        gather_tokens(words_window, U32, 11, 12, "words", slot_words)
-        experts(8, 11, 0)
-        experts(11, 12, 0)
-        experts(8, 12, 1)
-        experts(8, 12, 2)
-        experts(4, 8, 3)
-        experts(8, 12, 3)
+            evict(y[b][:, first * C : last * C], bank[:, 0 : (last - first) * C])
 
         wp_bf = keep.tile([P, M, 4], BF16, name="wp_bf", align_bytes=64)
         wp_codes = keep.tile([P, M], U32, name="wp_codes", align_bytes=64)
         wp_scales = keep.tile([P, M], U8, name="wp_scales", align_bytes=64)
-        nc.vector.tensor_copy(wp_bf[:], wp_raw[:].rearrange("p j f -> p f j"))
-        nc.vector.quantize_mx(
-            out=wp_codes[:].bitcast(FP8X4), scales=wp_scales[:], in_=wp_bf[:].rearrange("p f j -> p (f j)")
-        )
+
+        words_window = xw[:].bitcast(U32)
+        for g in range(GROUPS):
+            gather_tokens(xs[:], U8, GROUP * g, GROUP * (g + 1), "scales", slot_scales)
+        gather_tokens(words_window, U32, 0, GROUP, "words", slot_words)
+        experts(0, GROUP, 0)
+        experts(0, GROUP, 1)
+        gather_tokens(words_window, U32, GROUP, 2 * GROUP, "words", slot_words)
+        experts(GROUP, 2 * GROUP, 0)
+        gather_tokens(words_window, U32, 2 * GROUP, E - 1, "words", slot_words)
+        gather_tokens(words_window, U32, E - 1, E, "words", slot_words)
+        experts(2 * GROUP, E - 1, 0)
+        experts(E - 1, E, 0, nc.vector.tensor_copy)
+        for g in range(1, GROUPS):
+            experts(GROUP * g, GROUP * (g + 1), 1)
+        for b in range(2, NB):
+            for g in range(GROUPS):
+                experts(GROUP * g, GROUP * (g + 1), b)
 
         sums = {}
+        rounded = {}
         c_bf = {}
 
-        def combine(ci, b):
+        def quantize_wp():
+            nc.scalar.copy(wp_bf[:], wp_raw[:].rearrange("p j f -> p f j"))
+            nc.vector.quantize_mx(
+                out=wp_codes[:].bitcast(FP8X4), scales=wp_scales[:], in_=wp_bf[:].rearrange("p f j -> p (f j)")
+            )
+
+        def combine(ci, b, new_banks):
             t0, tw = starts[ci], TOKEN_CHUNKS[ci]
-            tiles = tw // P
-            if b == 0:
-                sums[ci] = [psum.tile([P, N], F32, name="bank") for j in range(tiles)]
+            first = t0 // P
+            if new_banks:
+                for j in range(tw // P):
+                    sums[first + j] = psum.tile([P, BANK], F32, name="sums")
             terms = []
             for i in range(2):
                 term = ring.tile([P, tw], F32, name=f"term{i}")
                 nc.vector.tensor_tensor(
-                    term[:],
-                    y[b][:].indirect(pos_sb[i][:, t0 // 16 : (t0 + tw) // 16]),
-                    gate_sb[ci][:, i, :],
-                    MULT,
+                    term[:], y[b][:].indirect(pos_sb[i][:, t0 // 16 : (t0 + tw) // 16]), gate_sb[ci][:, i, :], MULT
                 )
                 terms.append(term)
-            for j in range(tiles):
+            for j in range(tw // P):
                 for i in range(2):
                     nc.tensor.matmul(
-                        sums[ci][j][:, b * P : (b + 1) * P],
+                        sums[first + j][:, b * P : (b + 1) * P],
                         lhsT=terms[i][:, j * P : (j + 1) * P],
                         rhs=ident[:],
                         is_transpose=True,
@@ -160,33 +162,35 @@ def tile_moe_nxt_lin_none_kernel(
                         stop=(i == 1),
                     )
 
-        def turn_back(ci):
-            tw = TOKEN_CHUNKS[ci]
-            tiles = tw // P
-            back = psum.tile([P, N], F32, name="bank")
-            for j in range(tiles):
-                ct = ring.tile([P, N], BF16, name="ct")
-                nc.scalar.copy(
-                    ct[:].rearrange("p (u w e) -> p u w e", u=2, e=2),
-                    sums[ci][j][:].rearrange("p (w u e) -> p u w e", u=2, e=2),
-                )
-                pairs = ct[:].bitcast(F32)
-                for u in range(2):
-                    nc.tensor.transpose(
-                        back[:, (2 * j + u) * P : (2 * j + u + 1) * P], pairs[:, u * P : (u + 1) * P], ident[:]
-                    )
-            c_bf[ci] = keep.tile([P, 4 * tw], BF16, name=f"c_bf{ci}", align_bytes=64)
+        def round_sums(j, b0, b1):
+            if b0 == 0:
+                rounded[j] = ring.tile([P, N], BF16, name="rounded")
+            w = slice(b0 * P // 4, b1 * P // 4)
             nc.scalar.copy(
-                c_bf[ci][:].bitcast(F32).rearrange("p (j t u) -> p j t u", j=tiles, u=2),
-                back[:, 0 : 2 * tw].rearrange("p (j u t) -> p j t u", j=tiles, u=2),
+                rounded[j][:].rearrange("p (u w e) -> p u w e", u=2, e=2)[:, :, w, :],
+                sums[j][:].rearrange("p (w u e) -> p u w e", u=2, e=2)[:, :, w, :],
             )
 
-        def project(ci):
-            t0, tw = starts[ci], TOKEN_CHUNKS[ci]
-            c_codes = keep.tile([P, tw], U32, name=f"c_codes{ci}", align_bytes=64)
-            c_scales = keep.tile([P, tw], U8, name=f"c_scales{ci}", align_bytes=64)
-            nc.vector.quantize_mx(out=c_codes[:].bitcast(FP8X4), scales=c_scales[:], in_=c_bf[ci][:])
-            acc = psum.tile([P, N], F32, name="bank")
+        def turn_back(j0, j1):
+            c_bf[j0] = keep.tile([P, (j1 - j0) * N], BF16, name=f"c_bf{j0}", align_bytes=64)
+            for j in range(j0, j1):
+                if j not in rounded:
+                    round_sums(j, 0, NB)
+                back = psum.tile([P, BANK], F32, name="bank")
+                pairs = rounded[j][:].bitcast(F32)
+                for u in range(2):
+                    nc.tensor.transpose(back[:, u * P : (u + 1) * P], pairs[:, u * P : (u + 1) * P], ident[:])
+                nc.scalar.copy(
+                    c_bf[j0][:, (j - j0) * N : (j - j0 + 1) * N].bitcast(F32).rearrange("p (t u) -> p t u", u=2),
+                    back[:, 0 : 2 * P].rearrange("p (u t) -> p t u", u=2),
+                )
+
+        def project(j0, j1, evict):
+            t0, tw = j0 * P, (j1 - j0) * P
+            c_codes = keep.tile([P, tw], U32, name=f"c_codes{j0}", align_bytes=64)
+            c_scales = keep.tile([P, tw], U8, name=f"c_scales{j0}", align_bytes=64)
+            nc.vector.quantize_mx(out=c_codes[:].bitcast(FP8X4), scales=c_scales[:], in_=c_bf[j0][:])
+            acc = psum.tile([P, BANK], F32, name="bank")
             nc.tensor.matmul_mx(
                 out=acc[:, 0:tw],
                 lhsT=wp_codes[:].bitcast(FP8X4),
@@ -196,19 +200,27 @@ def tile_moe_nxt_lin_none_kernel(
                 start=True,
                 stop=True,
             )
-            res = keep.tile([P, tw], F32, name=f"res{ci}")
-            nc.scalar.copy(res[:], acc[:, 0:tw])
+            res = keep.tile([P, tw], F32, name=f"res{j0}")
+            evict(res[:], acc[:, 0:tw])
             nc.sync.dma_start(out[:, t0 : t0 + tw], res[:])
 
-        last = len(TOKEN_CHUNKS) - 1
-        for ci in range(last + 1):
-            combine(ci, 0)
-            if ci > 0:
-                turn_back(ci - 1)
-            for b in range(1, NB):
-                combine(ci, b)
-            if ci > 0:
-                project(ci - 1)
-
-        turn_back(last)
-        project(last)
+        for b in range(NB):
+            combine(0, b, b == 0)
+        quantize_wp()
+        combine(1, 0, True)
+        turn_back(0, 2)
+        turn_back(2, 3)
+        for b in range(1, NB):
+            combine(1, b, False)
+        project(0, 2, nc.scalar.copy)
+        combine(2, 0, True)
+        turn_back(3, 5)
+        for b in range(1, NB - 1):
+            combine(2, b, False)
+        round_sums(5, 0, NB - 1)
+        combine(2, NB - 1, True)
+        round_sums(5, NB - 1, NB)
+        turn_back(5, 6)
+        project(2, 3, nc.vector.tensor_copy)
+        project(3, 5, nc.vector.tensor_copy)
+        project(5, 6, nc.scalar.copy)

@@ -23,9 +23,10 @@ MULT = mybir.AluOpType.mult
 
 GROUP = BANK // C
 GROUPS = E // GROUP
+HALF = N // 2
 TOKEN_CHUNKS = (384, 256, 128)
 TERM_BUFS = 4
-BANK_BUFS = 4
+BANKS = 8
 
 
 def tile_moe_nxt_lin_none_kernel(
@@ -35,24 +36,23 @@ def tile_moe_nxt_lin_none_kernel(
     with ExitStack() as ctx:
         keep = ctx.enter_context(tc.tile_pool(name="keep", bufs=1))
         ring = ctx.enter_context(tc.tile_pool(name="ring", bufs=TERM_BUFS))
-        psum = ctx.enter_context(tc.psum_pool(name="psum", bufs=BANK_BUFS))
+        psum = ctx.enter_context(tc.psum_pool(name="psum", bufs=1))
 
         offs_sb = keep.tile([P, S // 16], U16, name="offs_sb")
         pos_sb = [keep.tile([P, T // 16], U16, name=f"pos_sb{i}") for i in range(2)]
         xw = keep.tile([P, T], I32, name="xw", align_bytes=64)
         xs = keep.tile([P, T], U8, name="xs", align_bytes=64)
         ws = keep.tile([P, E * N], U8, name="ws", align_bytes=64)
-        ww = [keep.tile([P, GROUP * 2 * N], U8, name=f"ww{g}", align_bytes=64) for g in range(GROUPS)]
+        ww = [keep.tile([P, E * 2 * HALF], U8, name=f"ww{h}", align_bytes=64) for h in range(2)]
+        banks = [psum.tile([P, BANK], F32, name=f"bank{k}") for k in range(BANKS)]
         starts = [sum(TOKEN_CHUNKS[:ci]) for ci in range(len(TOKEN_CHUNKS))]
         gate_sb = [keep.tile([P, 2, tw], F32, name=f"gate_sb{ci}") for ci, tw in enumerate(TOKEN_CHUNKS)]
         wp_raw = keep.tile([P, 4, M], F32, name="wp_raw")
         ident = keep.tile([P, P], F32, name="ident")
 
-        nc.gpsimd.memset(xs[:].bitcast(I32), 0)
         nc.vector.memset(ws[:].bitcast(I32), 0)
         make_identity(nc, ident[:])
 
-        xs_rows = x_scales[0].rearrange("(q r) t -> r q t", r=4)
         ws_rows = w_scales.rearrange("e a (q r) n -> r q (e a) n", r=4)
         ww_rows = w_words.rearrange("e a p n -> p (e a) n")
 
@@ -60,23 +60,33 @@ def tile_moe_nxt_lin_none_kernel(
             t0, tw = starts[ci], TOKEN_CHUNKS[ci]
             nc.sync.dma_start(gate_sb[ci][:], gate[:, 0:P, t0 : t0 + tw].rearrange("i p t -> p i t"))
 
+        def load_weight_words(h, first, last):
+            nc.sync.dma_start(
+                ww[h][:, first * 2 * HALF : last * 2 * HALF]
+                .bitcast(I32)
+                .rearrange("p (e n) -> p e n", e=last - first),
+                ww_rows[:, first:last, 2 * h * HALF : 2 * (h + 1) * HALF].bitcast(I32),
+            )
+
         nc.sync.dma_start(offs_sb[:], offs)
-        for r in range(4):
-            queue = nc.sync if r < 2 else nc.scalar
-            queue.dma_start(xs[r:P:32, :].bitcast(I32), xs_rows[r].bitcast(I32))
+        for q in range(4):
+            queue = nc.sync if q < 2 else nc.scalar
+            queue.dma_start(
+                xs[32 * q : 32 * (q + 1), :].bitcast(I32),
+                x_scales[0, 4 * q : 4 * q + 4, :].bitcast(I32).partition_broadcast(8),
+            )
         nc.sync.dma_start(xw[:], x_words[0].rearrange("p t r -> p (t r)").bitcast(I32))
         for r in range(4):
             nc.sync.dma_start(
                 ws[r:P:32, :].bitcast(I32).rearrange("q (e n) -> q e n", e=E), ws_rows[r].bitcast(I32)
             )
-        for g in range(GROUPS):
-            nc.sync.dma_start(
-                ww[g][:].bitcast(I32).rearrange("p (e n) -> p e n", e=GROUP),
-                ww_rows[:, g * GROUP : (g + 1) * GROUP, :].bitcast(I32),
-            )
+        load_weight_words(0, 0, GROUP)
+        load_weight_words(0, GROUP, E)
         nc.sync.dma_start(pos_sb[0][:], pos1)
         nc.sync.dma_start(pos_sb[1][:], pos2)
         load_gate(0)
+        load_weight_words(1, 0, GROUP)
+        load_weight_words(1, GROUP, E)
         nc.sync.dma_start(wp_raw[:], wp.rearrange("(p j) f -> p j f", j=4))
         for ci in range(1, len(TOKEN_CHUNKS)):
             load_gate(ci)
@@ -91,13 +101,12 @@ def tile_moe_nxt_lin_none_kernel(
             for e in range(first, last):
                 by_expert[e] = tile[:, (e - first) * C : (e - first + 1) * C]
 
-        def experts(first, last, b, evict=nc.scalar.copy):
-            bank = psum.tile([P, BANK], F32, name="bank")
+        def experts(first, last, b, bank, evict=nc.scalar.copy):
             for e in range(first, last):
-                g, u = divmod(e, GROUP)
+                h, col = divmod(b * P, HALF)
                 nc.tensor.matmul_mx(
                     out=bank[:, (e - first) * C : (e - first + 1) * C],
-                    lhsT=ww[g][:, 2 * (u * N + b * P) : 2 * (u * N + (b + 1) * P)].bitcast(FP4X4),
+                    lhsT=ww[h][:, 2 * (e * HALF + col) : 2 * (e * HALF + col + P)].bitcast(FP4X4),
                     lhsT_scale=ws[:, e * N + b * P : e * N + (b + 1) * P],
                     rhs=slot_words[e].bitcast(FP8X4),
                     rhs_scale=slot_scales[e],
@@ -114,19 +123,19 @@ def tile_moe_nxt_lin_none_kernel(
         for g in range(GROUPS):
             gather_tokens(xs[:], U8, GROUP * g, GROUP * (g + 1), "scales", slot_scales)
         gather_tokens(words_window, U32, 0, GROUP, "words", slot_words)
-        experts(0, GROUP, 0)
-        experts(0, GROUP, 1)
+        experts(0, GROUP, 0, banks[0])
+        experts(0, GROUP, 1, banks[1])
         gather_tokens(words_window, U32, GROUP, 2 * GROUP, "words", slot_words)
-        experts(GROUP, 2 * GROUP, 0)
+        experts(GROUP, 2 * GROUP, 0, banks[2])
+        experts(GROUP, 2 * GROUP, 1, banks[3])
         gather_tokens(words_window, U32, 2 * GROUP, E - 1, "words", slot_words)
         gather_tokens(words_window, U32, E - 1, E, "words", slot_words)
-        experts(2 * GROUP, E - 1, 0)
-        experts(E - 1, E, 0, nc.vector.tensor_copy)
-        for g in range(1, GROUPS):
-            experts(GROUP * g, GROUP * (g + 1), 1)
+        experts(2 * GROUP, E - 1, 0, banks[4])
+        experts(E - 1, E, 0, banks[5], nc.vector.tensor_copy)
+        experts(2 * GROUP, E, 1, banks[6])
         for b in range(2, NB):
             for g in range(GROUPS):
-                experts(GROUP * g, GROUP * (g + 1), b)
+                experts(GROUP * g, GROUP * (g + 1), b, banks[(1 + GROUPS * b + g) % BANKS])
 
         sums = {}
         rounded = {}
@@ -138,12 +147,11 @@ def tile_moe_nxt_lin_none_kernel(
                 out=wp_codes[:].bitcast(FP8X4), scales=wp_scales[:], in_=wp_bf[:].rearrange("p f j -> p (f j)")
             )
 
-        def combine(ci, b, new_banks):
+        def combine(ci, b, new_banks=()):
             t0, tw = starts[ci], TOKEN_CHUNKS[ci]
             first = t0 // P
-            if new_banks:
-                for j in range(tw // P):
-                    sums[first + j] = psum.tile([P, BANK], F32, name="sums")
+            for j, k in enumerate(new_banks):
+                sums[first + j] = banks[k]
             terms = []
             for i in range(2):
                 term = ring.tile([P, tw], F32, name=f"term{i}")
@@ -171,12 +179,12 @@ def tile_moe_nxt_lin_none_kernel(
                 sums[j][:].rearrange("p (w u e) -> p u w e", u=2, e=2)[:, :, w, :],
             )
 
-        def turn_back(j0, j1):
+        def turn_back(j0, j1, turn_banks):
             c_bf[j0] = keep.tile([P, (j1 - j0) * N], BF16, name=f"c_bf{j0}", align_bytes=64)
             for j in range(j0, j1):
                 if j not in rounded:
                     round_sums(j, 0, NB)
-                back = psum.tile([P, BANK], F32, name="bank")
+                back = banks[turn_banks[j - j0]]
                 pairs = rounded[j][:].bitcast(F32)
                 for u in range(2):
                     nc.tensor.transpose(back[:, u * P : (u + 1) * P], pairs[:, u * P : (u + 1) * P], ident[:])
@@ -185,12 +193,11 @@ def tile_moe_nxt_lin_none_kernel(
                     back[:, 0 : 2 * P].rearrange("p (u t) -> p t u", u=2),
                 )
 
-        def project(j0, j1, evict):
+        def project(j0, j1, acc, evict):
             t0, tw = j0 * P, (j1 - j0) * P
             c_codes = keep.tile([P, tw], U32, name=f"c_codes{j0}", align_bytes=64)
             c_scales = keep.tile([P, tw], U8, name=f"c_scales{j0}", align_bytes=64)
             nc.vector.quantize_mx(out=c_codes[:].bitcast(FP8X4), scales=c_scales[:], in_=c_bf[j0][:])
-            acc = psum.tile([P, BANK], F32, name="bank")
             nc.tensor.matmul_mx(
                 out=acc[:, 0:tw],
                 lhsT=wp_codes[:].bitcast(FP8X4),
@@ -204,23 +211,24 @@ def tile_moe_nxt_lin_none_kernel(
             evict(res[:], acc[:, 0:tw])
             nc.sync.dma_start(out[:, t0 : t0 + tw], res[:])
 
-        for b in range(NB):
-            combine(0, b, b == 0)
-        quantize_wp()
-        combine(1, 0, True)
-        turn_back(0, 2)
-        turn_back(2, 3)
+        combine(0, 0, (2, 3, 4))
         for b in range(1, NB):
-            combine(1, b, False)
-        project(0, 2, nc.scalar.copy)
-        combine(2, 0, True)
-        turn_back(3, 5)
+            combine(0, b)
+        quantize_wp()
+        combine(1, 0, (5, 6))
+        turn_back(0, 2, (7, 0))
+        turn_back(2, 3, (1,))
+        for b in range(1, NB):
+            combine(1, b)
+        project(0, 2, banks[4], nc.scalar.copy)
+        combine(2, 0, (2,))
+        turn_back(3, 5, (7, 0))
         for b in range(1, NB - 1):
-            combine(2, b, False)
+            combine(2, b)
         round_sums(5, 0, NB - 1)
-        combine(2, NB - 1, True)
+        combine(2, NB - 1, (3,))
         round_sums(5, NB - 1, NB)
-        turn_back(5, 6)
-        project(2, 3, nc.vector.tensor_copy)
-        project(3, 5, nc.vector.tensor_copy)
-        project(5, 6, nc.scalar.copy)
+        turn_back(5, 6, (1,))
+        project(2, 3, banks[5], nc.vector.tensor_copy)
+        project(3, 5, banks[6], nc.vector.tensor_copy)
+        project(5, 6, banks[7], nc.scalar.copy)

@@ -24,8 +24,10 @@ MULT = mybir.AluOpType.mult
 GROUP = BANK // C
 GROUPS = E // GROUP
 HALF = N // 2
-TOKEN_CHUNKS = (384, 256, 128)
-TERM_BUFS = 4
+SCALE_WINDOW = 4 * S // 3
+TILES = T // P
+EARLY = 4
+TERM_SLOTS = 3
 BANKS = 8
 
 
@@ -35,30 +37,25 @@ def tile_moe_nxt_lin_none_kernel(
     nc = tc.nc
     with ExitStack() as ctx:
         keep = ctx.enter_context(tc.tile_pool(name="keep", bufs=1))
-        ring = ctx.enter_context(tc.tile_pool(name="ring", bufs=TERM_BUFS))
         psum = ctx.enter_context(tc.psum_pool(name="psum", bufs=1))
 
         offs_sb = keep.tile([P, S // 16], U16, name="offs_sb")
         pos_sb = [keep.tile([P, T // 16], U16, name=f"pos_sb{i}") for i in range(2)]
         xw = keep.tile([P, T], I32, name="xw", align_bytes=64)
-        xs = keep.tile([P, T], U8, name="xs", align_bytes=64)
+        xs = keep.tile([P, SCALE_WINDOW], U8, name="xs", align_bytes=64)
         ws = keep.tile([P, E * N], U8, name="ws", align_bytes=64)
         ww = [keep.tile([P, E * 2 * HALF], U8, name=f"ww{h}", align_bytes=64) for h in range(2)]
-        banks = [psum.tile([P, BANK], F32, name=f"bank{k}") for k in range(BANKS)]
-        starts = [sum(TOKEN_CHUNKS[:ci]) for ci in range(len(TOKEN_CHUNKS))]
-        gate_sb = [keep.tile([P, 2, tw], F32, name=f"gate_sb{ci}") for ci, tw in enumerate(TOKEN_CHUNKS)]
+        gate_sb = [keep.tile([P, T], F32, name=f"gate_sb{i}") for i in range(2)]
         wp_raw = keep.tile([P, 4, M], F32, name="wp_raw")
         ident = keep.tile([P, P], F32, name="ident")
+        banks = [psum.tile([P, BANK], F32, name=f"bank{k}") for k in range(BANKS)]
 
         nc.vector.memset(ws[:].bitcast(I32), 0)
+        nc.gpsimd.memset(xs[:, T:].bitcast(I32), 0)
         make_identity(nc, ident[:])
 
         ws_rows = w_scales.rearrange("e a (q r) n -> r q (e a) n", r=4)
         ww_rows = w_words.rearrange("e a p n -> p (e a) n")
-
-        def load_gate(ci):
-            t0, tw = starts[ci], TOKEN_CHUNKS[ci]
-            nc.sync.dma_start(gate_sb[ci][:], gate[:, 0:P, t0 : t0 + tw].rearrange("i p t -> p i t"))
 
         def load_weight_words(h, first, last):
             nc.sync.dma_start(
@@ -72,7 +69,7 @@ def tile_moe_nxt_lin_none_kernel(
         for q in range(4):
             queue = nc.sync if q < 2 else nc.scalar
             queue.dma_start(
-                xs[32 * q : 32 * (q + 1), :].bitcast(I32),
+                xs[32 * q : 32 * (q + 1), 0:T].bitcast(I32),
                 x_scales[0, 4 * q : 4 * q + 4, :].bitcast(I32).partition_broadcast(8),
             )
         nc.sync.dma_start(xw[:], x_words[0].rearrange("p t r -> p (t r)").bitcast(I32))
@@ -82,124 +79,113 @@ def tile_moe_nxt_lin_none_kernel(
             )
         load_weight_words(0, 0, GROUP)
         load_weight_words(0, GROUP, E)
-        nc.sync.dma_start(pos_sb[0][:], pos1)
-        nc.sync.dma_start(pos_sb[1][:], pos2)
-        load_gate(0)
-        load_weight_words(1, 0, GROUP)
-        load_weight_words(1, GROUP, E)
         nc.sync.dma_start(wp_raw[:], wp.rearrange("(p j) f -> p j f", j=4))
-        for ci in range(1, len(TOKEN_CHUNKS)):
-            load_gate(ci)
+        for i, pos in enumerate((pos1, pos2)):
+            nc.sync.dma_start(pos_sb[i][:], pos)
+            nc.sync.dma_start(gate_sb[i][:], gate[i, 0:P, :])
+        load_weight_words(1, 0, E)
 
         y = [keep.tile([P, S], F32, name=f"y{b}") for b in range(NB)]
-        slot_scales = {}
+        slot_scales = keep.tile([P, S], U8, name="slot_scales", align_bytes=64)
         slot_words = {}
 
-        def gather_tokens(window, dtype, first, last, label, by_expert):
-            tile = keep.tile([P, (last - first) * C], dtype, name=f"{label}{first}", align_bytes=64)
-            nc.vector.tensor_copy(tile[:], window.indirect(offs_sb[:, first * C // 16 : last * C // 16]))
+        def gather_words(first, last):
+            tile = keep.tile([P, (last - first) * C], U32, name=f"words{first}", align_bytes=64)
+            nc.vector.tensor_copy(tile[:], xw[:].bitcast(U32).indirect(offs_sb[:, first * C // 16 : last * C // 16]))
             for e in range(first, last):
-                by_expert[e] = tile[:, (e - first) * C : (e - first + 1) * C]
+                slot_words[e] = tile[:, (e - first) * C : (e - first + 1) * C]
 
-        def experts(first, last, b, bank, evict=nc.scalar.copy):
+        def experts(first, last, b, k, evict=nc.scalar.copy):
+            h, col = divmod(b * P, HALF)
             for e in range(first, last):
-                h, col = divmod(b * P, HALF)
                 nc.tensor.matmul_mx(
-                    out=bank[:, (e - first) * C : (e - first + 1) * C],
+                    out=banks[k][:, (e - first) * C : (e - first + 1) * C],
                     lhsT=ww[h][:, 2 * (e * HALF + col) : 2 * (e * HALF + col + P)].bitcast(FP4X4),
                     lhsT_scale=ws[:, e * N + b * P : e * N + (b + 1) * P],
                     rhs=slot_words[e].bitcast(FP8X4),
-                    rhs_scale=slot_scales[e],
+                    rhs_scale=slot_scales[:, e * C : (e + 1) * C],
                     start=True,
                     stop=True,
                 )
-            evict(y[b][:, first * C : last * C], bank[:, 0 : (last - first) * C])
+            evict(y[b][:, first * C : last * C], banks[k][:, 0 : (last - first) * C])
 
-        wp_bf = keep.tile([P, M, 4], BF16, name="wp_bf", align_bytes=64)
+        terms = [
+            [keep.tile([P, EARLY * P], F32, name=f"term{s}_{i}", align_bytes=64) for i in range(2)]
+            for s in range(TERM_SLOTS)
+        ]
+        wp_bf = terms[0][0][:, 0 : 2 * M].bitcast(BF16)
         wp_codes = keep.tile([P, M], U32, name="wp_codes", align_bytes=64)
         wp_scales = keep.tile([P, M], U8, name="wp_scales", align_bytes=64)
 
-        words_window = xw[:].bitcast(U32)
-        for g in range(GROUPS):
-            gather_tokens(xs[:], U8, GROUP * g, GROUP * (g + 1), "scales", slot_scales)
-        gather_tokens(words_window, U32, 0, GROUP, "words", slot_words)
-        experts(0, GROUP, 0, banks[0])
-        experts(0, GROUP, 1, banks[1])
-        gather_tokens(words_window, U32, GROUP, 2 * GROUP, "words", slot_words)
-        experts(GROUP, 2 * GROUP, 0, banks[2])
-        experts(GROUP, 2 * GROUP, 1, banks[3])
-        gather_tokens(words_window, U32, 2 * GROUP, E - 1, "words", slot_words)
-        gather_tokens(words_window, U32, E - 1, E, "words", slot_words)
-        experts(2 * GROUP, E - 1, 0, banks[4])
-        experts(E - 1, E, 0, banks[5], nc.vector.tensor_copy)
-        experts(2 * GROUP, E, 1, banks[6])
-        for b in range(2, NB):
+        nc.scalar.copy(wp_bf.rearrange("p (f j) -> p f j", j=4), wp_raw[:].rearrange("p j f -> p f j"))
+        nc.vector.tensor_copy(slot_scales[:], xs[:].indirect(offs_sb[:]))
+        gather_words(0, GROUP)
+        experts(0, GROUP, 0, 0)
+        gather_words(GROUP, 2 * GROUP)
+        experts(GROUP, 2 * GROUP, 0, 1)
+        gather_words(2 * GROUP, E - 2)
+        gather_words(E - 2, E - 1)
+        gather_words(E - 1, E)
+        experts(2 * GROUP, E - 2, 0, 2, nc.vector.tensor_copy)
+        nc.vector.quantize_mx(out=wp_codes[:].bitcast(FP8X4), scales=wp_scales[:], in_=wp_bf)
+        experts(E - 2, E - 1, 0, 3)
+        experts(E - 1, E, 0, 4)
+        for b in range(1, NB):
             for g in range(GROUPS):
-                experts(GROUP * g, GROUP * (g + 1), b, banks[(1 + GROUPS * b + g) % BANKS])
+                experts(GROUP * g, GROUP * (g + 1), b, 2 + g)
 
-        sums = {}
-        rounded = {}
-        c_bf = {}
+        spans = [(0, 2), (2, EARLY)] + [(j, j + 1) for j in range(EARLY, TILES)]
+        rounded = {j0: keep.tile([P, (j1 - j0) * N], BF16, name=f"rounded{j0}") for j0, j1 in spans}
+        c_bf = keep.tile([P, T * 4], BF16, name="c_bf", align_bytes=64)
 
-        def quantize_wp():
-            nc.scalar.copy(wp_bf[:], wp_raw[:].rearrange("p j f -> p f j"))
-            nc.vector.quantize_mx(
-                out=wp_codes[:].bitcast(FP8X4), scales=wp_scales[:], in_=wp_bf[:].rearrange("p f j -> p (f j)")
-            )
-
-        def combine(ci, b, new_banks=()):
-            t0, tw = starts[ci], TOKEN_CHUNKS[ci]
-            first = t0 // P
-            for j, k in enumerate(new_banks):
-                sums[first + j] = banks[k]
-            terms = []
+        def combine(b, slot, runs, at=0):
+            t0, t1 = runs[0][0] * P, runs[-1][1] * P
             for i in range(2):
-                term = ring.tile([P, tw], F32, name=f"term{i}")
+                term = terms[slot][i][:, at : at + t1 - t0]
                 nc.vector.tensor_tensor(
-                    term[:], y[b][:].indirect(pos_sb[i][:, t0 // 16 : (t0 + tw) // 16]), gate_sb[ci][:, i, :], MULT
+                    term,
+                    y[b][:].indirect(pos_sb[i][:, t0 // 16 : t1 // 16]),
+                    gate_sb[i][:, t0:t1],
+                    MULT,
                 )
-                terms.append(term)
-            for j in range(tw // P):
-                for i in range(2):
-                    nc.tensor.matmul(
-                        sums[first + j][:, b * P : (b + 1) * P],
-                        lhsT=terms[i][:, j * P : (j + 1) * P],
-                        rhs=ident[:],
-                        is_transpose=True,
-                        start=(i == 0),
-                        stop=(i == 1),
-                    )
+                for j0, j1, k in runs:
+                    for j in range(j0, j1):
+                        nc.tensor.matmul(
+                            banks[k][:, (j - j0) * P : (j - j0 + 1) * P],
+                            lhsT=term[:, j * P - t0 : (j + 1) * P - t0],
+                            rhs=ident[:],
+                            is_transpose=True,
+                            start=(i == 0 and j == j0),
+                            stop=(i == 1 and j == j1 - 1),
+                        )
+            words = slice(b * P // 4, (b + 1) * P // 4)
+            for j0, j1, k in runs:
+                for a0, a1 in spans:
+                    if j0 <= a0 and a1 <= j1:
+                        nc.scalar.copy(
+                            rounded[a0][:].rearrange("p (j u w e) -> p j u w e", u=2, w=P, e=2)[:, :, :, words, :],
+                            banks[k][:, (a0 - j0) * P : (a1 - j0) * P].rearrange(
+                                "p (j w u e) -> p j u w e", u=2, w=P // 4, e=2
+                            ),
+                        )
 
-        def round_sums(j, b0, b1):
-            if b0 == 0:
-                rounded[j] = ring.tile([P, N], BF16, name="rounded")
-            w = slice(b0 * P // 4, b1 * P // 4)
+        def turn_back(j0, j1, k):
+            pairs = rounded[j0][:].bitcast(F32)
+            width = (j1 - j0) * 2 * P
+            for col in range(0, width, P):
+                nc.tensor.transpose(banks[k][:, col : col + P], pairs[:, col : col + P], ident[:])
             nc.scalar.copy(
-                rounded[j][:].rearrange("p (u w e) -> p u w e", u=2, e=2)[:, :, w, :],
-                sums[j][:].rearrange("p (w u e) -> p u w e", u=2, e=2)[:, :, w, :],
+                c_bf[:, j0 * N : j1 * N].bitcast(F32).rearrange("p (j t u) -> p j t u", t=P, u=2),
+                banks[k][:, 0:width].rearrange("p (j u t) -> p j t u", t=P, u=2),
             )
 
-        def turn_back(j0, j1, turn_banks):
-            c_bf[j0] = keep.tile([P, (j1 - j0) * N], BF16, name=f"c_bf{j0}", align_bytes=64)
-            for j in range(j0, j1):
-                if j not in rounded:
-                    round_sums(j, 0, NB)
-                back = banks[turn_banks[j - j0]]
-                pairs = rounded[j][:].bitcast(F32)
-                for u in range(2):
-                    nc.tensor.transpose(back[:, u * P : (u + 1) * P], pairs[:, u * P : (u + 1) * P], ident[:])
-                nc.scalar.copy(
-                    c_bf[j0][:, (j - j0) * N : (j - j0 + 1) * N].bitcast(F32).rearrange("p (t u) -> p t u", u=2),
-                    back[:, 0 : 2 * P].rearrange("p (u t) -> p t u", u=2),
-                )
-
-        def project(j0, j1, acc, evict):
+        def project(j0, j1, k, evict):
             t0, tw = j0 * P, (j1 - j0) * P
             c_codes = keep.tile([P, tw], U32, name=f"c_codes{j0}", align_bytes=64)
             c_scales = keep.tile([P, tw], U8, name=f"c_scales{j0}", align_bytes=64)
-            nc.vector.quantize_mx(out=c_codes[:].bitcast(FP8X4), scales=c_scales[:], in_=c_bf[j0][:])
+            nc.vector.quantize_mx(out=c_codes[:].bitcast(FP8X4), scales=c_scales[:], in_=c_bf[:, j0 * N : j1 * N])
             nc.tensor.matmul_mx(
-                out=acc[:, 0:tw],
+                out=banks[k][:, 0:tw],
                 lhsT=wp_codes[:].bitcast(FP8X4),
                 lhsT_scale=wp_scales[:],
                 rhs=c_codes[:].bitcast(FP8X4),
@@ -208,27 +194,22 @@ def tile_moe_nxt_lin_none_kernel(
                 stop=True,
             )
             res = keep.tile([P, tw], F32, name=f"res{j0}")
-            evict(res[:], acc[:, 0:tw])
+            evict(res[:], banks[k][:, 0:tw])
             nc.sync.dma_start(out[:, t0 : t0 + tw], res[:])
 
-        combine(0, 0, (2, 3, 4))
-        for b in range(1, NB):
-            combine(0, b)
-        quantize_wp()
-        combine(1, 0, (5, 6))
-        turn_back(0, 2, (7, 0))
-        turn_back(2, 3, (1,))
-        for b in range(1, NB):
-            combine(1, b)
-        project(0, 2, banks[4], nc.scalar.copy)
-        combine(2, 0, (2,))
-        turn_back(3, 5, (7, 0))
-        for b in range(1, NB - 1):
-            combine(2, b)
-        round_sums(5, 0, NB - 1)
-        combine(2, NB - 1, (3,))
-        round_sums(5, NB - 1, NB)
-        turn_back(5, 6, (1,))
-        project(2, 3, banks[5], nc.vector.tensor_copy)
-        project(3, 5, banks[6], nc.vector.tensor_copy)
-        project(5, 6, banks[7], nc.scalar.copy)
+        combine(0, 0, [(0, EARLY, 3)])
+        combine(1, 1, [(0, EARLY, 4)])
+        combine(2, 2, [(0, EARLY, 1)])
+        combine(3, 0, [(0, EARLY, 2)])
+        combine(0, 1, [(EARLY, TILES, 3)])
+        turn_back(0, 2, 4)
+        turn_back(2, 4, 5)
+        combine(1, 2, [(EARLY, TILES, 4)])
+        combine(2, 0, [(EARLY, TILES, 5)])
+        combine(3, 0, [(4, 5, 4)], 2 * P)
+        combine(3, 0, [(5, 6, 5)], 3 * P)
+        turn_back(4, 5, 6)
+        turn_back(5, 6, 7)
+        project(0, EARLY, 5, nc.scalar.copy)
+        project(4, 5, 0, nc.vector.tensor_copy)
+        project(5, 6, 1, nc.vector.tensor_copy)

@@ -79,11 +79,12 @@ def tile_moe_nxt_lin_none_kernel(
             )
         load_weight_words(0, 0, GROUP)
         load_weight_words(0, GROUP, E)
-        nc.sync.dma_start(wp_raw[:], wp.rearrange("(p j) f -> p j f", j=4))
         for i, pos in enumerate((pos1, pos2)):
             nc.sync.dma_start(pos_sb[i][:], pos)
             nc.sync.dma_start(gate_sb[i][:], gate[i, 0:P, :])
-        load_weight_words(1, 0, E)
+        for g in range(GROUPS):
+            load_weight_words(1, g * GROUP, (g + 1) * GROUP)
+        nc.sync.dma_start(wp_raw[:], wp.rearrange("(p j) f -> p j f", j=4))
 
         y = [keep.tile([P, S], F32, name=f"y{b}") for b in range(NB)]
         slot_scales = keep.tile([P, S], U8, name="slot_scales", align_bytes=64)
@@ -110,14 +111,13 @@ def tile_moe_nxt_lin_none_kernel(
             evict(y[b][:, first * C : last * C], banks[k][:, 0 : (last - first) * C])
 
         terms = [
-            [keep.tile([P, EARLY * P], F32, name=f"term{s}_{i}", align_bytes=64) for i in range(2)]
+            [keep.tile([P, T], F32, name=f"term{s}_{i}", align_bytes=64) for i in range(2)]
             for s in range(TERM_SLOTS)
         ]
-        wp_bf = terms[0][0][:, 0 : 2 * M].bitcast(BF16)
+        wp_bf = keep.tile([P, 4 * M], BF16, name="wp_bf", align_bytes=64)
         wp_codes = keep.tile([P, M], U32, name="wp_codes", align_bytes=64)
         wp_scales = keep.tile([P, M], U8, name="wp_scales", align_bytes=64)
 
-        nc.scalar.copy(wp_bf.rearrange("p (f j) -> p f j", j=4), wp_raw[:].rearrange("p j f -> p f j"))
         nc.vector.tensor_copy(slot_scales[:], xs[:].indirect(offs_sb[:]))
         gather_words(0, GROUP)
         experts(0, GROUP, 0, 0)
@@ -127,7 +127,6 @@ def tile_moe_nxt_lin_none_kernel(
         gather_words(E - 2, E - 1)
         gather_words(E - 1, E)
         experts(2 * GROUP, E - 2, 0, 2, nc.vector.tensor_copy)
-        nc.vector.quantize_mx(out=wp_codes[:].bitcast(FP8X4), scales=wp_scales[:], in_=wp_bf)
         experts(E - 2, E - 1, 0, 3)
         experts(E - 1, E, 0, 4)
         for b in range(1, NB):
@@ -136,12 +135,14 @@ def tile_moe_nxt_lin_none_kernel(
 
         spans = [(0, 2), (2, EARLY)] + [(j, j + 1) for j in range(EARLY, TILES)]
         rounded = {j0: keep.tile([P, (j1 - j0) * N], BF16, name=f"rounded{j0}") for j0, j1 in spans}
-        c_bf = keep.tile([P, T * 4], BF16, name="c_bf", align_bytes=64)
+        last_term = keep.tile([P, N], F32, name="last_term", align_bytes=64)
+        c_bf = {j0: keep.tile([P, (j1 - j0) * N], BF16, name=f"c_bf{j0}", align_bytes=64)[:] for j0, j1 in spans[1:]}
+        c_bf[0] = last_term[:].bitcast(BF16)
 
-        def combine(b, slot, runs, at=0):
+        def combine(b, pair, runs, at=0):
             t0, t1 = runs[0][0] * P, runs[-1][1] * P
             for i in range(2):
-                term = terms[slot][i][:, at : at + t1 - t0]
+                term = pair[i][:, at : at + t1 - t0]
                 nc.vector.tensor_tensor(
                     term,
                     y[b][:].indirect(pos_sb[i][:, t0 // 16 : t1 // 16]),
@@ -175,7 +176,7 @@ def tile_moe_nxt_lin_none_kernel(
             for col in range(0, width, P):
                 nc.tensor.transpose(banks[k][:, col : col + P], pairs[:, col : col + P], ident[:])
             nc.scalar.copy(
-                c_bf[:, j0 * N : j1 * N].bitcast(F32).rearrange("p (j t u) -> p j t u", t=P, u=2),
+                c_bf[j0].bitcast(F32).rearrange("p (j t u) -> p j t u", t=P, u=2),
                 banks[k][:, 0:width].rearrange("p (j u t) -> p j t u", t=P, u=2),
             )
 
@@ -183,7 +184,7 @@ def tile_moe_nxt_lin_none_kernel(
             t0, tw = j0 * P, (j1 - j0) * P
             c_codes = keep.tile([P, tw], U32, name=f"c_codes{j0}", align_bytes=64)
             c_scales = keep.tile([P, tw], U8, name=f"c_scales{j0}", align_bytes=64)
-            nc.vector.quantize_mx(out=c_codes[:].bitcast(FP8X4), scales=c_scales[:], in_=c_bf[:, j0 * N : j1 * N])
+            nc.vector.quantize_mx(out=c_codes[:].bitcast(FP8X4), scales=c_scales[:], in_=c_bf[j0])
             nc.tensor.matmul_mx(
                 out=banks[k][:, 0:tw],
                 lhsT=wp_codes[:].bitcast(FP8X4),
@@ -197,19 +198,21 @@ def tile_moe_nxt_lin_none_kernel(
             evict(res[:], banks[k][:, 0:tw])
             nc.sync.dma_start(out[:, t0 : t0 + tw], res[:])
 
-        combine(0, 0, [(0, EARLY, 3)])
-        combine(1, 1, [(0, EARLY, 4)])
-        combine(2, 2, [(0, EARLY, 1)])
-        combine(3, 0, [(0, EARLY, 2)])
-        combine(0, 1, [(EARLY, TILES, 3)])
+        combine(0, terms[0], [(0, EARLY, 2), (EARLY, TILES, 3)])
+        combine(1, terms[1], [(0, EARLY, 4)])
+        nc.scalar.copy(wp_bf[:].rearrange("p (f j) -> p f j", j=4), wp_raw[:].rearrange("p j f -> p f j"))
+        nc.vector.quantize_mx(out=wp_codes[:].bitcast(FP8X4), scales=wp_scales[:], in_=wp_bf[:])
+        combine(2, terms[2], [(0, EARLY, 0)])
+        combine(3, terms[0], [(0, EARLY, 1)])
+        combine(1, terms[1], [(EARLY, TILES, 2)])
         turn_back(0, 2, 4)
         turn_back(2, 4, 5)
-        combine(1, 2, [(EARLY, TILES, 4)])
-        combine(2, 0, [(EARLY, TILES, 5)])
-        combine(3, 0, [(4, 5, 4)], 2 * P)
-        combine(3, 0, [(5, 6, 5)], 3 * P)
+        combine(2, terms[2], [(EARLY, TILES, 1)])
+        combine(3, terms[2], [(4, 5, 2)], 2 * P)
+        project(0, 2, 0, nc.scalar.copy)
+        combine(3, (last_term, terms[2][1]), [(5, 6, 1)], 3 * P)
         turn_back(4, 5, 6)
         turn_back(5, 6, 7)
-        project(0, EARLY, 5, nc.scalar.copy)
-        project(4, 5, 0, nc.vector.tensor_copy)
-        project(5, 6, 1, nc.vector.tensor_copy)
+        project(2, 4, 1, nc.scalar.copy)
+        project(4, 5, 4, nc.vector.tensor_copy)
+        project(5, 6, 3, nc.vector.tensor_copy)

@@ -48,10 +48,13 @@ def tile_moe_nxt_lin_none_kernel(
         gate_sb = [keep.tile([P, T], F32, name=f"gate_sb{i}") for i in range(2)]
         wp_raw = keep.tile([P, 4, M], F32, name="wp_raw")
         ident = keep.tile([P, P], F32, name="ident")
+        gate_rows = keep.tile([P, P], F32, name="gate_rows")
+        gate_cols = keep.tile([P, 2 * TILES], F32, name="gate_cols")
         banks = [psum.tile([P, BANK], F32, name=f"bank{k}") for k in range(BANKS)]
 
         nc.vector.memset(ws[:].bitcast(I32), 0)
         nc.gpsimd.memset(xs[:, T:].bitcast(I32), 0)
+        nc.gpsimd.memset(gate_rows[:], 0.0)
         make_identity(nc, ident[:])
 
         ws_rows = w_scales.rearrange("e a (q r) n -> r q (e a) n", r=4)
@@ -72,6 +75,7 @@ def tile_moe_nxt_lin_none_kernel(
                 xs[32 * q : 32 * (q + 1), 0:T].bitcast(I32),
                 x_scales[0, 4 * q : 4 * q + 4, :].bitcast(I32).partition_broadcast(8),
             )
+        nc.scalar.dma_start(gate_rows[0 : 2 * TILES, :], gate[:, 0, :].rearrange("i (j t) -> i j t", t=P))
         nc.sync.dma_start(xw[:], x_words[0].rearrange("p t r -> p (t r)").bitcast(I32))
         for r in range(4):
             nc.sync.dma_start(
@@ -79,12 +83,23 @@ def tile_moe_nxt_lin_none_kernel(
             )
         load_weight_words(0, 0, GROUP)
         load_weight_words(0, GROUP, E)
-        for i, pos in enumerate((pos1, pos2)):
-            nc.sync.dma_start(pos_sb[i][:], pos)
-            nc.sync.dma_start(gate_sb[i][:], gate[i, 0:P, :])
+        nc.sync.dma_start(pos_sb[0][:], pos1)
+        nc.sync.dma_start(pos_sb[1][:], pos2)
         for g in range(GROUPS):
             load_weight_words(1, g * GROUP, (g + 1) * GROUP)
         nc.sync.dma_start(wp_raw[:], wp.rearrange("(p j) f -> p j f", j=4))
+
+        nc.tensor.transpose(banks[7][:, 0:P], gate_rows[:], ident[:])
+        nc.scalar.copy(gate_cols[:], banks[7][:, 0 : 2 * TILES])
+        for i in range(2):
+            for half in range(2):
+                bank = banks[4 + 2 * i + half]
+                for u in range(TILES // 2):
+                    col = i * TILES + half * TILES // 2 + u
+                    nc.tensor.transpose(
+                        bank[:, u * P : (u + 1) * P], gate_cols[:, col : col + 1].to_broadcast([P, P]), ident[:]
+                    )
+                nc.scalar.copy(gate_sb[i][:, half * T // 2 : (half + 1) * T // 2], bank[:, 0 : T // 2])
 
         y = [keep.tile([P, S], F32, name=f"y{b}") for b in range(NB)]
         slot_scales = keep.tile([P, S], U8, name="slot_scales", align_bytes=64)
@@ -138,6 +153,7 @@ def tile_moe_nxt_lin_none_kernel(
         last_term = keep.tile([P, N], F32, name="last_term", align_bytes=64)
         c_bf = {j0: keep.tile([P, (j1 - j0) * N], BF16, name=f"c_bf{j0}", align_bytes=64)[:] for j0, j1 in spans[1:]}
         c_bf[0] = last_term[:].bitcast(BF16)
+        last_pair = (last_term[:, 0 : 2 * P], last_term[:, 2 * P : 4 * P])
 
         def combine(b, pair, runs, at=0):
             t0, t1 = runs[0][0] * P, runs[-1][1] * P
@@ -203,16 +219,16 @@ def tile_moe_nxt_lin_none_kernel(
         nc.scalar.copy(wp_bf[:].rearrange("p (f j) -> p f j", j=4), wp_raw[:].rearrange("p j f -> p f j"))
         nc.vector.quantize_mx(out=wp_codes[:].bitcast(FP8X4), scales=wp_scales[:], in_=wp_bf[:])
         combine(2, terms[2], [(0, EARLY, 0)])
-        combine(3, terms[0], [(0, EARLY, 1)])
-        combine(1, terms[1], [(EARLY, TILES, 2)])
-        turn_back(0, 2, 4)
-        turn_back(2, 4, 5)
-        combine(2, terms[2], [(EARLY, TILES, 1)])
-        combine(3, terms[2], [(4, 5, 2)], 2 * P)
+        combine(3, terms[0], [(0, 2, 1), (2, EARLY, 5)])
+        turn_back(0, 2, 6)
+        combine(1, terms[1], [(EARLY, TILES, 1)])
+        turn_back(2, 4, 7)
+        combine(2, terms[2], [(EARLY, TILES, 5)])
+        combine(3, terms[2], [(4, 5, 1)], 2 * P)
         project(0, 2, 0, nc.scalar.copy)
-        combine(3, (last_term, terms[2][1]), [(5, 6, 1)], 3 * P)
-        turn_back(4, 5, 6)
-        turn_back(5, 6, 7)
-        project(2, 4, 1, nc.scalar.copy)
-        project(4, 5, 4, nc.vector.tensor_copy)
-        project(5, 6, 3, nc.vector.tensor_copy)
+        combine(3, last_pair, [(5, 6, 3)])
+        turn_back(4, 5, 4)
+        turn_back(5, 6, 6)
+        project(2, 4, 3, nc.scalar.copy)
+        project(4, 5, 7, nc.vector.tensor_copy)
+        project(5, 6, 2, nc.vector.tensor_copy)

@@ -43,7 +43,7 @@ def tile_moe_nxt_lin_none_kernel(
         pos_sb = [keep.tile([P, T // 16], U16, name=f"pos_sb{i}") for i in range(2)]
         xw = keep.tile([P, T], I32, name="xw", align_bytes=64)
         xs = keep.tile([P, SCALE_WINDOW], U8, name="xs", align_bytes=64)
-        ws = keep.tile([P, E * N], U8, name="ws", align_bytes=64)
+        ws = [keep.tile([P, E * HALF], U8, name=f"ws{h}", align_bytes=64) for h in range(2)]
         ww = [keep.tile([P, E * 2 * HALF], U8, name=f"ww{h}", align_bytes=64) for h in range(2)]
         gate_sb = [keep.tile([P, T], F32, name=f"gate_sb{i}") for i in range(2)]
         wp_raw = keep.tile([P, 4, M], F32, name="wp_raw")
@@ -52,13 +52,20 @@ def tile_moe_nxt_lin_none_kernel(
         gate_cols = keep.tile([P, 2 * TILES], F32, name="gate_cols")
         banks = [psum.tile([P, BANK], F32, name=f"bank{k}") for k in range(BANKS)]
 
-        nc.vector.memset(ws[:].bitcast(I32), 0)
-        nc.gpsimd.memset(xs[:, T:].bitcast(I32), 0)
-        nc.gpsimd.memset(gate_rows[:], 0.0)
+        nc.vector.memset(ws[0][:].bitcast(I32), 0)
+        nc.vector.memset(xs[:, T:].bitcast(I32), 0)
+        nc.vector.memset(ws[1][:].bitcast(I32), 0)
         make_identity(nc, ident[:])
 
         ws_rows = w_scales.rearrange("e a (q r) n -> r q (e a) n", r=4)
         ww_rows = w_words.rearrange("e a p n -> p (e a) n")
+
+        def load_weight_scales(h):
+            for r in range(4):
+                nc.sync.dma_start(
+                    ws[h][r:P:32, :].bitcast(I32).rearrange("q (e n) -> q e n", e=E),
+                    ws_rows[r][:, :, h * HALF : (h + 1) * HALF].bitcast(I32),
+                )
 
         def load_weight_words(h, first, last):
             nc.sync.dma_start(
@@ -75,16 +82,14 @@ def tile_moe_nxt_lin_none_kernel(
                 xs[32 * q : 32 * (q + 1), 0:T].bitcast(I32),
                 x_scales[0, 4 * q : 4 * q + 4, :].bitcast(I32).partition_broadcast(8),
             )
-        nc.scalar.dma_start(gate_rows[0 : 2 * TILES, :], gate[:, 0, :].rearrange("i (j t) -> i j t", t=P))
         nc.sync.dma_start(xw[:], x_words[0].rearrange("p t r -> p (t r)").bitcast(I32))
-        for r in range(4):
-            nc.sync.dma_start(
-                ws[r:P:32, :].bitcast(I32).rearrange("q (e n) -> q e n", e=E), ws_rows[r].bitcast(I32)
-            )
-        load_weight_words(0, 0, GROUP)
-        load_weight_words(0, GROUP, E)
+        nc.sync.dma_start(gate_rows[:], gate.rearrange("i n (j t) -> (n j) i t", t=P)[0 : P // 2])
+        load_weight_scales(0)
+        for g in range(GROUPS):
+            load_weight_words(0, g * GROUP, (g + 1) * GROUP)
         nc.sync.dma_start(pos_sb[0][:], pos1)
         nc.sync.dma_start(pos_sb[1][:], pos2)
+        load_weight_scales(1)
         for g in range(GROUPS):
             load_weight_words(1, g * GROUP, (g + 1) * GROUP)
         nc.sync.dma_start(wp_raw[:], wp.rearrange("(p j) f -> p j f", j=4))
@@ -95,7 +100,7 @@ def tile_moe_nxt_lin_none_kernel(
             for half in range(2):
                 bank = banks[4 + 2 * i + half]
                 for u in range(TILES // 2):
-                    col = i * TILES + half * TILES // 2 + u
+                    col = 2 * (half * TILES // 2 + u) + i
                     nc.tensor.transpose(
                         bank[:, u * P : (u + 1) * P], gate_cols[:, col : col + 1].to_broadcast([P, P]), ident[:]
                     )
@@ -117,7 +122,7 @@ def tile_moe_nxt_lin_none_kernel(
                 nc.tensor.matmul_mx(
                     out=banks[k][:, (e - first) * C : (e - first + 1) * C],
                     lhsT=ww[h][:, 2 * (e * HALF + col) : 2 * (e * HALF + col + P)].bitcast(FP4X4),
-                    lhsT_scale=ws[:, e * N + b * P : e * N + (b + 1) * P],
+                    lhsT_scale=ws[h][:, e * HALF + col : e * HALF + col + P],
                     rhs=slot_words[e].bitcast(FP8X4),
                     rhs_scale=slot_scales[:, e * C : (e + 1) * C],
                     start=True,

@@ -85,14 +85,15 @@ def tile_moe_nxt_lin_none_kernel(
         nc.sync.dma_start(xw[:], x_words[0].rearrange("p t r -> p (t r)").bitcast(I32))
         nc.sync.dma_start(gate_rows[:], gate.rearrange("i n (j t) -> (n j) i t", t=P)[0 : P // 2])
         load_weight_scales(0)
-        for g in range(GROUPS):
+        load_weight_words(0, 0, GROUP)
+        nc.sync.dma_start(wp_raw[:], wp.rearrange("(p j) f -> p j f", j=4))
+        for g in range(1, GROUPS):
             load_weight_words(0, g * GROUP, (g + 1) * GROUP)
         nc.sync.dma_start(pos_sb[0][:], pos1)
         nc.sync.dma_start(pos_sb[1][:], pos2)
         load_weight_scales(1)
         for g in range(GROUPS):
             load_weight_words(1, g * GROUP, (g + 1) * GROUP)
-        nc.sync.dma_start(wp_raw[:], wp.rearrange("(p j) f -> p j f", j=4))
 
         nc.tensor.transpose(banks[7][:, 0:P], gate_rows[:], ident[:])
         nc.scalar.copy(gate_cols[:], banks[7][:, 0 : 2 * TILES])
@@ -135,6 +136,7 @@ def tile_moe_nxt_lin_none_kernel(
             for s in range(TERM_SLOTS)
         ]
         wp_bf = keep.tile([P, 4 * M], BF16, name="wp_bf", align_bytes=64)
+        nc.scalar.copy(wp_bf[:].rearrange("p (f j) -> p f j", j=4), wp_raw[:].rearrange("p j f -> p f j"))
         wp_codes = keep.tile([P, M], U32, name="wp_codes", align_bytes=64)
         wp_scales = keep.tile([P, M], U8, name="wp_scales", align_bytes=64)
 
@@ -146,6 +148,7 @@ def tile_moe_nxt_lin_none_kernel(
         gather_words(2 * GROUP, E - 2)
         gather_words(E - 2, E - 1)
         gather_words(E - 1, E)
+        nc.vector.quantize_mx(out=wp_codes[:].bitcast(FP8X4), scales=wp_scales[:], in_=wp_bf[:])
         experts(2 * GROUP, E - 2, 0, 2, nc.vector.tensor_copy)
         experts(E - 2, E - 1, 0, 3)
         experts(E - 1, E, 0, 4)
@@ -154,7 +157,7 @@ def tile_moe_nxt_lin_none_kernel(
                 experts(GROUP * g, GROUP * (g + 1), b, 2 + g)
 
         spans = [(0, 2), (2, EARLY)] + [(j, j + 1) for j in range(EARLY, TILES)]
-        rounded = {j0: keep.tile([P, (j1 - j0) * N], BF16, name=f"rounded{j0}") for j0, j1 in spans}
+        rounded = keep.tile([P, TILES * N], BF16, name="rounded")
         last_term = keep.tile([P, N], F32, name="last_term", align_bytes=64)
         c_bf = {j0: keep.tile([P, (j1 - j0) * N], BF16, name=f"c_bf{j0}", align_bytes=64)[:] for j0, j1 in spans[1:]}
         c_bf[0] = last_term[:].bitcast(BF16)
@@ -182,17 +185,13 @@ def tile_moe_nxt_lin_none_kernel(
                         )
             words = slice(b * P // 4, (b + 1) * P // 4)
             for j0, j1, k in runs:
-                for a0, a1 in spans:
-                    if j0 <= a0 and a1 <= j1:
-                        nc.scalar.copy(
-                            rounded[a0][:].rearrange("p (j u w e) -> p j u w e", u=2, w=P, e=2)[:, :, :, words, :],
-                            banks[k][:, (a0 - j0) * P : (a1 - j0) * P].rearrange(
-                                "p (j w u e) -> p j u w e", u=2, w=P // 4, e=2
-                            ),
-                        )
+                nc.scalar.copy(
+                    rounded[:, j0 * N : j1 * N].rearrange("p (j u w e) -> p j u w e", u=2, w=P, e=2)[:, :, :, words, :],
+                    banks[k][:, 0 : (j1 - j0) * P].rearrange("p (j w u e) -> p j u w e", u=2, w=P // 4, e=2),
+                )
 
         def turn_back(j0, j1, k):
-            pairs = rounded[j0][:].bitcast(F32)
+            pairs = rounded[:, j0 * N : j1 * N].bitcast(F32)
             width = (j1 - j0) * 2 * P
             for col in range(0, width, P):
                 nc.tensor.transpose(banks[k][:, col : col + P], pairs[:, col : col + P], ident[:])
@@ -221,8 +220,6 @@ def tile_moe_nxt_lin_none_kernel(
 
         combine(0, terms[0], [(0, EARLY, 2), (EARLY, TILES, 3)])
         combine(1, terms[1], [(0, EARLY, 4)])
-        nc.scalar.copy(wp_bf[:].rearrange("p (f j) -> p f j", j=4), wp_raw[:].rearrange("p j f -> p f j"))
-        nc.vector.quantize_mx(out=wp_codes[:].bitcast(FP8X4), scales=wp_scales[:], in_=wp_bf[:])
         combine(2, terms[2], [(0, EARLY, 0)])
         combine(3, terms[0], [(0, 2, 1), (2, EARLY, 5)])
         turn_back(0, 2, 6)

@@ -20,14 +20,14 @@ U8 = mybir.dt.uint8
 FP8X4 = mybir.dt.float8_e4m3fn_x4
 FP4X4 = mybir.dt.float4_e2m1fn_x4
 MULT = mybir.AluOpType.mult
+ADD = mybir.AluOpType.add
+COPY = mybir.ActivationFunctionType.Copy
 
 GROUP = BANK // C
 GROUPS = E // GROUP
-HALF = N // 2
-SCALE_WINDOW = 4 * S // 3
+SCALE_WINDOW = 1408
 TILES = T // P
-EARLY = 4
-TERM_SLOTS = 3
+FUSED = 4
 BANKS = 8
 
 
@@ -43,37 +43,21 @@ def tile_moe_nxt_lin_none_kernel(
         pos_sb = [keep.tile([P, T // 16], U16, name=f"pos_sb{i}") for i in range(2)]
         xw = keep.tile([P, T], I32, name="xw", align_bytes=64)
         xs = keep.tile([P, SCALE_WINDOW], U8, name="xs", align_bytes=64)
-        ws = [keep.tile([P, E * HALF], U8, name=f"ws{h}", align_bytes=64) for h in range(2)]
-        ww = [keep.tile([P, E * 2 * HALF], U8, name=f"ww{h}", align_bytes=64) for h in range(2)]
-        gate_sb = [keep.tile([P, T], F32, name=f"gate_sb{i}") for i in range(2)]
+        ws = keep.tile([P, E * N], U8, name="ws", align_bytes=64)
+        ww = [keep.tile([P, GROUP * 2 * N], U8, name=f"ww{g}", align_bytes=64) for g in range(GROUPS)]
+        gate_sb = [keep.tile([P, FUSED * P], F32, name=f"gate_sb{i}") for i in range(2)]
         wp_raw = keep.tile([P, 4, M], F32, name="wp_raw")
         ident = keep.tile([P, P], F32, name="ident")
-        gate_rows = keep.tile([P, P], F32, name="gate_rows")
+        gate_rows = keep.tile([P, P], F32, name="gate_rows", tag="rows_then_scales", align_bytes=64)
         gate_cols = keep.tile([P, 2 * TILES], F32, name="gate_cols")
         banks = [psum.tile([P, BANK], F32, name=f"bank{k}") for k in range(BANKS)]
 
-        nc.vector.memset(ws[0][:].bitcast(I32), 0)
         nc.vector.memset(xs[:, T:].bitcast(I32), 0)
-        nc.vector.memset(ws[1][:].bitcast(I32), 0)
+        nc.vector.memset(ws[:].bitcast(I32), 0)
         make_identity(nc, ident[:])
 
         ws_rows = w_scales.rearrange("e a (q r) n -> r q (e a) n", r=4)
         ww_rows = w_words.rearrange("e a p n -> p (e a) n")
-
-        def load_weight_scales(h):
-            for r in range(4):
-                nc.sync.dma_start(
-                    ws[h][r:P:32, :].bitcast(I32).rearrange("q (e n) -> q e n", e=E),
-                    ws_rows[r][:, :, h * HALF : (h + 1) * HALF].bitcast(I32),
-                )
-
-        def load_weight_words(h, first, last):
-            nc.sync.dma_start(
-                ww[h][:, first * 2 * HALF : last * 2 * HALF]
-                .bitcast(I32)
-                .rearrange("p (e n) -> p e n", e=last - first),
-                ww_rows[:, first:last, 2 * h * HALF : 2 * (h + 1) * HALF].bitcast(I32),
-            )
 
         nc.sync.dma_start(offs_sb[:], offs)
         for q in range(4):
@@ -84,32 +68,39 @@ def tile_moe_nxt_lin_none_kernel(
             )
         nc.sync.dma_start(xw[:], x_words[0].rearrange("p t r -> p (t r)").bitcast(I32))
         nc.sync.dma_start(gate_rows[:], gate.rearrange("i n (j t) -> (n j) i t", t=P)[0 : P // 2])
-        load_weight_scales(0)
-        load_weight_words(0, 0, GROUP)
+        for r in range(4):
+            nc.sync.dma_start(
+                ws[r:P:32, :].bitcast(I32).rearrange("q (e n) -> q e n", e=E), ws_rows[r].bitcast(I32)
+            )
+        for g in range(GROUPS):
+            nc.sync.dma_start(
+                ww[g][:].bitcast(I32).rearrange("p (e n) -> p e n", e=GROUP),
+                ww_rows[:, g * GROUP : (g + 1) * GROUP, :].bitcast(I32),
+            )
         nc.sync.dma_start(wp_raw[:], wp.rearrange("(p j) f -> p j f", j=4))
-        for g in range(1, GROUPS):
-            load_weight_words(0, g * GROUP, (g + 1) * GROUP)
         nc.sync.dma_start(pos_sb[0][:], pos1)
         nc.sync.dma_start(pos_sb[1][:], pos2)
-        load_weight_scales(1)
-        for g in range(GROUPS):
-            load_weight_words(1, g * GROUP, (g + 1) * GROUP)
 
         nc.tensor.transpose(banks[7][:, 0:P], gate_rows[:], ident[:])
         nc.scalar.copy(gate_cols[:], banks[7][:, 0 : 2 * TILES])
         for i in range(2):
-            for half in range(2):
-                bank = banks[4 + 2 * i + half]
-                for u in range(TILES // 2):
-                    col = 2 * (half * TILES // 2 + u) + i
-                    nc.tensor.transpose(
-                        bank[:, u * P : (u + 1) * P], gate_cols[:, col : col + 1].to_broadcast([P, P]), ident[:]
-                    )
-                nc.scalar.copy(gate_sb[i][:, half * T // 2 : (half + 1) * T // 2], bank[:, 0 : T // 2])
+            bank = banks[5 + i]
+            for j in range(FUSED):
+                col = 2 * j + i
+                nc.tensor.transpose(
+                    bank[:, j * P : (j + 1) * P], gate_cols[:, col : col + 1].to_broadcast([P, P]), ident[:]
+                )
+            nc.scalar.copy(gate_sb[i][:], bank[:])
 
         y = [keep.tile([P, S], F32, name=f"y{b}") for b in range(NB)]
-        slot_scales = keep.tile([P, S], U8, name="slot_scales", align_bytes=64)
+        slot_scales = {}
         slot_words = {}
+
+        def gather_scales(first, last, tag):
+            tile = keep.tile([P, (last - first) * C], U8, name=f"scales{first}", tag=tag, align_bytes=64)
+            nc.vector.tensor_copy(tile[:], xs[:].indirect(offs_sb[:, first * C // 16 : last * C // 16]))
+            for e in range(first, last):
+                slot_scales[e] = tile[:, (e - first) * C : (e - first + 1) * C]
 
         def gather_words(first, last):
             tile = keep.tile([P, (last - first) * C], U32, name=f"words{first}", align_bytes=64)
@@ -118,85 +109,98 @@ def tile_moe_nxt_lin_none_kernel(
                 slot_words[e] = tile[:, (e - first) * C : (e - first + 1) * C]
 
         def experts(first, last, b, k, evict=nc.scalar.copy):
-            h, col = divmod(b * P, HALF)
             for e in range(first, last):
+                g, u = divmod(e, GROUP)
+                col = u * N + b * P
                 nc.tensor.matmul_mx(
                     out=banks[k][:, (e - first) * C : (e - first + 1) * C],
-                    lhsT=ww[h][:, 2 * (e * HALF + col) : 2 * (e * HALF + col + P)].bitcast(FP4X4),
-                    lhsT_scale=ws[h][:, e * HALF + col : e * HALF + col + P],
+                    lhsT=ww[g][:, 2 * col : 2 * (col + P)].bitcast(FP4X4),
+                    lhsT_scale=ws[:, e * N + b * P : e * N + (b + 1) * P],
                     rhs=slot_words[e].bitcast(FP8X4),
-                    rhs_scale=slot_scales[:, e * C : (e + 1) * C],
+                    rhs_scale=slot_scales[e],
                     start=True,
                     stop=True,
                 )
             evict(y[b][:, first * C : last * C], banks[k][:, 0 : (last - first) * C])
 
-        terms = [
-            [keep.tile([P, T], F32, name=f"term{s}_{i}", align_bytes=64) for i in range(2)]
-            for s in range(TERM_SLOTS)
-        ]
         wp_bf = keep.tile([P, 4 * M], BF16, name="wp_bf", align_bytes=64)
-        nc.scalar.copy(wp_bf[:].rearrange("p (f j) -> p f j", j=4), wp_raw[:].rearrange("p j f -> p f j"))
+        nc.gpsimd.tensor_copy(wp_bf[:].rearrange("p (f j) -> p f j", j=4), wp_raw[:].rearrange("p j f -> p f j"))
         wp_codes = keep.tile([P, M], U32, name="wp_codes", align_bytes=64)
         wp_scales = keep.tile([P, M], U8, name="wp_scales", align_bytes=64)
 
-        nc.vector.tensor_copy(slot_scales[:], xs[:].indirect(offs_sb[:]))
+        gather_scales(0, 2 * GROUP, "first_scales")
         gather_words(0, GROUP)
-        experts(0, GROUP, 0, 0)
+        for b in range(NB):
+            experts(0, GROUP, b, b)
         gather_words(GROUP, 2 * GROUP)
-        experts(GROUP, 2 * GROUP, 0, 1)
+        experts(GROUP, 2 * GROUP, 0, 4)
+        experts(GROUP, 2 * GROUP, 1, 5)
+        gather_scales(2 * GROUP, E, "rows_then_scales")
         gather_words(2 * GROUP, E - 2)
         gather_words(E - 2, E - 1)
         gather_words(E - 1, E)
+        experts(GROUP, 2 * GROUP, 2, 6, nc.vector.tensor_copy)
+        experts(2 * GROUP, E - 2, 0, 7, nc.vector.tensor_copy)
         nc.vector.quantize_mx(out=wp_codes[:].bitcast(FP8X4), scales=wp_scales[:], in_=wp_bf[:])
-        experts(2 * GROUP, E - 2, 0, 2, nc.vector.tensor_copy)
-        experts(E - 2, E - 1, 0, 3)
-        experts(E - 1, E, 0, 4)
-        for b in range(1, NB):
-            for g in range(GROUPS):
-                experts(GROUP * g, GROUP * (g + 1), b, 2 + g)
+        experts(E - 2, E - 1, 0, 0)
+        experts(E - 1, E, 0, 1)
+        experts(2 * GROUP, E, 1, 2)
 
-        spans = [(0, 2), (2, EARLY)] + [(j, j + 1) for j in range(EARLY, TILES)]
-        rounded = keep.tile([P, TILES * N], BF16, name="rounded")
-        last_term = keep.tile([P, N], F32, name="last_term", align_bytes=64)
-        c_bf = {j0: keep.tile([P, (j1 - j0) * N], BF16, name=f"c_bf{j0}", align_bytes=64)[:] for j0, j1 in spans[1:]}
-        c_bf[0] = last_term[:].bitcast(BF16)
-        last_pair = (last_term[:, 0 : 2 * P], last_term[:, 2 * P : 4 * P])
+        rounded = keep.tile([P, FUSED * N], BF16, name="rounded")
+        plain_rounded = keep.tile([P, (TILES - FUSED) * N], BF16, name="plain_rounded")
+        first_terms = [keep.tile([P, N], F32, name=f"first_terms{j}") for j in range(FUSED, TILES)]
+        c_bf = {}
 
-        def combine(b, pair, runs, at=0):
-            t0, t1 = runs[0][0] * P, runs[-1][1] * P
-            for i in range(2):
-                term = pair[i][:, at : at + t1 - t0]
-                nc.vector.tensor_tensor(
-                    term,
-                    y[b][:].indirect(pos_sb[i][:, t0 // 16 : t1 // 16]),
-                    gate_sb[i][:, t0:t1],
-                    MULT,
-                )
-                for j0, j1, k in runs:
+        def fused(blocks, j0, j1, k, pair=None):
+            t0, t1 = j0 * P, j1 * P
+            nb = len(blocks)
+            for x, b in enumerate(blocks):
+                for i in range(2):
+                    if pair is None:
+                        term = keep.tile([P, t1 - t0], F32, name=f"term{b}_{j0}_{i}")[:]
+                    else:
+                        term = pair[i]
+                    nc.vector.tensor_tensor(
+                        term, y[b][:].indirect(pos_sb[i][:, t0 // 16 : t1 // 16]), gate_sb[i][:, t0:t1], MULT
+                    )
                     for j in range(j0, j1):
+                        col = ((j - j0) * nb + x) * P
                         nc.tensor.matmul(
-                            banks[k][:, (j - j0) * P : (j - j0 + 1) * P],
+                            banks[k][:, col : col + P],
                             lhsT=term[:, j * P - t0 : (j + 1) * P - t0],
                             rhs=ident[:],
                             is_transpose=True,
-                            start=(i == 0 and j == j0),
-                            stop=(i == 1 and j == j1 - 1),
+                            start=(x == 0 and i == 0 and j == j0),
+                            stop=(x == nb - 1 and i == 1 and j == j1 - 1),
                         )
-            words = slice(b * P // 4, (b + 1) * P // 4)
-            for j0, j1, k in runs:
-                nc.scalar.copy(
-                    rounded[:, j0 * N : j1 * N].rearrange("p (j u w e) -> p j u w e", u=2, w=P, e=2)[:, :, :, words, :],
-                    banks[k][:, 0 : (j1 - j0) * P].rearrange("p (j w u e) -> p j u w e", u=2, w=P // 4, e=2),
-                )
+
+        def round_bank(blocks, j0, j1, k):
+            nb = len(blocks)
+            words = slice(blocks[0] * P // 4, (blocks[-1] + 1) * P // 4)
+            nc.scalar.copy(
+                rounded[:, j0 * N : j1 * N].rearrange("p (j u w e) -> p j u w e", u=2, w=P, e=2)[:, :, :, words, :],
+                banks[k][:, 0 : (j1 - j0) * nb * P].rearrange("p (j w u e) -> p j u w e", u=2, w=nb * P // 4, e=2),
+            )
+
+        def plain(b, i, k0):
+            term = keep.tile([P, T - FUSED * P], F32, name=f"plain{b}_{i}")
+            nc.scalar.activation(term[:], y[b][:].indirect(pos_sb[i][:, FUSED * P // 16 :]), COPY)
+            for j in range(TILES - FUSED):
+                nc.tensor.transpose(banks[k0[j]][:, b * P : (b + 1) * P], term[:, j * P : (j + 1) * P], ident[:])
 
         def turn_back(j0, j1, k):
-            pairs = rounded[:, j0 * N : j1 * N].bitcast(F32)
             width = (j1 - j0) * 2 * P
-            for col in range(0, width, P):
-                nc.tensor.transpose(banks[k][:, col : col + P], pairs[:, col : col + P], ident[:])
+            for j in range(j0, j1):
+                for u in range(2):
+                    col = (2 * (j - j0) + u) * P
+                    if j < FUSED:
+                        pairs = rounded[:, j * N : (j + 1) * N].bitcast(F32)[:, u * P : (u + 1) * P]
+                    else:
+                        pairs = plain_rounded[:, (j - FUSED) * N : (j - FUSED + 1) * N].bitcast(F32)[:, u : 2 * P : 2]
+                    nc.tensor.transpose(banks[k][:, col : col + P], pairs, ident[:])
+            c_bf[j0] = keep.tile([P, (j1 - j0) * N], BF16, name=f"c_bf{j0}", align_bytes=64)
             nc.scalar.copy(
-                c_bf[j0].bitcast(F32).rearrange("p (j t u) -> p j t u", t=P, u=2),
+                c_bf[j0][:].bitcast(F32).rearrange("p (j t u) -> p j t u", t=P, u=2),
                 banks[k][:, 0:width].rearrange("p (j u t) -> p j t u", t=P, u=2),
             )
 
@@ -204,7 +208,7 @@ def tile_moe_nxt_lin_none_kernel(
             t0, tw = j0 * P, (j1 - j0) * P
             c_codes = keep.tile([P, tw], U32, name=f"c_codes{j0}", align_bytes=64)
             c_scales = keep.tile([P, tw], U8, name=f"c_scales{j0}", align_bytes=64)
-            nc.vector.quantize_mx(out=c_codes[:].bitcast(FP8X4), scales=c_scales[:], in_=c_bf[j0])
+            nc.vector.quantize_mx(out=c_codes[:].bitcast(FP8X4), scales=c_scales[:], in_=c_bf[j0][:])
             nc.tensor.matmul_mx(
                 out=banks[k][:, 0:tw],
                 lhsT=wp_codes[:].bitcast(FP8X4),
@@ -218,19 +222,49 @@ def tile_moe_nxt_lin_none_kernel(
             evict(res[:], banks[k][:, 0:tw])
             nc.sync.dma_start(out[:, t0 : t0 + tw], res[:])
 
-        combine(0, terms[0], [(0, EARLY, 2), (EARLY, TILES, 3)])
-        combine(1, terms[1], [(0, EARLY, 4)])
-        combine(2, terms[2], [(0, EARLY, 0)])
-        combine(3, terms[0], [(0, 2, 1), (2, EARLY, 5)])
+        first_banks, second_banks = (7, 0), (2, 3)
+        plain(0, 0, first_banks)
+        plain(1, 0, first_banks)
+        fused([0], 0, FUSED, 6)
+        experts(GROUP, 2 * GROUP, 3, 3)
+        experts(2 * GROUP, E, 2, 4)
+        plain(2, 0, first_banks)
+        experts(2 * GROUP, E, 3, 5)
+        plain(3, 0, first_banks)
+        fused([1], 0, FUSED, 1)
+        plain(0, 1, second_banks)
+        for j in range(FUSED, TILES):
+            nc.scalar.activation(
+                first_terms[j - FUSED][:], banks[first_banks[j - FUSED]][:], COPY, scale=gate_cols[:, 2 * j : 2 * j + 1]
+            )
+        plain(1, 1, second_banks)
+        fused([2, 3], 0, 2, 4)
+        plain(2, 1, second_banks)
+        plain(3, 1, second_banks)
+        round_bank([0], 0, FUSED, 6)
+        round_bank([1], 0, FUSED, 1)
+        round_bank([2, 3], 0, 2, 4)
+        fused([2], 2, FUSED, 5)
+        for j in range(FUSED, TILES):
+            nc.vector.scalar_tensor_tensor(
+                plain_rounded[:, (j - FUSED) * N : (j - FUSED + 1) * N],
+                banks[second_banks[j - FUSED]][:],
+                gate_cols[:, 2 * j + 1 : 2 * j + 2],
+                first_terms[j - FUSED][:],
+                MULT,
+                ADD,
+            )
         turn_back(0, 2, 6)
-        combine(1, terms[1], [(EARLY, TILES, 1)])
-        turn_back(2, 4, 7)
-        combine(2, terms[2], [(EARLY, TILES, 5)])
-        combine(3, terms[2], [(4, 5, 1)], 2 * P)
-        project(0, 2, 0, nc.scalar.copy)
-        combine(3, last_pair, [(5, 6, 3)])
-        turn_back(4, 5, 4)
-        turn_back(5, 6, 6)
-        project(2, 4, 3, nc.scalar.copy)
-        project(4, 5, 7, nc.vector.tensor_copy)
-        project(5, 6, 2, nc.vector.tensor_copy)
+        round_bank([2], 2, FUSED, 5)
+        turn_back(FUSED, TILES, 1)
+        last = first_terms[-1]
+        fused([3], 2, 3, 7, (last[:, 0:P], last[:, P : 2 * P]))
+        fused([3], 3, 4, 0, (last[:, 2 * P : 3 * P], last[:, 3 * P : 4 * P]))
+        round_bank([3], 2, 3, 7)
+        round_bank([3], 3, 4, 0)
+        project(0, 2, 2, nc.scalar.copy)
+        project(FUSED, TILES, 3, nc.scalar.copy)
+        turn_back(2, 3, 4)
+        turn_back(3, 4, 5)
+        project(2, 3, 6, nc.vector.tensor_copy)
+        project(3, 4, 1, nc.vector.tensor_copy)

@@ -24,7 +24,6 @@ ADD = mybir.AluOpType.add
 COPY = mybir.ActivationFunctionType.Copy
 
 GROUP = BANK // C
-GROUPS = E // GROUP
 SCALE_WINDOW = 1408
 TILES = T // P
 FUSED = 4
@@ -44,7 +43,6 @@ def tile_moe_nxt_lin_none_kernel(
         xw = keep.tile([P, T], I32, name="xw", align_bytes=64)
         xs = keep.tile([P, SCALE_WINDOW], U8, name="xs", align_bytes=64)
         ws = keep.tile([P, E * N], U8, name="ws", align_bytes=64)
-        ww = [keep.tile([P, GROUP * 2 * N], U8, name=f"ww{g}", align_bytes=64) for g in range(GROUPS)]
         gate_sb = [keep.tile([P, FUSED * P], F32, name=f"gate_sb{i}") for i in range(2)]
         wp_raw = keep.tile([P, 4, M], F32, name="wp_raw")
         ident = keep.tile([P, P], F32, name="ident")
@@ -72,14 +70,28 @@ def tile_moe_nxt_lin_none_kernel(
             nc.sync.dma_start(
                 ws[r:P:32, :].bitcast(I32).rearrange("q (e n) -> q e n", e=E), ws_rows[r].bitcast(I32)
             )
-        for g in range(GROUPS):
-            nc.sync.dma_start(
-                ww[g][:].bitcast(I32).rearrange("p (e n) -> p e n", e=GROUP),
-                ww_rows[:, g * GROUP : (g + 1) * GROUP, :].bitcast(I32),
-            )
-        nc.sync.dma_start(wp_raw[:], wp.rearrange("(p j) f -> p j f", j=4))
         nc.sync.dma_start(pos_sb[0][:], pos1)
         nc.sync.dma_start(pos_sb[1][:], pos2)
+        weight_words = {}
+
+        def load_weights(g, b0, b1):
+            width = 2 * P * (b1 - b0)
+            tile = keep.tile([P, GROUP * width], U8, name=f"ww{g}_{b0}", align_bytes=64)
+            nc.sync.dma_start(
+                tile[:].bitcast(I32).rearrange("p (e n) -> p e n", e=GROUP),
+                ww_rows[:, g * GROUP : (g + 1) * GROUP, 2 * P * b0 : 2 * P * b1].bitcast(I32),
+            )
+            for u in range(GROUP):
+                for b in range(b0, b1):
+                    col = u * width + 2 * P * (b - b0)
+                    weight_words[g * GROUP + u, b] = tile[:, col : col + 2 * P]
+
+        load_weights(0, 0, 2)
+        load_weights(0, 2, NB)
+        load_weights(1, 0, NB)
+        load_weights(2, 0, 2)
+        nc.sync.dma_start(wp_raw[:], wp.rearrange("(p j) f -> p j f", j=4))
+        load_weights(2, 2, NB)
 
         nc.tensor.transpose(banks[7][:, 0:P], gate_rows[:], ident[:])
         nc.scalar.copy(gate_cols[:], banks[7][:, 0 : 2 * TILES])
@@ -110,11 +122,9 @@ def tile_moe_nxt_lin_none_kernel(
 
         def experts(first, last, b, k, evict=nc.scalar.copy):
             for e in range(first, last):
-                g, u = divmod(e, GROUP)
-                col = u * N + b * P
                 nc.tensor.matmul_mx(
                     out=banks[k][:, (e - first) * C : (e - first + 1) * C],
-                    lhsT=ww[g][:, 2 * col : 2 * (col + P)].bitcast(FP4X4),
+                    lhsT=weight_words[e, b].bitcast(FP4X4),
                     lhsT_scale=ws[:, e * N + b * P : e * N + (b + 1) * P],
                     rhs=slot_words[e].bitcast(FP8X4),
                     rhs_scale=slot_scales[e],

@@ -36,6 +36,7 @@ def tile_moe_nxt_lin_none_kernel(
     nc = tc.nc
     with ExitStack() as ctx:
         keep = ctx.enter_context(tc.tile_pool(name="keep", bufs=1))
+        shared = ctx.enter_context(tc.tile_pool(name="shared", bufs=1))
         psum = ctx.enter_context(tc.psum_pool(name="psum", bufs=1))
 
         offs_sb = keep.tile([P, S // 16], U16, name="offs_sb")
@@ -46,7 +47,8 @@ def tile_moe_nxt_lin_none_kernel(
         gate_sb = [keep.tile([P, FUSED * P], F32, name=f"gate_sb{i}") for i in range(2)]
         wp_raw = keep.tile([P, 4, M], F32, name="wp_raw")
         ident = keep.tile([P, P], F32, name="ident")
-        gate_rows = keep.tile([P, P], F32, name="gate_rows", tag="rows_then_scales", align_bytes=64)
+        late = 4 * (S * NB + N * (TILES - FUSED))
+        gate_rows = shared.tile([P, P], F32, name="gate_rows", align_bytes=64, offset=late + GROUP * C - 64)
         gate_cols = keep.tile([P, 2 * TILES], F32, name="gate_cols")
         banks = [psum.tile([P, BANK], F32, name=f"bank{k}") for k in range(BANKS)]
 
@@ -88,10 +90,11 @@ def tile_moe_nxt_lin_none_kernel(
 
         load_weights(0, 0, 2)
         load_weights(0, 2, NB)
-        load_weights(1, 0, NB)
+        load_weights(1, 0, 2)
         load_weights(2, 0, 2)
-        nc.sync.dma_start(wp_raw[:], wp.rearrange("(p j) f -> p j f", j=4))
+        load_weights(1, 2, NB)
         load_weights(2, 2, NB)
+        nc.sync.dma_start(wp_raw[:], wp.rearrange("(p j) f -> p j f", j=4))
 
         nc.tensor.transpose(banks[7][:, 0:P], gate_rows[:], ident[:])
         nc.scalar.copy(gate_cols[:], banks[7][:, 0 : 2 * TILES])
@@ -104,19 +107,17 @@ def tile_moe_nxt_lin_none_kernel(
                 )
             nc.scalar.copy(gate_sb[i][:], bank[:])
 
-        y = [keep.tile([P, S], F32, name=f"y{b}") for b in range(NB)]
+        y = [shared.tile([P, S], F32, name=f"y{b}", align_bytes=64, offset=4 * S * b) for b in range(NB)]
         slot_scales = {}
         slot_words = {}
 
-        def gather_scales(first, last, tag):
-            tile = keep.tile([P, (last - first) * C], U8, name=f"scales{first}", tag=tag, align_bytes=64)
-            nc.vector.tensor_copy(tile[:], xs[:].indirect(offs_sb[:, first * C // 16 : last * C // 16]))
+        def gather_scales(first, last, tile):
+            nc.vector.tensor_copy(tile, xs[:].indirect(offs_sb[:, first * C // 16 : last * C // 16]))
             for e in range(first, last):
                 slot_scales[e] = tile[:, (e - first) * C : (e - first + 1) * C]
 
-        def gather_words(first, last):
-            tile = keep.tile([P, (last - first) * C], U32, name=f"words{first}", align_bytes=64)
-            nc.vector.tensor_copy(tile[:], xw[:].bitcast(U32).indirect(offs_sb[:, first * C // 16 : last * C // 16]))
+        def gather_words(first, last, tile):
+            nc.vector.tensor_copy(tile, xw[:].bitcast(U32).indirect(offs_sb[:, first * C // 16 : last * C // 16]))
             for e in range(first, last):
                 slot_words[e] = tile[:, (e - first) * C : (e - first + 1) * C]
 
@@ -133,43 +134,42 @@ def tile_moe_nxt_lin_none_kernel(
                 )
             evict(y[b][:, first * C : last * C], banks[k][:, 0 : (last - first) * C])
 
-        wp_bf = keep.tile([P, 4 * M], BF16, name="wp_bf", align_bytes=64)
-        nc.gpsimd.tensor_copy(wp_bf[:].rearrange("p (f j) -> p f j", j=4), wp_raw[:].rearrange("p j f -> p f j"))
-        wp_codes = keep.tile([P, M], U32, name="wp_codes", align_bytes=64)
         wp_scales = keep.tile([P, M], U8, name="wp_scales", align_bytes=64)
 
-        gather_scales(0, 2 * GROUP, "first_scales")
-        gather_words(0, GROUP)
+        early_scales = keep.tile([P, 2 * GROUP * C], U8, name="early_scales", align_bytes=64)
+        early_words = [keep.tile([P, GROUP * C], U32, name=f"early_words{g}", align_bytes=64) for g in range(2)]
+        late_scales = shared.tile([P, GROUP * C], U8, name="late_scales", align_bytes=64, offset=late)
+        late_words = shared.tile([P, GROUP * C], U32, name="late_words", align_bytes=64, offset=late + GROUP * C)
+        gather_scales(0, 2 * GROUP, early_scales[:])
+        gather_words(0, GROUP, early_words[0][:])
         for b in range(NB):
             experts(0, GROUP, b, b)
-        gather_words(GROUP, 2 * GROUP)
+        gather_words(GROUP, 2 * GROUP, early_words[1][:])
         experts(GROUP, 2 * GROUP, 0, 4)
-        experts(GROUP, 2 * GROUP, 1, 5)
-        gather_scales(2 * GROUP, E, "rows_then_scales")
-        gather_words(2 * GROUP, E - 2)
-        gather_words(E - 2, E - 1)
-        gather_words(E - 1, E)
-        experts(GROUP, 2 * GROUP, 2, 6, nc.vector.tensor_copy)
-        experts(2 * GROUP, E - 2, 0, 7, nc.vector.tensor_copy)
-        nc.vector.quantize_mx(out=wp_codes[:].bitcast(FP8X4), scales=wp_scales[:], in_=wp_bf[:])
+        gather_scales(2 * GROUP, E, late_scales[:])
+        gather_words(2 * GROUP, E - 2, late_words[:, 0 : 2 * C])
+        gather_words(E - 2, E - 1, late_words[:, 2 * C : 3 * C])
+        gather_words(E - 1, E, late_words[:, 3 * C : 4 * C])
+        experts(GROUP, 2 * GROUP, 1, 6, nc.vector.tensor_copy)
+        experts(2 * GROUP, E - 2, 0, 7)
         experts(E - 2, E - 1, 0, 0)
         experts(E - 1, E, 0, 1)
         experts(2 * GROUP, E, 1, 2)
 
-        rounded = keep.tile([P, FUSED * N], BF16, name="rounded")
-        plain_rounded = keep.tile([P, (TILES - FUSED) * N], BF16, name="plain_rounded")
-        first_terms = [keep.tile([P, N], F32, name=f"first_terms{j}") for j in range(FUSED, TILES)]
+        rounded = keep.tile([P, TILES * N], BF16, name="rounded")
+        first_terms = [
+            shared.tile([P, N], F32, name=f"first_terms{j}", align_bytes=64, offset=4 * (S * NB + N * (j - FUSED)))
+            for j in range(FUSED, TILES)
+        ]
+        wp_codes = shared.tile([P, M], U32, name="wp_codes", align_bytes=64, offset=4 * S * NB)
         c_bf = {}
 
-        def fused(blocks, j0, j1, k, pair=None):
+        def fused(blocks, j0, j1, k):
             t0, t1 = j0 * P, j1 * P
             nb = len(blocks)
             for x, b in enumerate(blocks):
                 for i in range(2):
-                    if pair is None:
-                        term = keep.tile([P, t1 - t0], F32, name=f"term{b}_{j0}_{i}")[:]
-                    else:
-                        term = pair[i]
+                    term = keep.tile([P, t1 - t0], F32, name=f"term{b}_{j0}_{i}")[:]
                     nc.vector.tensor_tensor(
                         term, y[b][:].indirect(pos_sb[i][:, t0 // 16 : t1 // 16]), gate_sb[i][:, t0:t1], MULT
                     )
@@ -203,10 +203,7 @@ def tile_moe_nxt_lin_none_kernel(
             for j in range(j0, j1):
                 for u in range(2):
                     col = (2 * (j - j0) + u) * P
-                    if j < FUSED:
-                        pairs = rounded[:, j * N : (j + 1) * N].bitcast(F32)[:, u * P : (u + 1) * P]
-                    else:
-                        pairs = plain_rounded[:, (j - FUSED) * N : (j - FUSED + 1) * N].bitcast(F32)[:, u : 2 * P : 2]
+                    pairs = rounded[:, j * N : (j + 1) * N].bitcast(F32)[:, u * P : (u + 1) * P]
                     nc.tensor.transpose(banks[k][:, col : col + P], pairs, ident[:])
             c_bf[j0] = keep.tile([P, (j1 - j0) * N], BF16, name=f"c_bf{j0}", align_bytes=64)
             nc.scalar.copy(
@@ -232,49 +229,52 @@ def tile_moe_nxt_lin_none_kernel(
             evict(res[:], banks[k][:, 0:tw])
             nc.sync.dma_start(out[:, t0 : t0 + tw], res[:])
 
-        first_banks, second_banks = (7, 0), (2, 3)
+        def add_second(j, k):
+            for u in range(2):
+                nc.vector.scalar_tensor_tensor(
+                    rounded[:, j * N : (j + 1) * N].rearrange("p (u w e) -> p u w e", u=2, e=2)[:, u],
+                    banks[k][:].rearrange("p (w u e) -> p u w e", u=2, e=2)[:, u],
+                    gate_cols[:, 2 * j + 1 : 2 * j + 2],
+                    first_terms[j - FUSED][:].rearrange("p (w u e) -> p u w e", u=2, e=2)[:, u],
+                    MULT,
+                    ADD,
+                )
+
+        first_banks, second_banks = (7, 0), (2, 5)
         plain(0, 0, first_banks)
         plain(1, 0, first_banks)
-        fused([0], 0, FUSED, 6)
-        experts(GROUP, 2 * GROUP, 3, 3)
+        experts(GROUP, 2 * GROUP, 2, 5)
         experts(2 * GROUP, E, 2, 4)
+        fused([0], 0, FUSED, 6)
         plain(2, 0, first_banks)
-        experts(2 * GROUP, E, 3, 5)
+        experts(GROUP, 2 * GROUP, 3, 3)
+        experts(2 * GROUP, E, 3, 1)
         plain(3, 0, first_banks)
-        fused([1], 0, FUSED, 1)
+        fused([1], 0, FUSED, 4)
         plain(0, 1, second_banks)
-        for j in range(FUSED, TILES):
-            nc.scalar.activation(
-                first_terms[j - FUSED][:], banks[first_banks[j - FUSED]][:], COPY, scale=gate_cols[:, 2 * j : 2 * j + 1]
-            )
         plain(1, 1, second_banks)
-        fused([2, 3], 0, 2, 4)
+        fused([2], 0, FUSED, 3)
         plain(2, 1, second_banks)
+        fused([3], 0, 2, 1)
         plain(3, 1, second_banks)
         round_bank([0], 0, FUSED, 6)
-        round_bank([1], 0, FUSED, 1)
-        round_bank([2, 3], 0, 2, 4)
-        fused([2], 2, FUSED, 5)
-        for j in range(FUSED, TILES):
-            nc.vector.scalar_tensor_tensor(
-                plain_rounded[:, (j - FUSED) * N : (j - FUSED + 1) * N],
-                banks[second_banks[j - FUSED]][:],
-                gate_cols[:, 2 * j + 1 : 2 * j + 2],
-                first_terms[j - FUSED][:],
-                MULT,
-                ADD,
-            )
-        turn_back(0, 2, 6)
-        round_bank([2], 2, FUSED, 5)
-        turn_back(FUSED, TILES, 1)
-        last = first_terms[-1]
-        fused([3], 2, 3, 7, (last[:, 0:P], last[:, P : 2 * P]))
-        fused([3], 3, 4, 0, (last[:, 2 * P : 3 * P], last[:, 3 * P : 4 * P]))
-        round_bank([3], 2, 3, 7)
-        round_bank([3], 3, 4, 0)
-        project(0, 2, 2, nc.scalar.copy)
-        project(FUSED, TILES, 3, nc.scalar.copy)
-        turn_back(2, 3, 4)
-        turn_back(3, 4, 5)
-        project(2, 3, 6, nc.vector.tensor_copy)
-        project(3, 4, 1, nc.vector.tensor_copy)
+        fused([3], 2, FUSED, 6)
+        round_bank([1], 0, FUSED, 4)
+        round_bank([2], 0, FUSED, 3)
+        round_bank([3], 0, 2, 1)
+        wp_bf = shared.tile([P, 4 * M], BF16, name="wp_bf", align_bytes=64, offset=4 * S * 3)
+        nc.gpsimd.tensor_copy(wp_bf[:].rearrange("p (f j) -> p f j", j=4), wp_raw[:].rearrange("p j f -> p f j"))
+        nc.vector.tensor_scalar(first_terms[0][:], banks[7][:], gate_cols[:, 8:9], None, MULT)
+        nc.scalar.activation(first_terms[1][:], banks[0][:], COPY, scale=gate_cols[:, 10:11])
+        round_bank([3], 2, FUSED, 6)
+        add_second(4, 2)
+        add_second(5, 5)
+        nc.vector.quantize_mx(out=wp_codes[:].bitcast(FP8X4), scales=wp_scales[:], in_=wp_bf[:])
+        turn_back(0, 2, 4)
+        turn_back(2, 4, 3)
+        turn_back(4, 5, 6)
+        turn_back(5, 6, 4)
+        project(0, 2, 1, nc.scalar.copy)
+        project(2, 4, 7, nc.scalar.copy)
+        project(4, 5, 2, nc.scalar.copy)
+        project(5, 6, 5, nc.vector.tensor_copy)

@@ -24,7 +24,6 @@ ADD = mybir.AluOpType.add
 COPY = mybir.ActivationFunctionType.Copy
 
 GROUP = BANK // C
-SCALE_WINDOW = 1408
 TILES = T // P
 FUSED = 4
 BANKS = 8
@@ -42,58 +41,53 @@ def tile_moe_nxt_lin_none_kernel(
         offs_sb = keep.tile([P, S // 16], U16, name="offs_sb")
         pos_sb = [keep.tile([P, T // 16], U16, name=f"pos_sb{i}") for i in range(2)]
         xw = keep.tile([P, T], I32, name="xw", align_bytes=64)
-        xs = keep.tile([P, SCALE_WINDOW], U8, name="xs", align_bytes=64)
+        xs = keep.tile([P, T], U8, name="xs", align_bytes=64)
         ws = keep.tile([P, E * N], U8, name="ws", align_bytes=64)
         gate_sb = [keep.tile([P, FUSED * P], F32, name=f"gate_sb{i}") for i in range(2)]
         wp_raw = keep.tile([P, 4, M], F32, name="wp_raw")
         ident = keep.tile([P, P], F32, name="ident")
         late = 4 * (S * NB + N * (TILES - FUSED))
-        gate_rows = shared.tile([P, P], F32, name="gate_rows", align_bytes=64, offset=late + GROUP * C - 64)
+        gate_rows = shared.tile([P, P], F32, name="gate_rows", align_bytes=64, offset=late + 2 * GROUP * C - 64)
         gate_cols = keep.tile([P, 2 * TILES], F32, name="gate_cols")
         banks = [psum.tile([P, BANK], F32, name=f"bank{k}") for k in range(BANKS)]
 
-        nc.vector.memset(xs[:, T:].bitcast(I32), 0)
         nc.vector.memset(ws[:].bitcast(I32), 0)
         make_identity(nc, ident[:])
 
         ws_rows = w_scales.rearrange("e a (q r) n -> r q (e a) n", r=4)
         ww_rows = w_words.rearrange("e a p n -> p (e a) n")
+        weight_words = {}
+
+        def load_weights(first, last):
+            tile = keep.tile([P, (last - first) * 2 * N], U8, name=f"ww{first}", align_bytes=64)
+            nc.sync.dma_start(
+                tile[:].bitcast(I32).rearrange("p (e n) -> p e n", e=last - first),
+                ww_rows[:, first:last, :].bitcast(I32),
+            )
+            for e in range(first, last):
+                for b in range(NB):
+                    col = (e - first) * 2 * N + 2 * P * b
+                    weight_words[e, b] = tile[:, col : col + 2 * P]
 
         nc.sync.dma_start(offs_sb[:], offs)
         for q in range(4):
             queue = nc.sync if q < 2 else nc.scalar
             queue.dma_start(
-                xs[32 * q : 32 * (q + 1), 0:T].bitcast(I32),
+                xs[32 * q : 32 * (q + 1), :].bitcast(I32),
                 x_scales[0, 4 * q : 4 * q + 4, :].bitcast(I32).partition_broadcast(8),
             )
         nc.sync.dma_start(xw[:], x_words[0].rearrange("p t r -> p (t r)").bitcast(I32))
         nc.sync.dma_start(gate_rows[:], gate.rearrange("i n (j t) -> (n j) i t", t=P)[0 : P // 2])
+        load_weights(0, 2)
         for r in range(4):
             nc.sync.dma_start(
                 ws[r:P:32, :].bitcast(I32).rearrange("q (e n) -> q e n", e=E), ws_rows[r].bitcast(I32)
             )
         nc.sync.dma_start(pos_sb[0][:], pos1)
         nc.sync.dma_start(pos_sb[1][:], pos2)
-        weight_words = {}
-
-        def load_weights(g, b0, b1):
-            width = 2 * P * (b1 - b0)
-            tile = keep.tile([P, GROUP * width], U8, name=f"ww{g}_{b0}", align_bytes=64)
-            nc.sync.dma_start(
-                tile[:].bitcast(I32).rearrange("p (e n) -> p e n", e=GROUP),
-                ww_rows[:, g * GROUP : (g + 1) * GROUP, 2 * P * b0 : 2 * P * b1].bitcast(I32),
-            )
-            for u in range(GROUP):
-                for b in range(b0, b1):
-                    col = u * width + 2 * P * (b - b0)
-                    weight_words[g * GROUP + u, b] = tile[:, col : col + 2 * P]
-
-        load_weights(0, 0, 2)
-        load_weights(0, 2, NB)
-        load_weights(1, 0, 2)
-        load_weights(2, 0, 2)
-        load_weights(1, 2, NB)
-        load_weights(2, 2, NB)
+        load_weights(2, GROUP)
+        load_weights(GROUP, 2 * GROUP)
+        load_weights(2 * GROUP, E)
         nc.sync.dma_start(wp_raw[:], wp.rearrange("(p j) f -> p j f", j=4))
 
         nc.tensor.transpose(banks[7][:, 0:P], gate_rows[:], ident[:])
@@ -121,40 +115,48 @@ def tile_moe_nxt_lin_none_kernel(
             for e in range(first, last):
                 slot_words[e] = tile[:, (e - first) * C : (e - first + 1) * C]
 
-        def experts(first, last, b, k, evict=nc.scalar.copy):
-            for e in range(first, last):
-                nc.tensor.matmul_mx(
-                    out=banks[k][:, (e - first) * C : (e - first + 1) * C],
-                    lhsT=weight_words[e, b].bitcast(FP4X4),
-                    lhsT_scale=ws[:, e * N + b * P : e * N + (b + 1) * P],
-                    rhs=slot_words[e].bitcast(FP8X4),
-                    rhs_scale=slot_scales[e],
-                    start=True,
-                    stop=True,
-                )
-            evict(y[b][:, first * C : last * C], banks[k][:, 0 : (last - first) * C])
+        def experts(first, last, blocks, k, evict=nc.scalar.copy):
+            width = (last - first) * C
+            for x, b in enumerate(blocks):
+                for e in range(first, last):
+                    col = x * width + (e - first) * C
+                    nc.tensor.matmul_mx(
+                        out=banks[k][:, col : col + C],
+                        lhsT=weight_words[e, b].bitcast(FP4X4),
+                        lhsT_scale=ws[:, e * N + b * P : e * N + (b + 1) * P],
+                        rhs=slot_words[e].bitcast(FP8X4),
+                        rhs_scale=slot_scales[e],
+                        start=True,
+                        stop=True,
+                    )
+            for x, b in enumerate(blocks):
+                evict(y[b][:, first * C : last * C], banks[k][:, x * width : (x + 1) * width])
 
         wp_scales = keep.tile([P, M], U8, name="wp_scales", align_bytes=64)
-
-        early_scales = keep.tile([P, 2 * GROUP * C], U8, name="early_scales", align_bytes=64)
+        early_scales = keep.tile([P, GROUP * C], U8, name="early_scales", align_bytes=64)
         early_words = [keep.tile([P, GROUP * C], U32, name=f"early_words{g}", align_bytes=64) for g in range(2)]
-        late_scales = shared.tile([P, GROUP * C], U8, name="late_scales", align_bytes=64, offset=late)
-        late_words = shared.tile([P, GROUP * C], U32, name="late_words", align_bytes=64, offset=late + GROUP * C)
-        gather_scales(0, 2 * GROUP, early_scales[:])
+        late_scales = shared.tile([P, 2 * GROUP * C], U8, name="late_scales", align_bytes=64, offset=late)
+        late_words = shared.tile([P, GROUP * C], U32, name="late_words", align_bytes=64, offset=late + 2 * GROUP * C)
+        gather_scales(0, GROUP, early_scales[:])
         gather_words(0, GROUP, early_words[0][:])
         for b in range(NB):
-            experts(0, GROUP, b, b)
+            experts(0, 2, [b], b)
+        experts(2, GROUP, [0, 1], 4)
+        experts(2, GROUP, [2, 3], 5)
         gather_words(GROUP, 2 * GROUP, early_words[1][:])
-        experts(GROUP, 2 * GROUP, 0, 4)
-        gather_scales(2 * GROUP, E, late_scales[:])
+        gather_scales(GROUP, 2 * GROUP, late_scales[:, 0 : GROUP * C])
+        experts(GROUP, 2 * GROUP, [0], 6)
+        experts(GROUP, 2 * GROUP, [1], 7)
+        gather_scales(2 * GROUP, E, late_scales[:, GROUP * C :])
         gather_words(2 * GROUP, E - 2, late_words[:, 0 : 2 * C])
         gather_words(E - 2, E - 1, late_words[:, 2 * C : 3 * C])
         gather_words(E - 1, E, late_words[:, 3 * C : 4 * C])
-        experts(GROUP, 2 * GROUP, 1, 6, nc.vector.tensor_copy)
-        experts(2 * GROUP, E - 2, 0, 7)
-        experts(E - 2, E - 1, 0, 0)
-        experts(E - 1, E, 0, 1)
-        experts(2 * GROUP, E, 1, 2)
+        experts(GROUP, 2 * GROUP, [2], 0, nc.vector.tensor_copy)
+        experts(GROUP, 2 * GROUP, [3], 1, nc.vector.tensor_copy)
+        experts(2 * GROUP, E - 2, [0], 2)
+        experts(E - 2, E - 1, [0], 3)
+        experts(E - 1, E, [0], 4)
+        experts(2 * GROUP, E, [1], 5)
 
         rounded = keep.tile([P, TILES * N], BF16, name="rounded")
         first_terms = [
@@ -162,7 +164,6 @@ def tile_moe_nxt_lin_none_kernel(
             for j in range(FUSED, TILES)
         ]
         wp_codes = shared.tile([P, M], U32, name="wp_codes", align_bytes=64, offset=4 * S * NB)
-        c_bf = {}
 
         def fused(blocks, j0, j1, k):
             t0, t1 = j0 * P, j1 * P
@@ -177,7 +178,7 @@ def tile_moe_nxt_lin_none_kernel(
                         col = ((j - j0) * nb + x) * P
                         nc.tensor.matmul(
                             banks[k][:, col : col + P],
-                            lhsT=term[:, j * P - t0 : (j + 1) * P - t0],
+                            lhsT=term[:, (j - j0) * P : (j - j0 + 1) * P],
                             rhs=ident[:],
                             is_transpose=True,
                             start=(x == 0 and i == 0 and j == j0),
@@ -192,39 +193,40 @@ def tile_moe_nxt_lin_none_kernel(
                 banks[k][:, 0 : (j1 - j0) * nb * P].rearrange("p (j w u e) -> p j u w e", u=2, w=nb * P // 4, e=2),
             )
 
-        def plain(b, i, k0):
+        def plain(b, i, ks):
             term = keep.tile([P, T - FUSED * P], F32, name=f"plain{b}_{i}")
             nc.scalar.activation(term[:], y[b][:].indirect(pos_sb[i][:, FUSED * P // 16 :]), COPY)
             for j in range(TILES - FUSED):
-                nc.tensor.transpose(banks[k0[j]][:, b * P : (b + 1) * P], term[:, j * P : (j + 1) * P], ident[:])
+                nc.tensor.transpose(banks[ks[j]][:, b * P : (b + 1) * P], term[:, j * P : (j + 1) * P], ident[:])
 
-        def turn_back(j0, j1, k):
+        def turn_back(j0, j1, k, dest, evict=nc.scalar.copy):
             width = (j1 - j0) * 2 * P
             for j in range(j0, j1):
                 for u in range(2):
                     col = (2 * (j - j0) + u) * P
                     pairs = rounded[:, j * N : (j + 1) * N].bitcast(F32)[:, u * P : (u + 1) * P]
                     nc.tensor.transpose(banks[k][:, col : col + P], pairs, ident[:])
-            c_bf[j0] = keep.tile([P, (j1 - j0) * N], BF16, name=f"c_bf{j0}", align_bytes=64)
-            nc.scalar.copy(
-                c_bf[j0][:].bitcast(F32).rearrange("p (j t u) -> p j t u", t=P, u=2),
+            evict(
+                dest.bitcast(F32).rearrange("p (j t u) -> p j t u", t=P, u=2),
                 banks[k][:, 0:width].rearrange("p (j u t) -> p j t u", t=P, u=2),
             )
 
-        def project(j0, j1, k, evict):
+        def project(j0, j1, c_bf, k, evict):
             t0, tw = j0 * P, (j1 - j0) * P
             c_codes = keep.tile([P, tw], U32, name=f"c_codes{j0}", align_bytes=64)
             c_scales = keep.tile([P, tw], U8, name=f"c_scales{j0}", align_bytes=64)
-            nc.vector.quantize_mx(out=c_codes[:].bitcast(FP8X4), scales=c_scales[:], in_=c_bf[j0][:])
-            nc.tensor.matmul_mx(
-                out=banks[k][:, 0:tw],
-                lhsT=wp_codes[:].bitcast(FP8X4),
-                lhsT_scale=wp_scales[:],
-                rhs=c_codes[:].bitcast(FP8X4),
-                rhs_scale=c_scales[:],
-                start=True,
-                stop=True,
-            )
+            nc.vector.quantize_mx(out=c_codes[:].bitcast(FP8X4), scales=c_scales[:], in_=c_bf[:])
+            for c0 in range(0, tw, 2 * P):
+                c1 = min(c0 + 2 * P, tw)
+                nc.tensor.matmul_mx(
+                    out=banks[k][:, c0:c1],
+                    lhsT=wp_codes[:].bitcast(FP8X4),
+                    lhsT_scale=wp_scales[:],
+                    rhs=c_codes[:, c0:c1].bitcast(FP8X4),
+                    rhs_scale=c_scales[:, c0:c1],
+                    start=True,
+                    stop=True,
+                )
             res = keep.tile([P, tw], F32, name=f"res{j0}")
             evict(res[:], banks[k][:, 0:tw])
             nc.sync.dma_start(out[:, t0 : t0 + tw], res[:])
@@ -240,41 +242,49 @@ def tile_moe_nxt_lin_none_kernel(
                     ADD,
                 )
 
-        first_banks, second_banks = (7, 0), (2, 5)
+        def first_term(j, k):
+            nc.scalar.activation(first_terms[j - FUSED][:], banks[k][:], COPY, scale=gate_cols[:, 2 * j : 2 * j + 1])
+
+        first_banks, second_banks = (2, 3), (4, 5)
         plain(0, 0, first_banks)
         plain(1, 0, first_banks)
-        experts(GROUP, 2 * GROUP, 2, 5)
-        experts(2 * GROUP, E, 2, 4)
-        fused([0], 0, FUSED, 6)
+        experts(2 * GROUP, E, [2], 6)
+        fused([0], 0, FUSED, 0)
         plain(2, 0, first_banks)
-        experts(GROUP, 2 * GROUP, 3, 3)
-        experts(2 * GROUP, E, 3, 1)
+        experts(2 * GROUP, E, [3], 7)
         plain(3, 0, first_banks)
-        fused([1], 0, FUSED, 4)
+        fused([1], 0, FUSED, 1)
         plain(0, 1, second_banks)
         plain(1, 1, second_banks)
-        fused([2], 0, FUSED, 3)
+        fused([2, 3], 0, 2, 6)
         plain(2, 1, second_banks)
-        fused([3], 0, 2, 1)
         plain(3, 1, second_banks)
-        round_bank([0], 0, FUSED, 6)
-        fused([3], 2, FUSED, 6)
-        round_bank([1], 0, FUSED, 4)
-        round_bank([2], 0, FUSED, 3)
-        round_bank([3], 0, 2, 1)
+        fused([2], 2, FUSED, 7)
+        round_bank([0], 0, FUSED, 0)
+        fused([3], 2, 3, 0)
+        round_bank([1], 0, FUSED, 1)
+        fused([3], 3, FUSED, 1)
+        round_bank([2, 3], 0, 2, 6)
+        first_term(4, 2)
+        round_bank([2], 2, FUSED, 7)
         wp_bf = shared.tile([P, 4 * M], BF16, name="wp_bf", align_bytes=64, offset=4 * S * 3)
         nc.gpsimd.tensor_copy(wp_bf[:].rearrange("p (f j) -> p f j", j=4), wp_raw[:].rearrange("p j f -> p f j"))
-        nc.vector.tensor_scalar(first_terms[0][:], banks[7][:], gate_cols[:, 8:9], None, MULT)
-        nc.scalar.activation(first_terms[1][:], banks[0][:], COPY, scale=gate_cols[:, 10:11])
-        round_bank([3], 2, FUSED, 6)
-        add_second(4, 2)
+        first_term(5, 3)
+        c01 = keep.tile([P, 2 * N], BF16, name="c01", align_bytes=64)
+        c23 = keep.tile([P, 2 * N], BF16, name="c23", align_bytes=64)
+        c4 = keep.tile([P, N], BF16, name="c4", align_bytes=64)
+        c5 = keep.tile([P, N], BF16, name="c5", align_bytes=64)
+        round_bank([3], 2, 3, 0)
+        turn_back(0, 2, 6, c01[:])
+        round_bank([3], 3, FUSED, 1)
+        add_second(4, 4)
         add_second(5, 5)
         nc.vector.quantize_mx(out=wp_codes[:].bitcast(FP8X4), scales=wp_scales[:], in_=wp_bf[:])
-        turn_back(0, 2, 4)
-        turn_back(2, 4, 3)
-        turn_back(4, 5, 6)
-        turn_back(5, 6, 4)
-        project(0, 2, 1, nc.scalar.copy)
-        project(2, 4, 7, nc.scalar.copy)
-        project(4, 5, 2, nc.scalar.copy)
-        project(5, 6, 5, nc.vector.tensor_copy)
+        turn_back(2, 3, 7, c23[:, 0:N])
+        turn_back(4, 5, 2, c4[:])
+        turn_back(3, 4, 0, c23[:, N:])
+        turn_back(5, 6, 3, c5[:])
+        project(0, 2, c01, 4, nc.scalar.copy)
+        project(2, 4, c23, 1, nc.scalar.copy)
+        project(4, 5, c4, 5, nc.scalar.copy)
+        project(5, 6, c5, 6, nc.vector.tensor_copy)

@@ -146,17 +146,15 @@ def tile_moe_nxt_lin_none_kernel(
         gather_words(GROUP, 2 * GROUP, early_words[1][:])
         gather_scales(GROUP, 2 * GROUP, late_scales[:, 0 : GROUP * C])
         experts(GROUP, 2 * GROUP, [0], 6)
-        experts(GROUP, 2 * GROUP, [1], 7)
         gather_scales(2 * GROUP, E, late_scales[:, GROUP * C :])
         gather_words(2 * GROUP, E - 2, late_words[:, 0 : 2 * C])
         gather_words(E - 2, E - 1, late_words[:, 2 * C : 3 * C])
         gather_words(E - 1, E, late_words[:, 3 * C : 4 * C])
-        experts(GROUP, 2 * GROUP, [2], 0, nc.vector.tensor_copy)
-        experts(GROUP, 2 * GROUP, [3], 1, nc.vector.tensor_copy)
-        experts(2 * GROUP, E - 2, [0], 2)
-        experts(E - 2, E - 1, [0], 3)
-        experts(E - 1, E, [0], 4)
-        experts(2 * GROUP, E, [1], 5)
+        experts(GROUP, 2 * GROUP, [1], 7, nc.vector.tensor_copy)
+        experts(2 * GROUP, E - 2, [0], 0)
+        experts(E - 2, E - 1, [0], 1)
+        experts(E - 1, E, [0], 2)
+        experts(2 * GROUP, E, [1], 3)
 
         rounded = keep.tile([P, TILES * N], BF16, name="rounded")
         first_terms = [
@@ -242,49 +240,55 @@ def tile_moe_nxt_lin_none_kernel(
                     ADD,
                 )
 
-        def first_term(j, k):
-            nc.scalar.activation(first_terms[j - FUSED][:], banks[k][:], COPY, scale=gate_cols[:, 2 * j : 2 * j + 1])
+        def first_term(j, k, on_vector=False):
+            scale = gate_cols[:, 2 * j : 2 * j + 1]
+            if on_vector:
+                nc.vector.tensor_scalar(first_terms[j - FUSED][:], banks[k][:], scale, None, MULT)
+            else:
+                nc.scalar.activation(first_terms[j - FUSED][:], banks[k][:], COPY, scale=scale)
 
-        first_banks, second_banks = (2, 3), (4, 5)
+        first_banks, second_banks = (4, 5), (2, 3)
         plain(0, 0, first_banks)
         plain(1, 0, first_banks)
-        experts(2 * GROUP, E, [2], 6)
-        fused([0], 0, FUSED, 0)
+        experts(GROUP, 2 * GROUP, [2], 0)
+        experts(2 * GROUP, E, [2], 1)
+        fused([0], 0, FUSED, 6)
         plain(2, 0, first_banks)
-        experts(2 * GROUP, E, [3], 7)
+        experts(GROUP, 2 * GROUP, [3], 2)
+        experts(2 * GROUP, E, [3], 3)
         plain(3, 0, first_banks)
-        fused([1], 0, FUSED, 1)
+        fused([1], 0, FUSED, 7)
         plain(0, 1, second_banks)
         plain(1, 1, second_banks)
-        fused([2, 3], 0, 2, 6)
+        fused([2, 3], 0, 2, 0)
         plain(2, 1, second_banks)
         plain(3, 1, second_banks)
-        fused([2], 2, FUSED, 7)
-        round_bank([0], 0, FUSED, 0)
-        fused([3], 2, 3, 0)
-        round_bank([1], 0, FUSED, 1)
-        fused([3], 3, FUSED, 1)
-        round_bank([2, 3], 0, 2, 6)
-        first_term(4, 2)
-        round_bank([2], 2, FUSED, 7)
+        fused([2], 2, FUSED, 1)
+        round_bank([0], 0, FUSED, 6)
+        fused([3], 2, 3, 6)
+        round_bank([1], 0, FUSED, 7)
+        fused([3], 3, FUSED, 7)
+        round_bank([2, 3], 0, 2, 0)
+        first_term(4, 4)
+        round_bank([2], 2, FUSED, 1)
         wp_bf = shared.tile([P, 4 * M], BF16, name="wp_bf", align_bytes=64, offset=4 * S * 3)
         nc.gpsimd.tensor_copy(wp_bf[:].rearrange("p (f j) -> p f j", j=4), wp_raw[:].rearrange("p j f -> p f j"))
-        first_term(5, 3)
+        first_term(5, 5, True)
         c01 = keep.tile([P, 2 * N], BF16, name="c01", align_bytes=64)
         c23 = keep.tile([P, 2 * N], BF16, name="c23", align_bytes=64)
         c4 = keep.tile([P, N], BF16, name="c4", align_bytes=64)
         c5 = keep.tile([P, N], BF16, name="c5", align_bytes=64)
-        round_bank([3], 2, 3, 0)
-        turn_back(0, 2, 6, c01[:])
-        round_bank([3], 3, FUSED, 1)
-        add_second(4, 4)
-        add_second(5, 5)
+        round_bank([3], 2, 3, 6)
+        turn_back(0, 2, 0, c01[:])
+        round_bank([3], 3, FUSED, 7)
+        add_second(4, 2)
+        add_second(5, 3)
         nc.vector.quantize_mx(out=wp_codes[:].bitcast(FP8X4), scales=wp_scales[:], in_=wp_bf[:])
-        turn_back(2, 3, 7, c23[:, 0:N])
-        turn_back(4, 5, 2, c4[:])
-        turn_back(3, 4, 0, c23[:, N:])
-        turn_back(5, 6, 3, c5[:])
-        project(0, 2, c01, 4, nc.scalar.copy)
-        project(2, 4, c23, 1, nc.scalar.copy)
-        project(4, 5, c4, 5, nc.scalar.copy)
-        project(5, 6, c5, 6, nc.vector.tensor_copy)
+        turn_back(2, 3, 1, c23[:, 0:N])
+        turn_back(4, 5, 4, c4[:])
+        turn_back(3, 4, 6, c23[:, N:])
+        turn_back(5, 6, 5, c5[:])
+        project(0, 2, c01, 2, nc.scalar.copy)
+        project(2, 4, c23, 7, nc.scalar.copy)
+        project(4, 5, c4, 3, nc.scalar.copy)
+        project(5, 6, c5, 0, nc.vector.tensor_copy)

@@ -58,16 +58,17 @@ def tile_moe_nxt_lin_none_kernel(
         ww_rows = w_words.rearrange("e a p n -> p (e a) n")
         weight_words = {}
 
-        def load_weights(first, last):
-            tile = keep.tile([P, (last - first) * 2 * N], U8, name=f"ww{first}", align_bytes=64)
+        def load_weights(g, b0, b1):
+            width = 2 * P * (b1 - b0)
+            tile = keep.tile([P, GROUP * width], U8, name=f"ww{g}_{b0}", align_bytes=64)
             nc.sync.dma_start(
-                tile[:].bitcast(I32).rearrange("p (e n) -> p e n", e=last - first),
-                ww_rows[:, first:last, :].bitcast(I32),
+                tile[:].bitcast(I32).rearrange("p (e n) -> p e n", e=GROUP),
+                ww_rows[:, g * GROUP : (g + 1) * GROUP, 2 * P * b0 : 2 * P * b1].bitcast(I32),
             )
-            for e in range(first, last):
-                for b in range(NB):
-                    col = (e - first) * 2 * N + 2 * P * b
-                    weight_words[e, b] = tile[:, col : col + 2 * P]
+            for u in range(GROUP):
+                for b in range(b0, b1):
+                    col = u * width + 2 * P * (b - b0)
+                    weight_words[g * GROUP + u, b] = tile[:, col : col + 2 * P]
 
         nc.sync.dma_start(offs_sb[:], offs)
         for q in range(4):
@@ -78,16 +79,18 @@ def tile_moe_nxt_lin_none_kernel(
             )
         nc.sync.dma_start(xw[:], x_words[0].rearrange("p t r -> p (t r)").bitcast(I32))
         nc.sync.dma_start(gate_rows[:], gate.rearrange("i n (j t) -> (n j) i t", t=P)[0 : P // 2])
-        load_weights(0, 2)
         for r in range(4):
             nc.sync.dma_start(
                 ws[r:P:32, :].bitcast(I32).rearrange("q (e n) -> q e n", e=E), ws_rows[r].bitcast(I32)
             )
         nc.sync.dma_start(pos_sb[0][:], pos1)
         nc.sync.dma_start(pos_sb[1][:], pos2)
-        load_weights(2, GROUP)
-        load_weights(GROUP, 2 * GROUP)
-        load_weights(2 * GROUP, E)
+        load_weights(0, 0, 2)
+        load_weights(0, 2, NB)
+        load_weights(1, 0, 2)
+        load_weights(2, 0, 2)
+        load_weights(1, 2, NB)
+        load_weights(2, 2, NB)
         nc.sync.dma_start(wp_raw[:], wp.rearrange("(p j) f -> p j f", j=4))
 
         nc.tensor.transpose(banks[7][:, 0:P], gate_rows[:], ident[:])
@@ -140,9 +143,7 @@ def tile_moe_nxt_lin_none_kernel(
         gather_scales(0, GROUP, early_scales[:])
         gather_words(0, GROUP, early_words[0][:])
         for b in range(NB):
-            experts(0, 2, [b], b)
-        experts(2, GROUP, [0, 1], 4)
-        experts(2, GROUP, [2, 3], 5)
+            experts(0, GROUP, [b], b)
         gather_words(GROUP, 2 * GROUP, early_words[1][:])
         gather_scales(GROUP, 2 * GROUP, late_scales[:, 0 : GROUP * C])
         experts(GROUP, 2 * GROUP, [0], 6)
@@ -273,7 +274,7 @@ def tile_moe_nxt_lin_none_kernel(
         round_bank([2], 2, FUSED, 1)
         wp_bf = shared.tile([P, 4 * M], BF16, name="wp_bf", align_bytes=64, offset=4 * S * 3)
         nc.gpsimd.tensor_copy(wp_bf[:].rearrange("p (f j) -> p f j", j=4), wp_raw[:].rearrange("p j f -> p f j"))
-        first_term(5, 5, True)
+        first_term(5, 5)
         c01 = keep.tile([P, 2 * N], BF16, name="c01", align_bytes=64)
         c23 = keep.tile([P, 2 * N], BF16, name="c23", align_bytes=64)
         c4 = keep.tile([P, N], BF16, name="c4", align_bytes=64)

@@ -21,11 +21,18 @@ FP8X4 = mybir.dt.float8_e4m3fn_x4
 FP4X4 = mybir.dt.float4_e2m1fn_x4
 MULT = mybir.AluOpType.mult
 ADD = mybir.AluOpType.add
+SUBTRACT = mybir.AluOpType.subtract
+MAX = mybir.AluOpType.max
+POW = mybir.AluOpType.pow
+IS_GE = mybir.AluOpType.is_ge
 COPY = mybir.ActivationFunctionType.Copy
+ABS = mybir.ActivationFunctionType.Abs
 
 GROUP = BANK // C
 TILES = T // P
-FUSED = 4
+SPLIT = 4
+RATIO_BOUND = 2.0**-30
+TINY = 2.0**-100
 BANKS = 8
 
 
@@ -43,10 +50,10 @@ def tile_moe_nxt_lin_none_kernel(
         xw = keep.tile([P, T], I32, name="xw", align_bytes=64)
         xs = keep.tile([P, T], U8, name="xs", align_bytes=64)
         ws = keep.tile([P, E * N], U8, name="ws", align_bytes=64)
-        gate_sb = [keep.tile([P, FUSED * P], F32, name=f"gate_sb{i}") for i in range(2)]
+        ratio_sb = shared.tile([P, T], F32, name="ratio_sb", align_bytes=64, offset=4 * S * NB + 16384)
         wp_raw = keep.tile([P, 4, M], F32, name="wp_raw")
         ident = keep.tile([P, P], F32, name="ident")
-        late = 4 * (S * NB + N * (TILES - FUSED))
+        late = 4 * S * NB
         gate_rows = shared.tile([P, P], F32, name="gate_rows", align_bytes=64, offset=late + 2 * GROUP * C - 64)
         gate_cols = keep.tile([P, 2 * TILES], F32, name="gate_cols")
         banks = [psum.tile([P, BANK], F32, name=f"bank{k}") for k in range(BANKS)]
@@ -93,16 +100,37 @@ def tile_moe_nxt_lin_none_kernel(
         load_weights(2, 2, NB)
         nc.sync.dma_start(wp_raw[:], wp.rearrange("(p j) f -> p j f", j=4))
 
-        nc.tensor.transpose(banks[7][:, 0:P], gate_rows[:], ident[:])
-        nc.scalar.copy(gate_cols[:], banks[7][:, 0 : 2 * TILES])
-        for i in range(2):
-            bank = banks[5 + i]
-            for j in range(FUSED):
-                col = 2 * j + i
-                nc.tensor.transpose(
-                    bank[:, j * P : (j + 1) * P], gate_cols[:, col : col + 1].to_broadcast([P, P]), ident[:]
-                )
-            nc.scalar.copy(gate_sb[i][:], bank[:])
+        nc.tensor.transpose(banks[2][:, 0:P], gate_rows[:], ident[:])
+        nc.scalar.copy(gate_cols[:], banks[2][:, 0 : 2 * TILES])
+        small = {
+            name: keep.tile([P, TILES], F32, name=name)[:]
+            for name in ("floor", "size", "step", "sign", "lack", "lift", "kept", "inverse", "signed", "minus_one")
+        }
+        codes_at = 4 * S * NB + 20480
+        second_tile = shared.tile([P, 16], F32, name="second", offset=codes_at + 4 * M - 32)
+        early_second = shared.tile([P, 1], F32, name="early_second", offset=late + 4096 + 8 * P * 11)
+        second = [early_second[:]]
+        second.extend(second_tile[:, 4 + j : 5 + j] for j in range(1, TILES))
+        ratio = keep.tile([P, TILES], F32, name="ratio")
+        nc.scalar.activation(small["floor"], banks[2][:, 0 : 2 * TILES : 2], ABS, scale=RATIO_BOUND)
+        nc.scalar.activation(small["size"], banks[2][:, 1 : 2 * TILES : 2], ABS)
+        nc.gpsimd.memset(small["minus_one"], -1.0)
+        nc.gpsimd.tensor_scalar(small["step"], gate_cols[:, 1::2], 0.0, 2.0, IS_GE, MULT)
+        nc.gpsimd.tensor_tensor(small["sign"], small["step"], small["minus_one"], ADD)
+        nc.gpsimd.tensor_tensor(small["signed"], gate_cols[:, 0::2], small["sign"], MULT)
+        nc.gpsimd.tensor_tensor(small["lack"], small["floor"], small["size"], SUBTRACT)
+        nc.gpsimd.tensor_scalar(small["lift"], small["lack"], TINY, 1.0, MAX, MULT)
+        nc.gpsimd.tensor_tensor(small["kept"], small["size"], small["lift"], ADD)
+        nc.gpsimd.tensor_tensor(small["inverse"], small["kept"], small["minus_one"], POW)
+        nc.gpsimd.tensor_tensor(ratio[:], small["signed"], small["inverse"], MULT)
+        nc.gpsimd.tensor_tensor(early_second[:], small["kept"][:, 0:1], small["sign"][:, 0:1], MULT)
+        nc.gpsimd.tensor_tensor(second_tile[:, 5:10], small["kept"][:, 1:], small["sign"][:, 1:], MULT)
+
+        def spread_ratio(j0, j1, k, evict):
+            for j in range(j0, j1):
+                col = (j - j0) * P
+                nc.tensor.transpose(banks[k][:, col : col + P], ratio[:, j : j + 1].to_broadcast([P, P]), ident[:])
+            evict(ratio_sb[:, j0 * P : j1 * P], banks[k][:, 0 : (j1 - j0) * P])
 
         y = [shared.tile([P, S], F32, name=f"y{b}", align_bytes=64, offset=4 * S * b) for b in range(NB)]
         slot_scales = {}
@@ -142,68 +170,68 @@ def tile_moe_nxt_lin_none_kernel(
         late_words = shared.tile([P, GROUP * C], U32, name="late_words", align_bytes=64, offset=late + 2 * GROUP * C)
         gather_scales(0, GROUP, early_scales[:])
         gather_words(0, GROUP, early_words[0][:])
-        for b in range(NB):
-            experts(0, GROUP, [b], b)
+        for b, k in enumerate((5, 1, 6, 7)):
+            experts(0, GROUP, [b], k)
         gather_words(GROUP, 2 * GROUP, early_words[1][:])
         gather_scales(GROUP, 2 * GROUP, late_scales[:, 0 : GROUP * C])
-        experts(GROUP, 2 * GROUP, [0], 6)
+        experts(GROUP, 2 * GROUP, [0], 4)
         gather_scales(2 * GROUP, E, late_scales[:, GROUP * C :])
         gather_words(2 * GROUP, E - 2, late_words[:, 0 : 2 * C])
         gather_words(E - 2, E - 1, late_words[:, 2 * C : 3 * C])
         gather_words(E - 1, E, late_words[:, 3 * C : 4 * C])
-        experts(GROUP, 2 * GROUP, [1], 7, nc.vector.tensor_copy)
-        experts(2 * GROUP, E - 2, [0], 0)
-        experts(E - 2, E - 1, [0], 1)
-        experts(E - 1, E, [0], 2)
-        experts(2 * GROUP, E, [1], 3)
+        spread_ratio(0, GROUP, 5, nc.scalar.copy)
+        spread_ratio(GROUP, TILES, 1, nc.vector.tensor_copy)
+        experts(GROUP, 2 * GROUP, [1], 3, nc.vector.tensor_copy)
+        experts(2 * GROUP, E - 2, [0], 6)
+        experts(E - 2, E - 1, [0], 7)
+        experts(E - 1, E, [0], 4)
+        experts(2 * GROUP, E, [1], 5)
 
-        rounded = keep.tile([P, TILES * N], BF16, name="rounded")
-        first_terms = [
-            shared.tile([P, N], F32, name=f"first_terms{j}", align_bytes=64, offset=4 * (S * NB + N * (j - FUSED)))
-            for j in range(FUSED, TILES)
-        ]
-        wp_codes = shared.tile([P, M], U32, name="wp_codes", align_bytes=64, offset=4 * S * NB)
+        rounded = [keep.tile([P, N], BF16, name=f"rounded{j}")[:] for j in range(3)]
+        rounded.extend(
+            shared.tile([P, N], BF16, name=f"rounded{j}", offset=4 * S * 3 + 2 * N * j)[:] for j in range(3, TILES)
+        )
+        wp_codes = shared.tile([P, M], U32, name="wp_codes", align_bytes=64, offset=codes_at)
+        turns = [0] * TILES
 
-        def fused(blocks, j0, j1, k):
+        def gather_results(engine, i, b, j0, j1, slot=None):
             t0, t1 = j0 * P, j1 * P
-            nb = len(blocks)
-            for x, b in enumerate(blocks):
-                for i in range(2):
-                    term = keep.tile([P, t1 - t0], F32, name=f"term{b}_{j0}_{i}")[:]
-                    nc.vector.tensor_tensor(
-                        term, y[b][:].indirect(pos_sb[i][:, t0 // 16 : t1 // 16]), gate_sb[i][:, t0:t1], MULT
-                    )
-                    for j in range(j0, j1):
-                        col = ((j - j0) * nb + x) * P
-                        nc.tensor.matmul(
-                            banks[k][:, col : col + P],
-                            lhsT=term[:, (j - j0) * P : (j - j0 + 1) * P],
-                            rhs=ident[:],
-                            is_transpose=True,
-                            start=(x == 0 and i == 0 and j == j0),
-                            stop=(x == nb - 1 and i == 1 and j == j1 - 1),
-                        )
+            if slot is None:
+                term = keep.tile([P, t1 - t0], F32, name=f"term{b}_{j0}_{i}")[:]
+            else:
+                term = shared.tile([P, t1 - t0], F32, name=f"term{b}_{j0}_{i}", offset=late + 4096 + 8 * P * slot)[:]
+            window = y[b][:].indirect(pos_sb[i][:, t0 // 16 : t1 // 16])
+            if i == 0:
+                nc.vector.tensor_tensor(term, window, ratio_sb[:, t0:t1], MULT)
+            elif engine == "vector":
+                nc.vector.tensor_copy(term, window)
+            else:
+                nc.scalar.activation(term, window, COPY)
+            for j in range(j0, j1):
+                nc.tensor.matmul(
+                    banks[j][:, b * P : (b + 1) * P],
+                    lhsT=term[:, (j - j0) * P : (j - j0 + 1) * P],
+                    rhs=ident[:],
+                    is_transpose=True,
+                    start=(turns[j] == 0),
+                    stop=(turns[j] == 2 * NB - 1),
+                )
+                turns[j] = turns[j] + 1
 
-        def round_bank(blocks, j0, j1, k):
-            nb = len(blocks)
-            words = slice(blocks[0] * P // 4, (blocks[-1] + 1) * P // 4)
-            nc.scalar.copy(
-                rounded[:, j0 * N : j1 * N].rearrange("p (j u w e) -> p j u w e", u=2, w=P, e=2)[:, :, :, words, :],
-                banks[k][:, 0 : (j1 - j0) * nb * P].rearrange("p (j w u e) -> p j u w e", u=2, w=nb * P // 4, e=2),
-            )
-
-        def plain(b, i, ks):
-            term = keep.tile([P, T - FUSED * P], F32, name=f"plain{b}_{i}")
-            nc.scalar.activation(term[:], y[b][:].indirect(pos_sb[i][:, FUSED * P // 16 :]), COPY)
-            for j in range(TILES - FUSED):
-                nc.tensor.transpose(banks[ks[j]][:, b * P : (b + 1) * P], term[:, j * P : (j + 1) * P], ident[:])
+        def round_tile(j, engine="scalar"):
+            dest = rounded[j].rearrange("p (u w e) -> p u w e", u=2, e=2)
+            sums = banks[j][:].rearrange("p (w u e) -> p u w e", u=2, e=2)
+            if engine == "vector":
+                nc.vector.tensor_scalar(dest, sums, second[j], None, MULT)
+            else:
+                nc.scalar.activation(dest, sums, COPY, scale=second[j])
 
         def turn_back(j0, j1, k, dest, evict=nc.scalar.copy):
             width = (j1 - j0) * 2 * P
             for j in range(j0, j1):
                 for u in range(2):
                     col = (2 * (j - j0) + u) * P
-                    pairs = rounded[:, j * N : (j + 1) * N].bitcast(F32)[:, u * P : (u + 1) * P]
+                    pairs = rounded[j].bitcast(F32)[:, u * P : (u + 1) * P]
                     nc.tensor.transpose(banks[k][:, col : col + P], pairs, ident[:])
             evict(
                 dest.bitcast(F32).rearrange("p (j t u) -> p j t u", t=P, u=2),
@@ -212,7 +240,7 @@ def tile_moe_nxt_lin_none_kernel(
 
         def project(j0, j1, c_bf, k, evict):
             t0, tw = j0 * P, (j1 - j0) * P
-            c_codes = keep.tile([P, tw], U32, name=f"c_codes{j0}", align_bytes=64)
+            c_codes = shared.tile([P, tw], U32, name=f"c_codes{j0}", align_bytes=64, offset=codes_at + 4 * (M + t0))
             c_scales = keep.tile([P, tw], U8, name=f"c_scales{j0}", align_bytes=64)
             nc.vector.quantize_mx(out=c_codes[:].bitcast(FP8X4), scales=c_scales[:], in_=c_bf[:])
             for c0 in range(0, tw, 2 * P):
@@ -230,66 +258,43 @@ def tile_moe_nxt_lin_none_kernel(
             evict(res[:], banks[k][:, 0:tw])
             nc.sync.dma_start(out[:, t0 : t0 + tw], res[:])
 
-        def add_second(j, k):
-            for u in range(2):
-                nc.vector.scalar_tensor_tensor(
-                    rounded[:, j * N : (j + 1) * N].rearrange("p (u w e) -> p u w e", u=2, e=2)[:, u],
-                    banks[k][:].rearrange("p (w u e) -> p u w e", u=2, e=2)[:, u],
-                    gate_cols[:, 2 * j + 1 : 2 * j + 2],
-                    first_terms[j - FUSED][:].rearrange("p (w u e) -> p u w e", u=2, e=2)[:, u],
-                    MULT,
-                    ADD,
-                )
-
-        def first_term(j, k, on_vector=False):
-            scale = gate_cols[:, 2 * j : 2 * j + 1]
-            if on_vector:
-                nc.vector.tensor_scalar(first_terms[j - FUSED][:], banks[k][:], scale, None, MULT)
-            else:
-                nc.scalar.activation(first_terms[j - FUSED][:], banks[k][:], COPY, scale=scale)
-
-        first_banks, second_banks = (4, 5), (2, 3)
-        plain(0, 0, first_banks)
-        plain(1, 0, first_banks)
-        experts(GROUP, 2 * GROUP, [2], 0)
-        experts(2 * GROUP, E, [2], 1)
-        fused([0], 0, FUSED, 6)
-        plain(2, 0, first_banks)
-        experts(GROUP, 2 * GROUP, [3], 2)
-        experts(2 * GROUP, E, [3], 3)
-        plain(3, 0, first_banks)
-        fused([1], 0, FUSED, 7)
-        plain(0, 1, second_banks)
-        plain(1, 1, second_banks)
-        fused([2, 3], 0, 2, 0)
-        plain(2, 1, second_banks)
-        plain(3, 1, second_banks)
-        fused([2], 2, FUSED, 1)
-        round_bank([0], 0, FUSED, 6)
-        fused([3], 2, 3, 6)
-        round_bank([1], 0, FUSED, 7)
-        fused([3], 3, FUSED, 7)
-        round_bank([2, 3], 0, 2, 0)
-        first_term(4, 4)
-        round_bank([2], 2, FUSED, 1)
-        wp_bf = shared.tile([P, 4 * M], BF16, name="wp_bf", align_bytes=64, offset=4 * S * 3)
-        nc.gpsimd.tensor_copy(wp_bf[:].rearrange("p (f j) -> p f j", j=4), wp_raw[:].rearrange("p j f -> p f j"))
-        first_term(5, 5)
+        experts(GROUP, 2 * GROUP, [2], 6)
+        experts(2 * GROUP, E, [2], 7)
+        experts(GROUP, 2 * GROUP, [3], 4)
+        experts(2 * GROUP, E, [3], 5)
+        gather_results("vector", 0, 0, 0, TILES)
+        gather_results("vector", 0, 1, 0, TILES, 0)
+        gather_results("scalar", 1, 0, 0, TILES)
+        gather_results("vector", 0, 2, 0, TILES)
+        wp_bf = shared.tile([P, 4 * M], BF16, name="wp_bf", align_bytes=64, offset=late + 4096)
+        nc.gpsimd.tensor_scalar(
+            wp_bf[:].rearrange("p (f j) -> p f j", j=4), wp_raw[:].rearrange("p j f -> p f j"), 1.0, 0.0, MULT, ADD
+        )
+        gather_results("vector", 1, 2, 0, 2)
+        gather_results("scalar", 1, 1, 0, TILES)
+        gather_results("vector", 1, 3, 0, 2)
+        gather_results("vector", 0, 3, 0, 2)
+        gather_results("scalar", 1, 2, 2, TILES)
+        gather_results("vector", 0, 3, 2, 4)
+        gather_results("vector", 1, 3, 2, 4)
+        gather_results("vector", 0, 3, 4, TILES)
+        round_tile(0)
+        round_tile(1)
+        round_tile(2)
         c01 = keep.tile([P, 2 * N], BF16, name="c01", align_bytes=64)
+        turn_back(0, 2, 6, c01[:])
+        gather_results("vector", 1, 3, 4, TILES, 11)
         c23 = keep.tile([P, 2 * N], BF16, name="c23", align_bytes=64)
         c4 = keep.tile([P, N], BF16, name="c4", align_bytes=64)
         c5 = keep.tile([P, N], BF16, name="c5", align_bytes=64)
-        round_bank([3], 2, 3, 6)
-        turn_back(0, 2, 0, c01[:])
-        round_bank([3], 3, FUSED, 7)
-        add_second(4, 2)
-        add_second(5, 3)
+        round_tile(3, "vector")
+        round_tile(4)
+        round_tile(5, "vector")
         nc.vector.quantize_mx(out=wp_codes[:].bitcast(FP8X4), scales=wp_scales[:], in_=wp_bf[:])
-        turn_back(2, 3, 1, c23[:, 0:N])
-        turn_back(4, 5, 4, c4[:])
-        turn_back(3, 4, 6, c23[:, N:])
-        turn_back(5, 6, 5, c5[:])
-        project(0, 2, c01, 2, nc.scalar.copy)
-        project(2, 4, c23, 7, nc.scalar.copy)
-        project(4, 5, c4, 3, nc.scalar.copy)
-        project(5, 6, c5, 0, nc.vector.tensor_copy)
+        turn_back(2, 4, 7, c23[:])
+        turn_back(4, 5, 0, c4[:])
+        turn_back(5, 6, 1, c5[:])
+        project(0, 2, c01, 5, nc.scalar.copy)
+        project(2, 4, c23, 4, nc.scalar.copy)
+        project(4, 5, c4, 2, nc.vector.tensor_copy)
+        project(5, 6, c5, 3, nc.vector.tensor_copy)

@@ -21,17 +21,14 @@ FP8X4 = mybir.dt.float8_e4m3fn_x4
 FP4X4 = mybir.dt.float4_e2m1fn_x4
 MULT = mybir.AluOpType.mult
 ADD = mybir.AluOpType.add
-SUBTRACT = mybir.AluOpType.subtract
-MAX = mybir.AluOpType.max
-POW = mybir.AluOpType.pow
-IS_GE = mybir.AluOpType.is_ge
 COPY = mybir.ActivationFunctionType.Copy
 ABS = mybir.ActivationFunctionType.Abs
+SIGN = mybir.ActivationFunctionType.Sign
 
 GROUP = BANK // C
 TILES = T // P
 SPLIT = 4
-RATIO_BOUND = 2.0**-30
+RATIO_BOUND = 2.0**-40
 TINY = 2.0**-100
 BANKS = 8
 
@@ -50,11 +47,11 @@ def tile_moe_nxt_lin_none_kernel(
         xw = keep.tile([P, T], I32, name="xw", align_bytes=64)
         xs = keep.tile([P, T], U8, name="xs", align_bytes=64)
         ws = keep.tile([P, E * N], U8, name="ws", align_bytes=64)
-        ratio_sb = shared.tile([P, T], F32, name="ratio_sb", align_bytes=64, offset=4 * S * NB + 16384)
+        ratio_sb = shared.tile([P, T], F32, name="ratio_sb", align_bytes=64, offset=4 * S * NB + 20480)
         wp_raw = keep.tile([P, 4, M], F32, name="wp_raw")
         ident = keep.tile([P, P], F32, name="ident")
         late = 4 * S * NB
-        gate_rows = shared.tile([P, P], F32, name="gate_rows", align_bytes=64, offset=late + 2 * GROUP * C - 64)
+        gate_rows = keep.tile([P, P], F32, name="gate_rows")
         gate_cols = keep.tile([P, 2 * TILES], F32, name="gate_cols")
         banks = [psum.tile([P, BANK], F32, name=f"bank{k}") for k in range(BANKS)]
 
@@ -84,8 +81,8 @@ def tile_moe_nxt_lin_none_kernel(
                 xs[32 * q : 32 * (q + 1), :].bitcast(I32),
                 x_scales[0, 4 * q : 4 * q + 4, :].bitcast(I32).partition_broadcast(8),
             )
-        nc.sync.dma_start(xw[:], x_words[0].rearrange("p t r -> p (t r)").bitcast(I32))
         nc.sync.dma_start(gate_rows[:], gate.rearrange("i n (j t) -> (n j) i t", t=P)[0 : P // 2])
+        nc.sync.dma_start(xw[:], x_words[0].rearrange("p t r -> p (t r)").bitcast(I32))
         for r in range(4):
             nc.sync.dma_start(
                 ws[r:P:32, :].bitcast(I32).rearrange("q (e n) -> q e n", e=E), ws_rows[r].bitcast(I32)
@@ -100,37 +97,41 @@ def tile_moe_nxt_lin_none_kernel(
         load_weights(2, 2, NB)
         nc.sync.dma_start(wp_raw[:], wp.rearrange("(p j) f -> p j f", j=4))
 
-        nc.tensor.transpose(banks[2][:, 0:P], gate_rows[:], ident[:])
-        nc.scalar.copy(gate_cols[:], banks[2][:, 0 : 2 * TILES])
+        nc.tensor.transpose(banks[6][:, 0:P], gate_rows[:], ident[:])
+        nc.scalar.copy(gate_cols[:], banks[6][:, 0 : 2 * TILES])
         small = {
             name: keep.tile([P, TILES], F32, name=name)[:]
-            for name in ("floor", "size", "step", "sign", "lack", "lift", "kept", "inverse", "signed", "minus_one")
+            for name in ("share", "kept", "size", "step", "sign", "inverse", "signed")
         }
-        codes_at = 4 * S * NB + 20480
+        floor_tile = shared.tile([P, 16], F32, name="floor", offset=late + 2 * GROUP * C - 32)
+        floor = floor_tile[:, 5 : 5 + TILES]
+        kept = small["kept"]
+        codes_at = 4 * S * NB + 24576
         second_tile = shared.tile([P, 16], F32, name="second", offset=codes_at + 4 * M - 32)
-        early_second = shared.tile([P, 1], F32, name="early_second", offset=late + 4096 + 8 * P * 11)
+        early_second = shared.tile([P, 1], F32, name="early_second", offset=late + 6144 + 8 * P * 11)
         second = [early_second[:]]
         second.extend(second_tile[:, 4 + j : 5 + j] for j in range(1, TILES))
         ratio = keep.tile([P, TILES], F32, name="ratio")
-        nc.scalar.activation(small["floor"], banks[2][:, 0 : 2 * TILES : 2], ABS, scale=RATIO_BOUND)
-        nc.scalar.activation(small["size"], banks[2][:, 1 : 2 * TILES : 2], ABS)
-        nc.gpsimd.memset(small["minus_one"], -1.0)
-        nc.gpsimd.tensor_scalar(small["step"], gate_cols[:, 1::2], 0.0, 2.0, IS_GE, MULT)
-        nc.gpsimd.tensor_tensor(small["sign"], small["step"], small["minus_one"], ADD)
+        nc.scalar.activation(small["share"], banks[6][:, 0 : 2 * TILES : 2], ABS, scale=RATIO_BOUND)
+        nc.scalar.activation(small["step"], banks[6][:, 1 : 2 * TILES : 2], SIGN)
+        nc.scalar.activation(small["size"], banks[6][:, 1 : 2 * TILES : 2], ABS)
+        nc.scalar.activation(floor, small["share"], COPY, bias=TINY)
+        nc.scalar.activation(small["sign"], small["step"], SIGN, bias=0.5)
+        nc.gpsimd.tensor_tensor(kept, small["size"], floor, ADD)
         nc.gpsimd.tensor_tensor(small["signed"], gate_cols[:, 0::2], small["sign"], MULT)
-        nc.gpsimd.tensor_tensor(small["lack"], small["floor"], small["size"], SUBTRACT)
-        nc.gpsimd.tensor_scalar(small["lift"], small["lack"], TINY, 1.0, MAX, MULT)
-        nc.gpsimd.tensor_tensor(small["kept"], small["size"], small["lift"], ADD)
-        nc.gpsimd.tensor_tensor(small["inverse"], small["kept"], small["minus_one"], POW)
+        nc.gpsimd.tensor_tensor(early_second[:], kept[:, 0:1], small["sign"][:, 0:1], MULT)
+        nc.gpsimd.tensor_tensor(second_tile[:, 5:10], kept[:, 1:], small["sign"][:, 1:], MULT)
+        nc.vector.reciprocal(small["inverse"], kept)
         nc.gpsimd.tensor_tensor(ratio[:], small["signed"], small["inverse"], MULT)
-        nc.gpsimd.tensor_tensor(early_second[:], small["kept"][:, 0:1], small["sign"][:, 0:1], MULT)
-        nc.gpsimd.tensor_tensor(second_tile[:, 5:10], small["kept"][:, 1:], small["sign"][:, 1:], MULT)
 
-        def spread_ratio(j0, j1, k, evict):
+        def spread_ratio(j0, j1, k):
             for j in range(j0, j1):
                 col = (j - j0) * P
                 nc.tensor.transpose(banks[k][:, col : col + P], ratio[:, j : j + 1].to_broadcast([P, P]), ident[:])
-            evict(ratio_sb[:, j0 * P : j1 * P], banks[k][:, 0 : (j1 - j0) * P])
+
+        spread_ratio(0, GROUP, 4)
+        nc.scalar.copy(ratio_sb[:, 0 : GROUP * P], banks[4][:])
+        spread_ratio(GROUP, TILES, 0)
 
         y = [shared.tile([P, S], F32, name=f"y{b}", align_bytes=64, offset=4 * S * b) for b in range(NB)]
         slot_scales = {}
@@ -165,27 +166,26 @@ def tile_moe_nxt_lin_none_kernel(
 
         wp_scales = keep.tile([P, M], U8, name="wp_scales", align_bytes=64)
         early_scales = keep.tile([P, GROUP * C], U8, name="early_scales", align_bytes=64)
-        early_words = [keep.tile([P, GROUP * C], U32, name=f"early_words{g}", align_bytes=64) for g in range(2)]
+        early_words = keep.tile([P, GROUP * C], U32, name="early_words", align_bytes=64)
         late_scales = shared.tile([P, 2 * GROUP * C], U8, name="late_scales", align_bytes=64, offset=late)
-        late_words = shared.tile([P, GROUP * C], U32, name="late_words", align_bytes=64, offset=late + 2 * GROUP * C)
+        late_words = shared.tile([P, 2 * GROUP * C], U32, name="late_words", align_bytes=64, offset=late + 2 * GROUP * C)
         gather_scales(0, GROUP, early_scales[:])
-        gather_words(0, GROUP, early_words[0][:])
-        for b, k in enumerate((5, 1, 6, 7)):
+        gather_words(0, GROUP, early_words[:])
+        for b, k in enumerate((5, 1, 2, 3)):
             experts(0, GROUP, [b], k)
-        gather_words(GROUP, 2 * GROUP, early_words[1][:])
+        gather_words(GROUP, 2 * GROUP, late_words[:, 0 : GROUP * C])
         gather_scales(GROUP, 2 * GROUP, late_scales[:, 0 : GROUP * C])
-        experts(GROUP, 2 * GROUP, [0], 4)
+        experts(GROUP, 2 * GROUP, [0], 6)
         gather_scales(2 * GROUP, E, late_scales[:, GROUP * C :])
-        gather_words(2 * GROUP, E - 2, late_words[:, 0 : 2 * C])
-        gather_words(E - 2, E - 1, late_words[:, 2 * C : 3 * C])
-        gather_words(E - 1, E, late_words[:, 3 * C : 4 * C])
-        spread_ratio(0, GROUP, 5, nc.scalar.copy)
-        spread_ratio(GROUP, TILES, 1, nc.vector.tensor_copy)
-        experts(GROUP, 2 * GROUP, [1], 3, nc.vector.tensor_copy)
-        experts(2 * GROUP, E - 2, [0], 6)
-        experts(E - 2, E - 1, [0], 7)
-        experts(E - 1, E, [0], 4)
-        experts(2 * GROUP, E, [1], 5)
+        gather_words(2 * GROUP, E - 2, late_words[:, 4 * C : 6 * C])
+        gather_words(E - 2, E - 1, late_words[:, 6 * C : 7 * C])
+        gather_words(E - 1, E, late_words[:, 7 * C : 8 * C])
+        nc.vector.tensor_copy(ratio_sb[:, GROUP * P :], banks[0][:, 0 : T - GROUP * P])
+        experts(GROUP, 2 * GROUP, [1], 7, nc.vector.tensor_copy)
+        experts(2 * GROUP, E - 2, [0], 4)
+        experts(E - 2, E - 1, [0], 5)
+        experts(E - 1, E, [0], 1)
+        experts(2 * GROUP, E, [1], 2)
 
         rounded = [keep.tile([P, N], BF16, name=f"rounded{j}")[:] for j in range(3)]
         rounded.extend(
@@ -199,7 +199,7 @@ def tile_moe_nxt_lin_none_kernel(
             if slot is None:
                 term = keep.tile([P, t1 - t0], F32, name=f"term{b}_{j0}_{i}")[:]
             else:
-                term = shared.tile([P, t1 - t0], F32, name=f"term{b}_{j0}_{i}", offset=late + 4096 + 8 * P * slot)[:]
+                term = shared.tile([P, t1 - t0], F32, name=f"term{b}_{j0}_{i}", offset=late + 6144 + 8 * P * slot)[:]
             window = y[b][:].indirect(pos_sb[i][:, t0 // 16 : t1 // 16])
             if i == 0:
                 nc.vector.tensor_tensor(term, window, ratio_sb[:, t0:t1], MULT)
@@ -258,15 +258,15 @@ def tile_moe_nxt_lin_none_kernel(
             evict(res[:], banks[k][:, 0:tw])
             nc.sync.dma_start(out[:, t0 : t0 + tw], res[:])
 
-        experts(GROUP, 2 * GROUP, [2], 6)
-        experts(2 * GROUP, E, [2], 7)
-        experts(GROUP, 2 * GROUP, [3], 4)
+        experts(GROUP, 2 * GROUP, [2], 3)
+        experts(GROUP, 2 * GROUP, [3], 6)
+        experts(2 * GROUP, E, [2], 4)
         experts(2 * GROUP, E, [3], 5)
         gather_results("vector", 0, 0, 0, TILES)
         gather_results("vector", 0, 1, 0, TILES, 0)
         gather_results("scalar", 1, 0, 0, TILES)
         gather_results("vector", 0, 2, 0, TILES)
-        wp_bf = shared.tile([P, 4 * M], BF16, name="wp_bf", align_bytes=64, offset=late + 4096)
+        wp_bf = shared.tile([P, 4 * M], BF16, name="wp_bf", align_bytes=64, offset=late + 6144)
         nc.gpsimd.tensor_scalar(
             wp_bf[:].rearrange("p (f j) -> p f j", j=4), wp_raw[:].rearrange("p j f -> p f j"), 1.0, 0.0, MULT, ADD
         )

@@ -132,6 +132,7 @@ def tile_moe_nxt_lin_none_kernel(
         spread_ratio(0, GROUP, 4)
         nc.scalar.copy(ratio_sb[:, 0 : GROUP * P], banks[4][:])
         spread_ratio(GROUP, TILES, 0)
+        nc.scalar.copy(ratio_sb[:, GROUP * P :], banks[0][:, 0 : T - GROUP * P])
 
         y = [shared.tile([P, S], F32, name=f"y{b}", align_bytes=64, offset=4 * S * b) for b in range(NB)]
         slot_scales = {}
@@ -161,7 +162,7 @@ def tile_moe_nxt_lin_none_kernel(
                         start=True,
                         stop=True,
                     )
-            for x, b in enumerate(blocks):
+            for x, b in enumerate(blocks if evict else []):
                 evict(y[b][:, first * C : last * C], banks[k][:, x * width : (x + 1) * width])
 
         wp_scales = keep.tile([P, M], U8, name="wp_scales", align_bytes=64)
@@ -171,8 +172,9 @@ def tile_moe_nxt_lin_none_kernel(
         late_words = shared.tile([P, 2 * GROUP * C], U32, name="late_words", align_bytes=64, offset=late + 2 * GROUP * C)
         gather_scales(0, GROUP, early_scales[:])
         gather_words(0, GROUP, early_words[:])
-        for b, k in enumerate((5, 1, 2, 3)):
+        for b, k in enumerate((5, 1, 2)):
             experts(0, GROUP, [b], k)
+        experts(0, GROUP, [3], 3, None)
         gather_words(GROUP, 2 * GROUP, late_words[:, 0 : GROUP * C])
         gather_scales(GROUP, 2 * GROUP, late_scales[:, 0 : GROUP * C])
         experts(GROUP, 2 * GROUP, [0], 6)
@@ -180,7 +182,7 @@ def tile_moe_nxt_lin_none_kernel(
         gather_words(2 * GROUP, E - 2, late_words[:, 4 * C : 6 * C])
         gather_words(E - 2, E - 1, late_words[:, 6 * C : 7 * C])
         gather_words(E - 1, E, late_words[:, 7 * C : 8 * C])
-        nc.vector.tensor_copy(ratio_sb[:, GROUP * P :], banks[0][:, 0 : T - GROUP * P])
+        nc.vector.tensor_copy(y[3][:, 0 : GROUP * C], banks[3][:])
         experts(GROUP, 2 * GROUP, [1], 7, nc.vector.tensor_copy)
         experts(2 * GROUP, E - 2, [0], 4)
         experts(E - 2, E - 1, [0], 5)

@@ -220,6 +220,12 @@ def tile_moe_nxt_lin_none_kernel(
                 )
                 turns[j] = turns[j] + 1
 
+        def round_wp(h, at):
+            tile = shared.tile([P, 2 * M], BF16, name=f"wp_bf{h}", align_bytes=64, offset=at)
+            rows = wp_raw[:].rearrange("p j f -> p f j")[:, h * M // 2 : (h + 1) * M // 2]
+            nc.gpsimd.tensor_scalar(tile[:].rearrange("p (f j) -> p f j", j=4), rows, 1.0, 0.0, MULT, ADD)
+            return tile
+
         def round_tile(j, engine="scalar"):
             dest = rounded[j].rearrange("p (u w e) -> p u w e", u=2, e=2)
             sums = banks[j][:].rearrange("p (w u e) -> p u w e", u=2, e=2)
@@ -268,10 +274,7 @@ def tile_moe_nxt_lin_none_kernel(
         gather_results("vector", 0, 1, 0, TILES, 0)
         gather_results("scalar", 1, 0, 0, TILES)
         gather_results("vector", 0, 2, 0, TILES)
-        wp_bf = shared.tile([P, 4 * M], BF16, name="wp_bf", align_bytes=64, offset=late + 6144)
-        nc.gpsimd.tensor_scalar(
-            wp_bf[:].rearrange("p (f j) -> p f j", j=4), wp_raw[:].rearrange("p j f -> p f j"), 1.0, 0.0, MULT, ADD
-        )
+        wp_bf = [round_wp(0, late + 6144)]
         gather_results("vector", 1, 2, 0, 2)
         gather_results("scalar", 1, 1, 0, TILES)
         gather_results("vector", 1, 3, 0, 2)
@@ -286,13 +289,16 @@ def tile_moe_nxt_lin_none_kernel(
         c01 = keep.tile([P, 2 * N], BF16, name="c01", align_bytes=64)
         turn_back(0, 2, 6, c01[:])
         gather_results("vector", 1, 3, 4, TILES, 11)
+        wp_bf.append(round_wp(1, 4 * S * 3))
         c23 = keep.tile([P, 2 * N], BF16, name="c23", align_bytes=64)
         c4 = keep.tile([P, N], BF16, name="c4", align_bytes=64)
         c5 = keep.tile([P, N], BF16, name="c5", align_bytes=64)
         round_tile(3, "vector")
         round_tile(4)
         round_tile(5, "vector")
-        nc.vector.quantize_mx(out=wp_codes[:].bitcast(FP8X4), scales=wp_scales[:], in_=wp_bf[:])
+        for h in range(2):
+            cols = slice(h * M // 2, (h + 1) * M // 2)
+            nc.vector.quantize_mx(out=wp_codes[:, cols].bitcast(FP8X4), scales=wp_scales[:, cols], in_=wp_bf[h][:])
         turn_back(2, 4, 7, c23[:])
         turn_back(4, 5, 0, c4[:])
         turn_back(5, 6, 1, c5[:])

@@ -275,11 +275,11 @@ def tile_moe_nxt_lin_none_kernel(
         gather_results("scalar", 1, 0, 0, TILES)
         gather_results("vector", 0, 2, 0, TILES)
         wp_bf = [round_wp(0, late + 6144)]
-        gather_results("vector", 1, 2, 0, 2)
+        gather_results("vector", 1, 2, 0, 1)
         gather_results("scalar", 1, 1, 0, TILES)
         gather_results("vector", 1, 3, 0, 2)
         gather_results("vector", 0, 3, 0, 2)
-        gather_results("scalar", 1, 2, 2, TILES)
+        gather_results("scalar", 1, 2, 1, TILES)
         gather_results("vector", 0, 3, 2, 4)
         gather_results("vector", 1, 3, 2, 4)
         gather_results("vector", 0, 3, 4, TILES)

from contextlib import ExitStack

import concourse.mybir as mybir
from concourse.masks import make_identity

K, T, E, C, N, M = 512, 768, 12, 128, 512, 128
S = E * C
P = 128
NB = N // P
BANK = 512
FLOPS = 2 * K * N * S + 2 * N * M * T
BYTES = K * T + 16 * T + E * (K * N // 2 + 16 * N) + 4 * N * M + 2 * 4 * T + 2 * P * (S + 2 * T) // 16 + 4 * M * T

F32 = mybir.dt.float32
BF16 = mybir.dt.bfloat16
I32 = mybir.dt.int32
U32 = mybir.dt.uint32
U16 = mybir.dt.uint16
U8 = mybir.dt.uint8
FP8X4 = mybir.dt.float8_e4m3fn_x4
FP4X4 = mybir.dt.float4_e2m1fn_x4
MULT = mybir.AluOpType.mult
ADD = mybir.AluOpType.add
COPY = mybir.ActivationFunctionType.Copy
ABS = mybir.ActivationFunctionType.Abs
SIGN = mybir.ActivationFunctionType.Sign

GROUP = BANK // C
TILES = T // P
SPLIT = 4
RATIO_BOUND = 2.0**-40
TINY = 2.0**-100
BANKS = 8


def tile_moe_nxt_lin_none_kernel(
    tc, x_words, x_scales, w_words, w_scales, wp, gate, offs, pos1, pos2, out
):
    nc = tc.nc
    with ExitStack() as ctx:
        keep = ctx.enter_context(tc.tile_pool(name="keep", bufs=1))
        shared = ctx.enter_context(tc.tile_pool(name="shared", bufs=1))
        psum = ctx.enter_context(tc.psum_pool(name="psum", bufs=1))

        offs_sb = keep.tile([P, S // 16], U16, name="offs_sb")
        pos_sb = [keep.tile([P, T // 16], U16, name=f"pos_sb{i}") for i in range(2)]
        xw = keep.tile([P, T], I32, name="xw", align_bytes=64)
        xs = keep.tile([P, T], U8, name="xs", align_bytes=64)
        ws = keep.tile([P, E * N], U8, name="ws", align_bytes=64)
        ratio_sb = shared.tile([P, T], F32, name="ratio_sb", align_bytes=64, offset=4 * S * NB + 20480)
        wp_raw = keep.tile([P, 4, M], F32, name="wp_raw")
        ident = keep.tile([P, P], F32, name="ident")
        late = 4 * S * NB
        gate_rows = keep.tile([P, P], F32, name="gate_rows")
        gate_cols = keep.tile([P, 2 * TILES], F32, name="gate_cols")
        banks = [psum.tile([P, BANK], F32, name=f"bank{k}") for k in range(BANKS)]

        nc.vector.memset(ws[:].bitcast(I32), 0)
        make_identity(nc, ident[:])

        ws_rows = w_scales.rearrange("e a (q r) n -> r q (e a) n", r=4)
        ww_rows = w_words.rearrange("e a p n -> p (e a) n")
        weight_words = {}

        def load_weights(g, b0, b1):
            width = 2 * P * (b1 - b0)
            tile = keep.tile([P, GROUP * width], U8, name=f"ww{g}_{b0}", align_bytes=64)
            nc.sync.dma_start(
                tile[:].bitcast(I32).rearrange("p (e n) -> p e n", e=GROUP),
                ww_rows[:, g * GROUP : (g + 1) * GROUP, 2 * P * b0 : 2 * P * b1].bitcast(I32),
            )
            for u in range(GROUP):
                for b in range(b0, b1):
                    col = u * width + 2 * P * (b - b0)
                    weight_words[g * GROUP + u, b] = tile[:, col : col + 2 * P]

        nc.sync.dma_start(offs_sb[:], offs)
        for q in range(4):
            queue = nc.sync if q < 2 else nc.scalar
            queue.dma_start(
                xs[32 * q : 32 * (q + 1), :].bitcast(I32),
                x_scales[0, 4 * q : 4 * q + 4, :].bitcast(I32).partition_broadcast(8),
            )
        nc.sync.dma_start(gate_rows[:], gate.rearrange("i n (j t) -> (n j) i t", t=P)[0 : P // 2])
        nc.sync.dma_start(xw[:], x_words[0].rearrange("p t r -> p (t r)").bitcast(I32))
        for r in range(4):
            nc.sync.dma_start(
                ws[r:P:32, :].bitcast(I32).rearrange("q (e n) -> q e n", e=E), ws_rows[r].bitcast(I32)
            )
        nc.sync.dma_start(pos_sb[0][:], pos1)
        nc.sync.dma_start(pos_sb[1][:], pos2)
        load_weights(0, 0, 2)
        load_weights(0, 2, NB)
        load_weights(1, 0, 2)
        load_weights(2, 0, 2)
        load_weights(1, 2, NB)
        load_weights(2, 2, NB)
        nc.sync.dma_start(wp_raw[:], wp.rearrange("(p j) f -> p j f", j=4))

        nc.tensor.transpose(banks[6][:, 0:P], gate_rows[:], ident[:])
        nc.scalar.copy(gate_cols[:], banks[6][:, 0 : 2 * TILES])
        small = {
            name: keep.tile([P, TILES], F32, name=name)[:]
            for name in ("share", "kept", "size", "step", "sign", "inverse", "signed")
        }
        floor_tile = shared.tile([P, 16], F32, name="floor", offset=late + 2 * GROUP * C - 32)
        floor = floor_tile[:, 5 : 5 + TILES]
        kept = small["kept"]
        codes_at = 4 * S * NB + 24576
        second_tile = shared.tile([P, 16], F32, name="second", offset=codes_at + 4 * M - 32)
        early_second = shared.tile([P, 1], F32, name="early_second", offset=late + 6144 + 8 * P * 11)
        second = [early_second[:]]
        second.extend(second_tile[:, 4 + j : 5 + j] for j in range(1, TILES))
        ratio = keep.tile([P, TILES], F32, name="ratio")
        nc.scalar.activation(small["share"], banks[6][:, 0 : 2 * TILES : 2], ABS, scale=RATIO_BOUND)
        nc.scalar.activation(small["step"], banks[6][:, 1 : 2 * TILES : 2], SIGN)
        nc.scalar.activation(small["size"], banks[6][:, 1 : 2 * TILES : 2], ABS)
        nc.scalar.activation(floor, small["share"], COPY, bias=TINY)
        nc.scalar.activation(small["sign"], small["step"], SIGN, bias=0.5)
        nc.gpsimd.tensor_tensor(kept, small["size"], floor, ADD)
        nc.gpsimd.tensor_tensor(small["signed"], gate_cols[:, 0::2], small["sign"], MULT)
        nc.gpsimd.tensor_tensor(early_second[:], kept[:, 0:1], small["sign"][:, 0:1], MULT)
        nc.gpsimd.tensor_tensor(second_tile[:, 5:10], kept[:, 1:], small["sign"][:, 1:], MULT)
        nc.vector.reciprocal(small["inverse"], kept)
        nc.gpsimd.tensor_tensor(ratio[:], small["signed"], small["inverse"], MULT)

        def spread_ratio(j0, j1, k):
            for j in range(j0, j1):
                col = (j - j0) * P
                nc.tensor.transpose(banks[k][:, col : col + P], ratio[:, j : j + 1].to_broadcast([P, P]), ident[:])

        spread_ratio(0, GROUP, 4)
        nc.scalar.copy(ratio_sb[:, 0 : GROUP * P], banks[4][:])
        spread_ratio(GROUP, TILES, 0)
        nc.scalar.copy(ratio_sb[:, GROUP * P :], banks[0][:, 0 : T - GROUP * P])

        y = [shared.tile([P, S], F32, name=f"y{b}", align_bytes=64, offset=4 * S * b) for b in range(NB)]
        slot_scales = {}
        slot_words = {}

        def gather_scales(first, last, tile):
            nc.vector.tensor_copy(tile, xs[:].indirect(offs_sb[:, first * C // 16 : last * C // 16]))
            for e in range(first, last):
                slot_scales[e] = tile[:, (e - first) * C : (e - first + 1) * C]

        def gather_words(first, last, tile):
            nc.vector.tensor_copy(tile, xw[:].bitcast(U32).indirect(offs_sb[:, first * C // 16 : last * C // 16]))
            for e in range(first, last):
                slot_words[e] = tile[:, (e - first) * C : (e - first + 1) * C]

        def experts(first, last, blocks, k, evict=nc.scalar.copy):
            width = (last - first) * C
            for x, b in enumerate(blocks):
                for e in range(first, last):
                    col = x * width + (e - first) * C
                    nc.tensor.matmul_mx(
                        out=banks[k][:, col : col + C],
                        lhsT=weight_words[e, b].bitcast(FP4X4),
                        lhsT_scale=ws[:, e * N + b * P : e * N + (b + 1) * P],
                        rhs=slot_words[e].bitcast(FP8X4),
                        rhs_scale=slot_scales[e],
                        start=True,
                        stop=True,
                    )
            for x, b in enumerate(blocks if evict else []):
                evict(y[b][:, first * C : last * C], banks[k][:, x * width : (x + 1) * width])

        wp_scales = keep.tile([P, M], U8, name="wp_scales", align_bytes=64)
        early_scales = keep.tile([P, GROUP * C], U8, name="early_scales", align_bytes=64)
        early_words = keep.tile([P, GROUP * C], U32, name="early_words", align_bytes=64)
        late_scales = shared.tile([P, 2 * GROUP * C], U8, name="late_scales", align_bytes=64, offset=late)
        late_words = shared.tile([P, 2 * GROUP * C], U32, name="late_words", align_bytes=64, offset=late + 2 * GROUP * C)
        gather_scales(0, GROUP, early_scales[:])
        gather_words(0, GROUP, early_words[:])
        for b, k in enumerate((5, 1, 2)):
            experts(0, GROUP, [b], k)
        experts(0, GROUP, [3], 3, None)
        gather_words(GROUP, 2 * GROUP, late_words[:, 0 : GROUP * C])
        gather_scales(GROUP, 2 * GROUP, late_scales[:, 0 : GROUP * C])
        experts(GROUP, 2 * GROUP, [0], 6)
        gather_scales(2 * GROUP, E, late_scales[:, GROUP * C :])
        gather_words(2 * GROUP, E - 2, late_words[:, 4 * C : 6 * C])
        gather_words(E - 2, E - 1, late_words[:, 6 * C : 7 * C])
        gather_words(E - 1, E, late_words[:, 7 * C : 8 * C])
        nc.vector.tensor_copy(y[3][:, 0 : GROUP * C], banks[3][:])
        experts(GROUP, 2 * GROUP, [1], 7, nc.vector.tensor_copy)
        experts(2 * GROUP, E - 2, [0], 4)
        experts(E - 2, E - 1, [0], 5)
        experts(E - 1, E, [0], 1)
        experts(2 * GROUP, E, [1], 2)

        rounded = [keep.tile([P, N], BF16, name=f"rounded{j}")[:] for j in range(3)]
        rounded.extend(
            shared.tile([P, N], BF16, name=f"rounded{j}", offset=4 * S * 3 + 2 * N * j)[:] for j in range(3, TILES)
        )
        wp_codes = shared.tile([P, M], U32, name="wp_codes", align_bytes=64, offset=codes_at)
        turns = [0] * TILES

        def gather_results(engine, i, b, j0, j1, slot=None):
            t0, t1 = j0 * P, j1 * P
            if slot is None:
                term = keep.tile([P, t1 - t0], F32, name=f"term{b}_{j0}_{i}")[:]
            else:
                term = shared.tile([P, t1 - t0], F32, name=f"term{b}_{j0}_{i}", offset=late + 6144 + 8 * P * slot)[:]
            window = y[b][:].indirect(pos_sb[i][:, t0 // 16 : t1 // 16])
            if i == 0:
                nc.vector.tensor_tensor(term, window, ratio_sb[:, t0:t1], MULT)
            elif engine == "vector":
                nc.vector.tensor_copy(term, window)
            else:
                nc.scalar.activation(term, window, COPY)
            for j in range(j0, j1):
                nc.tensor.matmul(
                    banks[j][:, b * P : (b + 1) * P],
                    lhsT=term[:, (j - j0) * P : (j - j0 + 1) * P],
                    rhs=ident[:],
                    is_transpose=True,
                    start=(turns[j] == 0),
                    stop=(turns[j] == 2 * NB - 1),
                )
                turns[j] = turns[j] + 1

        def round_wp(h, at):
            tile = shared.tile([P, 2 * M], BF16, name=f"wp_bf{h}", align_bytes=64, offset=at)
            rows = wp_raw[:].rearrange("p j f -> p f j")[:, h * M // 2 : (h + 1) * M // 2]
            nc.gpsimd.tensor_scalar(tile[:].rearrange("p (f j) -> p f j", j=4), rows, 1.0, 0.0, MULT, ADD)
            return tile

        def round_tile(j, engine="scalar"):
            dest = rounded[j].rearrange("p (u w e) -> p u w e", u=2, e=2)
            sums = banks[j][:].rearrange("p (w u e) -> p u w e", u=2, e=2)
            if engine == "vector":
                nc.vector.tensor_scalar(dest, sums, second[j], None, MULT)
            else:
                nc.scalar.activation(dest, sums, COPY, scale=second[j])

        def turn_back(j0, j1, k, dest, evict=nc.scalar.copy):
            width = (j1 - j0) * 2 * P
            for j in range(j0, j1):
                for u in range(2):
                    col = (2 * (j - j0) + u) * P
                    pairs = rounded[j].bitcast(F32)[:, u * P : (u + 1) * P]
                    nc.tensor.transpose(banks[k][:, col : col + P], pairs, ident[:])
            evict(
                dest.bitcast(F32).rearrange("p (j t u) -> p j t u", t=P, u=2),
                banks[k][:, 0:width].rearrange("p (j u t) -> p j t u", t=P, u=2),
            )

        def project(j0, j1, c_bf, k, evict):
            t0, tw = j0 * P, (j1 - j0) * P
            c_codes = shared.tile([P, tw], U32, name=f"c_codes{j0}", align_bytes=64, offset=codes_at + 4 * (M + t0))
            c_scales = keep.tile([P, tw], U8, name=f"c_scales{j0}", align_bytes=64)
            nc.vector.quantize_mx(out=c_codes[:].bitcast(FP8X4), scales=c_scales[:], in_=c_bf[:])
            for c0 in range(0, tw, 2 * P):
                c1 = min(c0 + 2 * P, tw)
                nc.tensor.matmul_mx(
                    out=banks[k][:, c0:c1],
                    lhsT=wp_codes[:].bitcast(FP8X4),
                    lhsT_scale=wp_scales[:],
                    rhs=c_codes[:, c0:c1].bitcast(FP8X4),
                    rhs_scale=c_scales[:, c0:c1],
                    start=True,
                    stop=True,
                )
            res = keep.tile([P, tw], F32, name=f"res{j0}")
            evict(res[:], banks[k][:, 0:tw])
            nc.sync.dma_start(out[:, t0 : t0 + tw], res[:])

        experts(GROUP, 2 * GROUP, [2], 3)
        experts(GROUP, 2 * GROUP, [3], 6)
        experts(2 * GROUP, E, [2], 4)
        experts(2 * GROUP, E, [3], 5)
        gather_results("vector", 0, 0, 0, TILES)
        gather_results("vector", 0, 1, 0, TILES, 0)
        gather_results("scalar", 1, 0, 0, TILES)
        gather_results("vector", 0, 2, 0, TILES)
        wp_bf = [round_wp(0, late + 6144)]
        gather_results("vector", 1, 2, 0, 1)
        gather_results("scalar", 1, 1, 0, TILES)
        gather_results("vector", 1, 3, 0, 2)
        gather_results("vector", 0, 3, 0, 2)
        gather_results("scalar", 1, 2, 1, TILES)
        gather_results("vector", 0, 3, 2, 4)
        gather_results("vector", 1, 3, 2, 4)
        gather_results("vector", 0, 3, 4, TILES)
        round_tile(0)
        round_tile(1)
        round_tile(2)
        c01 = keep.tile([P, 2 * N], BF16, name="c01", align_bytes=64)
        turn_back(0, 2, 6, c01[:])
        gather_results("vector", 1, 3, 4, TILES, 11)
        wp_bf.append(round_wp(1, 4 * S * 3))
        c23 = keep.tile([P, 2 * N], BF16, name="c23", align_bytes=64)
        c4 = keep.tile([P, N], BF16, name="c4", align_bytes=64)
        c5 = keep.tile([P, N], BF16, name="c5", align_bytes=64)
        round_tile(3, "vector")
        round_tile(4)
        round_tile(5, "vector")
        for h in range(2):
            cols = slice(h * M // 2, (h + 1) * M // 2)
            nc.vector.quantize_mx(out=wp_codes[:, cols].bitcast(FP8X4), scales=wp_scales[:, cols], in_=wp_bf[h][:])
        turn_back(2, 4, 7, c23[:])
        turn_back(4, 5, 0, c4[:])
        turn_back(5, 6, 1, c5[:])
        project(0, 2, c01, 5, nc.scalar.copy)
        project(2, 4, c23, 4, nc.scalar.copy)
        project(4, 5, c4, 2, nc.vector.tensor_copy)
        project(5, 6, c5, 3, nc.vector.tensor_copy)
